import numpy as np, ml_dtypes
CORES = [9,25,41,57]
N = 4
BF = ml_dtypes.bfloat16
def gentries(a):
    return np.ascontiguousarray(a.reshape(8, 16, -1).transpose(0, 2, 1)).reshape(8, -1)
def gtable(e):
    e = np.asarray(e); return np.ascontiguousarray(e.reshape(8, -1, 16).transpose(0, 2, 1)).reshape(128, -1).astype(np.int32)
V, CAP, D, R = 64, 16, 4, 2
def cube():
    P = np.indices((4, 4, 4, 4)).reshape(4, -1).T; P = P[(np.sort(P, 1) == np.arange(4)).all(1)]
    w = np.array([64, 16, 4, 1]); at = np.zeros(256, np.int64); at[P @ w] = np.arange(24)
    return at[P[:, P] @ w]
def cyclic():
    i = np.arange(24); return (i[:, None] + i) % 24
def dihedral():
    i = np.arange(24); r = i % 12; s = i // 12
    return (r[:, None] + np.where(s[:, None] == 1, -r, r)) % 12 + 12 * (s[:, None] ^ s)
def labelled(rng, plain=0, mixed=False):
    res = np.zeros((8, 24, 24), np.int64)
    for g in range(8):
        c = cyclic() if mixed and g in (2, 3) else dihedral() if mixed and g in (4, 5) else cube()
        lab = np.arange(24) if g < plain else rng.permutation(24)
        res[g][lab[:, None], lab[None, :]] = lab[c]
    return res
def values(rng):
    return rng.standard_normal((N, 128, V * 24), dtype=np.float32) * np.exp2(rng.integers(-2, 3, (N, 128, 1))).astype(np.float32)
def raw(rng, plain=0, mixed=False):
    q = (np.arange(N)[:, None, None, None] + 1 + rng.integers(0, N - 1, (N, 8, D, V))) % N
    slot = V + q * CAP + rng.integers(0, CAP, (N, 8, D, V)); own = rng.integers(0, V, (N, 8, D, V))
    return {"x": values(rng), "pose": rng.integers(0, 24, (N, 8, V)), "act": rng.integers(0, 24, (N, 8, R - 1, V)), "c": labelled(rng, plain, mixed),
            "shown": np.argsort(rng.random((N, 8, N, V)), -1)[..., :CAP], "nbr": np.where(rng.random((N, 8, D, V)) < 0.5, own, slot)}
def glists(a):
    return np.stack([gtable(v.reshape(8, -1)) for v in a])
def pack(d):
    c = d["c"]; rel = np.argsort(c, 2).transpose(0, 2, 1)
    every = lambda t: np.repeat(np.ascontiguousarray(t).reshape(1, 8, 576).astype(np.int32), N, 0)
    return {"x": np.ascontiguousarray(d["x"].astype(np.float32)), "pose": glists(d["pose"]), "act": glists(d["act"]), "rel": every(rel), "ct": every(c), "shown": glists(d["shown"]), "nbr": glists(d["nbr"])}
def setup_inputs(rng):
    return pack(raw(rng))
def setup_inputs_full(rng):
    d = raw(rng, mixed=True)
    for r in range(N):
        s = np.concatenate([V + q * CAP + np.arange(CAP) for q in range(N) if q != r])
        for g in range(8):
            flat = d["nbr"][r, g].reshape(-1).copy(); flat[rng.permutation(D * V)[:len(s)]] = s; d["nbr"][r, g] = flat.reshape(D, V)
    return pack(d)
def setup_inputs_repeat(rng):
    d = raw(rng); a, b, e, w = rng.permutation(N)[:4]; n = d["nbr"]
    n[a] = rng.integers(0, V, (8, D, V)); n[a, :, 0] = np.arange(V)
    n[b] = V + a * CAP + rng.integers(0, CAP, (8, D, V))
    n[e] = n[e][:, :1]; q0 = 1 if e == 0 else 0; q1 = N - 2 if e == N - 1 else N - 1
    n[e, :, :, 0] = 0; n[e, :, :, V - 1] = V - 1; n[e, :, :, 1] = V + q1 * CAP + CAP - 1; n[e, :, :, 2] = V + q0 * CAP
    d["shown"][w] = d["shown"][w][..., :1]
    return pack(d)
def setup_inputs_below(rng):
    d = raw(rng); k = rng.integers(0, 87, 8); k[rng.integers(0, 8)] = 86
    d["x"] = -rng.integers(1, 200, (N, 128, V * 24)).astype(np.float32) * np.repeat(np.exp2(k), 16)[:, None].astype(np.float32); return pack(d)
def setup_inputs_alike(rng):
    d = raw(rng, 2, True)
    for g in range(8):
        if g % 2 == 0:
            d["pose"][:, g] = rng.integers(0, 24); d["act"][:, g] = rng.integers(0, 24, (1, R - 1, 1))
        else:
            d["act"][:, g] = np.argmax((d["c"][g] == np.arange(24)).all(1))
    return pack(d)
def setup_inputs_spread(rng):
    d = raw(rng); k = (N, 1, V * 24)
    d["x"] = d["x"] * (np.exp2(rng.integers(-6, 7, k)) * (rng.random(k) > 0.0625)).astype(np.float32); return pack(d)
def check_inputs(d):
    bad = []; j = np.arange(24)
    def within(a, top): return bool((a >= 0).all() and (a < top).all())
    if not np.isfinite(d["x"]).all(): bad.append("finite")
    elif not (np.abs(d["x"]) <= 2.0 ** 94).all(): bad.append("size")
    if not within(d["pose"], 24): bad.append("pose")
    if not within(d["act"], 24): bad.append("act")
    if not within(d["shown"], V): bad.append("shown")
    for r in range(N):
        n = d["nbr"][r]
        if not within(n, V + N * CAP) or ((n >= V + r * CAP) & (n < V + r * CAP + CAP)).any(): bad.append("nbr"); break
    if not (d["rel"] == d["rel"][:1]).all() or not (d["ct"] == d["ct"][:1]).all(): bad.append("tables_alike")
    if not within(d["rel"], 24) or not within(d["ct"], 24): bad.append("tables_range")
    else:
        for g in range(8):
            c = d["ct"][0, g].reshape(24, 24).astype(np.int64); l = d["rel"][0, g].reshape(24, 24).astype(np.int64)
            if not ((np.sort(c, 1) == j).all() and (np.sort(c, 0) == j[:, None]).all() and (c[c] == c[:, c]).all()): bad.append("ct_group"); break
            if not (c[j[None, :], l] == j[:, None]).all(): bad.append("rel"); break
    return bad
def reference(x, pose, act, rel, ct, shown, nbr):
    f = x.reshape(N, 8, 16, V, 24)
    p = np.stack([gentries(v) for v in pose]).astype(np.int64)
    ac = np.stack([gentries(v) for v in act]).reshape(N, 8, R - 1, V).astype(np.int64)
    sh = np.stack([gentries(v) for v in shown]).reshape(N, 8, N, CAP)
    nb = np.stack([gentries(v) for v in nbr]).reshape(N, 8, D, V)
    for t in range(R):
        new = np.zeros(f.shape, np.float32); turned = np.zeros(p.shape, np.int64)
        for r in range(N):
            for g in range(8):
                fe = np.concatenate([f[r, g]] + [f[q, g][:, sh[q, g, r]] for q in range(N)], 1)
                pe = np.concatenate([p[r, g]] + [p[q, g][sh[q, g, r]] for q in range(N)])
                j = nb[r, g]
                e = rel[r, g][p[r, g][None, :] * 24 + pe[j]].astype(np.int64)
                k = ct[r, g][e[:, :, None] * 24 + np.arange(24)]
                new[r, g] = np.maximum.reduce(fe[:, j[:, :, None], k], axis=1)
                if t < R - 1: turned[r, g] = ct[r, g][p[r, g] * 24 + ac[r, g, t]]
        f = new; p = turned
    return {"y": np.ascontiguousarray(f.reshape(N, 128, V * 24))}

@@ -1,0 +1,432 @@
+import numpy as np
+from concourse.mybir import dt, AluOpType, AxisListType, ActivationFunctionType
+
+F, B, I, U = "float32", "bfloat16", "int32", "uint16"
+
+
+def _s(cols, d):
+    return ("sbuf", [128] + (cols if isinstance(cols, list) else [cols]), d)
+
+
+SCRATCH = {
+    "xs": _s(1536, F), "ish": _s(8, I), "ian": _s(20, I), "reln": _s([2, 24], I),
+    "pi": _s(1, I), "ci": _s(4, I), "cf": _s(4, F), "cc": _s(16, F), "pcols": _s(3, F),
+    "cq": _s(128, B), "cqg": _s(128, B), "cqh": _s(128, B), "c8": _s(96, F), "c24": _s(96, F),
+    "ct5": _s(640, B), "sg": _s(128, B), "sgl": _s(128, B), "sgh": _s(128, B), "tg": _s(128, B), "tgl": _s(128, B),
+    "tgh": _s(128, B), "idf": _s(128, F), "m16": _s(16, B), "gm": _s(8, F),
+    "rn4": _s([4, 16], F), "bd": _s([4, 128], B), "rt": _s([2, 512], B), "rm": _s([2, 512], B), "rte": _s(256, B),
+    "f8": _s(8, F), "f20": _s(20, F), "sps": _s(48, B), "spp": _s(64, B), "spa": _s(64, B), "spn": _s(256, B),
+    "eq": _s([4, 48], B), "ohs": _s([2, 48], B), "oh0": _s([2, 64], B), "oha": _s([2, 64], B), "ohd": _s([2, 64], B),
+    "ohb": _s([2, 64], B), "pbs": _s([2, 64], F), "mbs": _s([2, 64], F),
+    "dg": _s(16, F), "ecol": _s(1, F), "ohe": _s(2, F), "sge": _s([2, 128], B),
+    "ls0": _s(72, U), "l0f": _s(96, F), "l0": _s(96, U), "pfs": _s(96, F), "lrf": _s(384, F), "lr0": _s(384, U),
+    "lr1": _s(128, U), "ls1": _s(24, U), "lfi": _s(96, I), "lfh": _s(96, I), "lft": _s(96, F), "lfu": _s(96, F),
+    "lfv": _s(96, F), "lf": _s(96, U),
+    "snd0": _s(1152, F), "snd1": _s([3, 384], F), "win0": _s(3072, F), "win1": _s(3072, F),
+    "n1a": _s(768, F), "n1b": _s(768, F), "yo": _s(1536, F),
+}
+for _t in range(2):
+    for _k in range(3):
+        for _n in ("ga", "gb", "ma", "mb"):
+            SCRATCH["%s%d%d" % (_n, _t, _k)] = _s(512, F)
+for _b in range(8):
+    SCRATCH["bank%d" % _b] = ("psum", [128, 512], F)
+SEMAPHORES = ["cv", "cs", "ctn", "cg", "arr0", "arr1k0", "arr1k1", "arr1k2", "sent"] + ["ld%d" % i for i in range(8)] + ["st%d" % i for i in range(4)]
+COPY = ActivationFunctionType.Copy
+A = AluOpType
+
+
+def _queues(g, T):
+    q = {"V": g.vector, "S": g.scalar, "T": g.tensor, "G": g, "Y": g.sync}
+    csem = {"V": "cv", "S": "cs", "T": "ctn", "G": "cg"}
+    cnt = {}
+    known = {e: {} for e in q}
+    wrote, read = {}, {}
+
+    def after(e, tok):
+        sem, val, snap = tok[1], tok[2], tok[3]
+        if known[e].get(sem, 0) < val:
+            q[e].wait_ge(T.sem[sem], val)
+            known[e][sem] = val
+            for s, v in snap.items():
+                if known[e].get(s, 0) < v:
+                    known[e][s] = v
+
+    def op(e, fn, reads=(), writes=(), sem=None, inc=1, signal=True):
+        toks = []
+        for k in reads:
+            if k in wrote:
+                toks.append(wrote[k])
+            if k.startswith("bank"):
+                toks += [t for t in read.get(k, []) if t[0] != e]
+        for k in writes:
+            if k in wrote and not (e == "T" and wrote[k][0] == "T"):
+                toks.append(wrote[k])
+            toks += [t for t in read.get(k, []) if t[0] != e]
+        best = {}
+        for t in toks:
+            if t[1] not in best or best[t[1]][2] < t[2]:
+                best[t[1]] = t
+        for t in best.values():
+            after(e, t)
+        ins = fn()
+        if not signal:
+            return
+        name = sem or csem[e]
+        cnt[name] = cnt.get(name, 0) + inc
+        ins.then_inc(T.sem[name], inc)
+        tok = (e, name, cnt[name], dict(known[e]))
+        for k in reads:
+            read.setdefault(k, []).append(tok)
+        for k in writes:
+            wrote[k] = tok
+            read[k] = []
+
+    def wait(e, sem, val):
+        if known[e].get(sem, 0) < val:
+            q[e].wait_ge(T.sem[sem], val)
+            known[e][sem] = val
+    return q, op, wait, cnt
+
+
+def rank_program(g, core, T, topo):
+    r = T.rank_of(core)
+    if r is None:
+        return
+    ranks = list(T.cores)
+    n_ranks = len(ranks)
+    dests = [(r + 1 + j) % n_ranks for j in range(n_ranks - 1)]
+    q, op, wait, cnt = _queues(g, T)
+    v, s, te = g.vector, g.scalar, g.tensor
+    nen = {d: len(topo.engines(core, ranks[d])) for d in dests}
+    nin = sum(len(topo.engines(ranks[d], core)) for d in dests)
+
+    def bank(b):
+        return T["bank%d" % b]
+
+    def ts(out, in0, s1, s2, o0, o1, reads, writes):
+        if o1 is None:
+            op("V", lambda: v.tensor_scalar(out, in0, s1, None, o0), reads, writes)
+        else:
+            op("V", lambda: v.tensor_scalar(out, in0, s1, s2, o0, o1), reads, writes)
+
+    def tt(out, a, b, o, reads, writes):
+        op("V", lambda: v.tensor_tensor(out, a, b, o), reads, writes)
+
+    def vcopy(out, a, reads, writes):
+        op("V", lambda: v.tensor_copy(out, a), reads, writes)
+
+    def act(out, a, reads, writes, scale=None):
+        if scale is None:
+            op("S", lambda: s.activation(out, a, COPY), reads, writes)
+        else:
+            op("S", lambda: s.activation(out, a, COPY, scale=scale), reads, writes)
+
+    def mm(b, c0, n, parts):
+        out = bank(b)[:, c0:c0 + n]
+        for i, (l, rh, keys) in enumerate(parts):
+            op("T", lambda: te.matmul(out, l, rh, i == 0, i == len(parts) - 1), keys, ["bank%d" % b])
+
+    op("Y", lambda: g.sync.dma_start(T.reln[:, 0, :], T.rel[:, 0:384]), [], ["relnA"], "ld0", 16)
+    op("S", lambda: s.dma_start(T.ish[:, 0:4], T.shown[:]), [], ["ishA"], "ld1", 16)
+    op("Y", lambda: g.sync.dma_start(T.reln[:, 1, :], T.rel[:, 192:576]), [], ["relnB"], "ld2", 16)
+    op("S", lambda: s.dma_start(T.ish[:, 4:8], T.pose[:]), [], ["ishB"], "ld3", 16)
+    op("Y", lambda: g.sync.dma_start(T.xs[:], T.x[:]), [], ["xs"], "ld4", 16)
+    op("Y", lambda: g.sync.dma_start(T.ian[:, 0:4], T.act[:]), [], ["ianA"], "ld5", 16)
+    op("Y", lambda: g.sync.dma_start(T.ian[:, 4:20], T.nbr[:]), [], ["ianB"], "ld6", 16)
+
+    def iota(out, pat, base, cm, key, flag=True):
+        if flag:
+            op("G", lambda: g.iota(out, pat, base, cm, allow_small_or_imprecise_dtypes=True), [], [key])
+        else:
+            op("G", lambda: g.iota(out, pat, base, cm), [], [key])
+    iota(T.pi[:], [[1, 1]], 0, 1, "pi", False)
+    iota(T.cq[:], [[1, 128]], 0, 0, "cq")
+    iota(T.cqg[:], [[1, 8], [0, 16]], 0, 0, "cqg")
+    iota(T.pcols[:, 0:1], [[1, 1]], 0, 1, "colP")
+    iota(T.pcols[:, 1:2], [[1, 1]], 8, 1, "colPp8")
+    iota(T.pcols[:, 2:3], [[1, 1]], -8, 1, "colPm8")
+    iota(T.cqh[:], [[1, 16], [0, 8]], 0, 0, "cqh")
+    iota(T.c24[:], [[0, 3], [48, 32]], 0, 0, "c24a")
+    iota(T.c8[:], [[0, 3], [0, 2], [16, 16]], 0, 0, "c8a")
+    op("V", lambda: v.tensor_scalar(T.ci[:, 0:1], T.pi[:], 4, None, A.arith_shift_right), ["pi"], ["ci0"])
+    op("V", lambda: v.tensor_scalar(T.ci[:, 1:2], T.pi[:], 15, None, A.bitwise_and), ["pi"], ["ci1"])
+    op("V", lambda: v.tensor_scalar(T.ci[:, 2:3], T.pi[:], 3, 1, A.arith_shift_right, A.bitwise_and), ["pi"], ["ci2"])
+    op("V", lambda: v.tensor_scalar(T.ci[:, 3:4], T.pi[:], 7, None, A.bitwise_and), ["pi"], ["ci3"])
+    vcopy(T.cf[:], T.ci[:], ["ci0", "ci1", "ci2", "ci3"], ["cf"])
+    gc, pc, hc, k8 = (T.cf[:, j:j + 1] for j in range(4))
+    ccn = {}
+
+    def col(name):
+        return T.cc[:, ccn[name]:ccn[name] + 1]
+
+    def mkcol(name, src, m, a, reads=("cf",)):
+        ccn[name] = len(ccn)
+        ts(col(name), src, float(m), float(a), A.mult, A.add, list(reads), ["c_" + name])
+    ts(T.gm[:], T.cq[:, 0:8], gc, None, A.is_equal, None, ["cq", "cf"], ["gm"])
+    ts(T.m16[:], T.cq[:, 0:16], pc, None, A.is_equal, None, ["cq", "cf"], ["m16"])
+    ts(T.sg[:], T.cqg[:], gc, None, A.is_equal, None, ["cqg", "cf"], ["sg"])
+    mkcol("nh", hc, -1, 1)
+    mkcol("p8", pc, 1, 8)
+    for u in range(1, 4):
+        mkcol("v%d" % u, pc, 1, 16 * u)
+    mkcol("g2", gc, 2, 0)
+    mkcol("g21", gc, 2, 1)
+    colP, colPp8, colPm8 = (T.pcols[:, j:j + 1] for j in range(3))
+    c5 = T.ct5
+    ts(c5[:, 0:128], T.cq[:], colPp8, col("nh"), A.is_equal, A.mult, ["cq", "colPp8", "c_nh"], ["t5b"])
+    ts(c5[:, 128:256], T.cq[:], colP, None, A.is_equal, None, ["cq", "colP"], ["t5i"])
+    ts(c5[:, 256:384], T.cq[:], colPm8, hc, A.is_equal, A.mult, ["cq", "colPm8", "cf"], ["t5a"])
+    ts(T.tg[:], T.cqg[:], gc, 24.0, A.is_equal, A.mult, ["cqg", "cf"], ["tg"])
+    ts(T.tgl[:], T.cqh[:], col("g2"), 24.0, A.is_equal, A.mult, ["cqh", "c_g2"], ["tgl"])
+    ts(T.tgh[:], T.cqh[:], col("g21"), 24.0, A.is_equal, A.mult, ["cqh", "c_g21"], ["tgh"])
+
+    for y in range(2):
+        vcopy(T.rn4[:, y::2, :], T.reln[:, :, 8 * y:8 * y + 16], ["relnA", "relnB"], ["rn4%d" % y])
+    for j in range(8):
+        out, sc = T.bd[:, :, 16 * j:16 * j + 16], T.gm[:, j:j + 1]
+        if j % 2:
+            act(out, T.rn4[:], ["rn40", "rn41", "gm"], ["bd%d" % j], sc)
+        else:
+            ts(out, T.rn4[:], sc, None, A.mult, None, ["rn40", "rn41", "gm"], ["bd%d" % j])
+    bdk = ["bd%d" % j for j in range(8)]
+    for y in range(2):
+        mm(5 + y, 0, 256, [(T.bd[:, y, :], c5[:, 0:256], bdk + ["t5b", "t5i"])])
+        mm(5 + y, 256, 256, [(T.bd[:, 2 + y, :], c5[:, 128:384], bdk + ["t5i", "t5a"])])
+        act(T.rt[:, y, :], bank(5 + y)[:], ["bank%d" % (5 + y)], ["rt%d" % y])
+
+    def rt(y, name):
+        j = {"W": 0, "E1": 1, "E2": 2, "U": 3}[name]
+        return T.rt[:, y, 128 * j:128 * j + 128]
+
+    def rm(y, j):
+        return T.rm[:, y, 128 * j:128 * j + 128]
+
+    def look(name, oh, par, key):
+        return [(rt(y, name), oh[:, y, par::2], ["rt%d" % y, key + str(y)]) for y in range(2)]
+
+    vcopy(T.f8[:], T.ish[:], ["ishA", "ishB"], ["f8"])
+    for j, d in enumerate(dests):
+        ts(T.sps[:, 16 * j:16 * j + 16], T.m16[:], T.f8[:, d:d + 1], None, A.mult, None, ["m16", "f8"], ["sps%d" % j])
+    spk = ["sps0", "sps1", "sps2"]
+    mm(0, 0, 48, [(T.sg[:], T.sps[:], ["sg"] + spk)])
+    vc = [pc] + [col("v%d" % u) for u in range(1, 4)]
+    vk = ["cf", "c_v1", "c_v2", "c_v3"]
+    for u in range(4):
+        ts(T.eq[:, u, :], bank(0)[:, 0:48], vc[u], T.f8[:, 4 + u:5 + u], A.is_equal, A.mult, ["bank0", vk[u], "f8"], ["eq%d" % u])
+    mm(1, 0, 48, [(T.sg[:], T.eq[:, u, :], ["sg", "eq%d" % u]) for u in range(4)])
+
+    def onehot(dst, b, n, key):
+        ts(dst[:, 0, :], bank(b)[:, 0:n], pc, None, A.is_equal, None, ["bank%d" % b, "cf"], [key + "0"])
+        ts(dst[:, 1, :], bank(b)[:, 0:n], col("p8"), hc, A.is_equal, A.mult, ["bank%d" % b, "cf", "c_p8"], [key + "1"])
+    onehot(T.ohs, 1, 48, "ohs")
+    ev, od = T.sps[:, 0::2], T.sps[:, 1::2]
+    mm(2, 0, 24, [(T.tg[:], ev, ["tg"] + spk)] + look("E1", T.ohs, 0, "ohs"))
+    mm(3, 0, 24, [(T.tgl[:], ev, ["tgl"] + spk), (T.tgh[:], od, ["tgh"] + spk)] + look("U", T.ohs, 0, "ohs") + look("W", T.ohs, 1, "ohs"))
+    mm(4, 0, 24, [(T.tg[:], od, ["tg"] + spk)] + look("E2", T.ohs, 1, "ohs"))
+    for c in range(3):
+        vcopy(T.ls0[:, c::3], bank(2 + c)[:, 0:24], ["bank%d" % (2 + c)], ["ls0%d" % c])
+    lsk = ["ls00", "ls01", "ls02", "xs"]
+
+    def slot0(e, a, b, key):
+        src, out = T.xs[:].indirect(T.ls0[:, a:b]), T.snd0[:, 16 * a:16 * b]
+        if e == "V":
+            vcopy(out, src, lsk, [key])
+        else:
+            act(out, src, lsk, [key])
+    slot0("V", 0, 24, "snd0a")
+    slot0("S", 24, 48, "snd0b")
+    slot0("V", 48, 60, "snd0c")
+    slot0("S", 60, 72, "snd0d")
+
+    def send(d, out, src, sem, keys):
+        rid, pid = topo.addr(ranks[d])[:2]
+        op("G", lambda: g.remote_dma(out, src, T.sem[sem], T.sem.sent, pid, rid, topo.mask(core, ranks[d])), keys, [], signal=False)
+    for j, d in enumerate(dests):
+        c0 = 24 * (64 + 16 * r)
+        send(d, T.win0[:, c0:c0 + 384], T.snd0[:, 384 * j:384 * j + 384], "arr0", [["snd0a"], ["snd0b"], ["snd0c", "snd0d"]][j])
+
+    ts(T.c24[:, 32:64], T.c24[:, 32:64], hc, None, A.add, None, ["c24a", "cf"], ["c24h"]) if False else None
+    mkcol("h24", hc, 24, 0)
+    mkcol("h8", hc, 8, 0)
+    mkcol("big", hc, -100, 100)
+    ts(T.c24[:, 32:64], T.c24[:, 32:64], col("h24"), None, A.add, None, ["c24a", "c_h24"], ["c24b"])
+    ts(T.c24[:, 64:96], T.c24[:, 64:96], 24.0, None, A.add, None, ["c24a"], ["c24c"])
+    for u in range(4):
+        ts(T.spp[:, 16 * u:16 * u + 16], T.m16[:], T.f8[:, 4 + u:5 + u], None, A.mult, None, ["m16", "f8"], ["spp%d" % u])
+    mm(0, 0, 64, [(T.sg[:], T.spp[:], ["sg"] + ["spp%d" % u for u in range(4)])])
+    onehot(T.oh0, 0, 64, "oh0")
+    vcopy(T.pbs[:, 0, :], bank(0)[:, 0:64], ["bank0"], ["pbs0"])
+    ts(T.pbs[:, 1, :], bank(0)[:, 0:64], col("big"), None, A.add, None, ["bank0", "c_big"], ["pbs1"])
+
+    def natural(b, oh, key):
+        mm(b, 0, 32, look("E1", oh, 0, key))
+        mm(b, 32, 32, look("U", oh, 0, key) + look("W", oh, 1, key))
+        mm(b, 64, 32, look("E2", oh, 1, key))
+    natural(2, T.oh0, "oh0")
+    tt(T.l0f[:], bank(2)[:, 0:96], T.c24[:], A.add, ["bank2", "c24a", "c24b", "c24c"], ["l0f"])
+    for c in range(3):
+        vcopy(T.l0[:, c::3], T.l0f[:, 32 * c:32 * c + 32], ["l0f"], ["l0%d" % c])
+    l0k = ["l00", "l01", "l02", "xs"]
+    act(T.win0[:, 768:1536], T.xs[:].indirect(T.l0[:, 48:96]), l0k, ["win0b"])
+
+    vcopy(T.f20[:], T.ian[:], ["ianA", "ianB"], ["f20"])
+    for u in range(4):
+        ts(T.spa[:, 16 * u:16 * u + 16], T.m16[:], T.f20[:, u:u + 1], None, A.mult, None, ["m16", "f20"], ["spa%d" % u])
+    mm(1, 0, 64, [(T.sg[:], T.spa[:], ["sg"] + ["spa%d" % u for u in range(4)])])
+    mm(3, 0, 64, [(rt(y, "E1"), T.oh0[:, y, :], ["rt%d" % y, "oh0%d" % y]) for y in range(2)])
+    mm(3, 64, 64, [(rt(y, "E2"), T.oh0[:, y, :], ["rt%d" % y, "oh0%d" % y]) for y in range(2)])
+    vcopy(T.mbs[:, 0, :], bank(1)[:, 0:64], ["bank1"], ["mbs0"])
+    ts(T.mbs[:, 1, :], bank(1)[:, 0:64], col("big"), None, A.add, None, ["bank1", "c_big"], ["mbs1"])
+    for x in range(2):
+        tt(T.oha[:, x, :], bank(3)[:, 64 * x:64 * x + 64], T.mbs[:, x, :], A.is_equal, ["bank3", "mbs%d" % x], ["oha%d" % x])
+    for y in range(2):
+        mm(4, 64 * y, 64, [(T.bd[:, 2 * x + y, :], T.oha[:, x, :], bdk + ["oha%d" % x]) for x in range(2)])
+    ts(c5[:, 384:512], T.cq[:], colP, col("nh"), A.is_equal, A.mult, ["cq", "colP", "c_nh"], ["t5l"])
+    ts(c5[:, 512:640], T.cq[:], colP, hc, A.is_equal, A.mult, ["cq", "colP", "cf"], ["t5h"])
+    for y in range(2):
+        for x in range(2):
+            mm(5 + y, 256 * x, 256, [(T.bd[:, 2 * x + y, :], c5[:, 384:640], bdk + ["t5l", "t5h"])])
+        act(T.rm[:, y, :], bank(5 + y)[:], ["bank%d" % (5 + y)], ["rm%d" % y])
+    vcopy(T.win0[:, 0:768], T.xs[:].indirect(T.l0[:, 0:48]), l0k, ["win0a"])
+    for y in range(2):
+        tt(T.ohd[:, y, :], bank(4)[:, 64 * y:64 * y + 64], T.pbs[:, y, :], A.is_equal, ["bank4", "pbs%d" % y], ["ohd%d" % y])
+    for j in range(16):
+        act(T.spn[:, 16 * j:16 * j + 16], T.m16[:], ["m16", "f20"], ["spn%d" % j], T.f20[:, 4 + j:5 + j])
+    snk = ["spn%d" % j for j in range(16)]
+    tiles = [("M", 0, "R", "W"), ("M", 2, "M", 1), ("R", "U", "M", 3)]
+
+    def half(y, kind, name):
+        return (rt(y, name), "rt%d" % y) if kind == "R" else (rm(y, name), "rm%d" % y)
+    for k, (ka, na, kb, nb) in enumerate(tiles):
+        parts = []
+        for par, kind, name in ((0, ka, na), (1, kb, nb)):
+            for y in range(2):
+                t, key = half(y, kind, name)
+                parts.append((t, T.ohd[:, y, par::2], [key, "ohd%d" % y]))
+        mm(2, 32 * k, 32, parts)
+    vcopy(T.pfs[:], bank(2)[:, 0:96], ["bank2"], ["pfs"])
+    nev, nod = T.spn[:, 0::2], T.spn[:, 1::2]
+    mm(7, 0, 128, [(T.tgl[:], nev, ["tgl"] + snk), (T.tgh[:], nod, ["tgh"] + snk)])
+    for k in range(3):
+        for n in range(4):
+            c = 128 * k + 32 * n
+            tt(T.lrf[:, c:c + 32], bank(7)[:, 32 * n:32 * n + 32], T.pfs[:, 32 * k:32 * k + 32], A.add, ["bank7", "pfs"], ["lrf%d%d" % (k, n)])
+    for k in range(3):
+        vcopy(T.lr0[:, 128 * k:128 * k + 128], T.lrf[:, 128 * k:128 * k + 128], ["lrf%d%d" % (k, n) for n in range(4)], ["lr0%d" % k])
+    ts(T.sgl[:], T.cqh[:], col("g2"), None, A.is_equal, None, ["cqh", "c_g2"], ["sgl"])
+    ts(T.sgh[:], T.cqh[:], col("g21"), None, A.is_equal, None, ["cqh", "c_g21"], ["sgh"])
+    ts(T.idf[:], T.cq[:], colP, None, A.is_equal, None, ["cq", "colP"], ["idf"])
+    mm(1, 0, 24, [(T.sgl[:], ev, ["sgl"] + spk), (T.sgh[:], od, ["sgh"] + spk)])
+    mm(0, 0, 128, [(T.sgl[:], nev, ["sgl"] + snk), (T.sgh[:], nod, ["sgh"] + snk)])
+    ts(T.ls1[:], bank(1)[:, 0:24], 8.0, k8, A.mult, A.add, ["bank1", "cf"], ["ls1"])
+    ts(T.lr1[:], bank(0)[:, 0:128], 8.0, k8, A.mult, A.add, ["bank0", "cf"], ["lr1"])
+    tt(T.dg[:], T.rn4[:, 0, :], T.m16[:], A.mult, ["rn40", "m16"], ["dg"])
+    op("V", lambda: v.tensor_reduce(T.ecol[:], T.dg[:], AxisListType.X, A.add), ["dg"], ["ecol"])
+    ts(T.ohe[:, 0:1], T.cf[:, 1:2], T.ecol[:], None, A.is_equal, None, ["cf", "ecol"], ["ohe0"])
+    ts(T.ohe[:, 1:2], col("p8"), T.ecol[:], hc, A.is_equal, A.mult, ["cf", "c_p8", "ecol"], ["ohe1"])
+    for x in range(2):
+        ts(T.sge[:, x, :], T.sg[:], T.ohe[:, x:x + 1], None, A.mult, None, ["sg", "ohe%d" % x], ["sge%d" % x])
+    for y in range(2):
+        mm(5, 128 * y, 128, [(T.bd[:, 2 * x + y, :], T.sge[:, x, :], bdk + ["sge%d" % x]) for x in range(2)])
+    vcopy(T.rte[:], bank(5)[:, 0:256], ["bank5"], ["rte"])
+    mm(6, 0, 64, [(T.rte[:, 128 * y:128 * y + 128], T.oha[:, y, :], ["rte", "oha%d" % y]) for y in range(2)])
+    onehot(T.ohb, 6, 64, "ohb")
+    natural(3, T.ohb, "ohb")
+    vcopy(T.lfi[:], bank(3)[:, 0:96], ["bank3"], ["lfi"])
+    op("V", lambda: v.tensor_scalar(T.lfh[:], T.lfi[:], 3, None, A.arith_shift_right), ["lfi"], ["lfh"])
+    ts(T.c8[:, 32:64], T.c8[:, 32:64], col("h8"), None, A.add, None, ["c8a", "c_h8"], ["c8b"])
+    ts(T.c8[:, 64:96], T.c8[:, 64:96], 8.0, None, A.add, None, ["c8a"], ["c8c"])
+    ts(T.lft[:], T.lfh[:], 248.0, None, A.mult, None, ["lfh"], ["lft"])
+    tt(T.lfu[:], T.lfi[:], T.c8[:], A.add, ["lfi", "c8a", "c8b", "c8c"], ["lfu"])
+    tt(T.lfv[:], T.lft[:], T.lfu[:], A.add, ["lft", "lfu"], ["lfv"])
+    for c in range(3):
+        vcopy(T.lf[:, c::3], T.lfv[:, 32 * c:32 * c + 32], ["lfv"], ["lf%d" % c])
+    lfk = ["lf0", "lf1", "lf2"]
+
+    def rounds(t):
+        def win(k):
+            return T.win0[:] if t == 0 else T.win1[:, 1024 * k:1024 * k + 1024]
+
+        def lst(k, n, a=0, b=32):
+            c = 128 * k + 32 * n
+            return T.lr0[:, c + a:c + b] if t == 0 else T.lr1[:, 32 * n + a:32 * n + b]
+
+        def keys(k):
+            return ["win0a", "win0b", "lr0%d" % k] if t == 0 else ["f1%d0" % k, "f1%d1" % k, "lr1"]
+
+        def arrived(e, k):
+            if t == 0:
+                wait(e, "arr0", nin)
+            else:
+                wait(e, "arr1k%d" % k, nin)
+
+        def buf(n, k):
+            return T["%s%d%d" % (n, t, k)]
+
+        def bk(n, k, h=None):
+            return "%s%d%d" % (n, t, k) + ("" if h is None else "h%d" % h)
+
+        def target(k, h):
+            if t == 0:
+                return T.win1[:, 1024 * k + 256 * h:1024 * k + 256 * h + 256], "f1%d%d" % (k, h)
+            return T["n1" + "ab"[h]][:, 256 * k:256 * k + 256], "n1%d%d" % (h, k)
+
+        def scalar(k):
+            arrived("S", k)
+            if k == 0:
+                for h in range(2):
+                    act(buf("ga", k)[:, 256 * h:256 * h + 256], win(k).indirect(lst(k, 0, 16 * h, 16 * h + 16)), keys(k), [bk("ga", k, h)])
+                return
+            act(buf("ga", k)[:], win(k).indirect(lst(k, 0)), keys(k), [bk("ga", k)])
+            b = 4 + k + 2 * (t == 0) - 2 * (t == 0)
+            mm(b, 0, 512, [(T.idf[:], buf("ga", k)[:], ["idf", bk("ga", k)])])
+            act(buf("gb", k)[:], win(k).indirect(lst(k, 1)), keys(k), [bk("gb", k)])
+
+        def vector(k):
+            arrived("V", k)
+            hs = [slice(256 * h, 256 * h + 256) for h in range(2)]
+            if k == 0:
+                for n, (src, dst) in enumerate((("ga", "ma"), ("ma", "mb"), ("mb", None)), 1):
+                    for h in range(2):
+                        out, key = (buf(dst, k)[:, hs[h]], bk(dst, k, h)) if dst else target(k, h)
+                        tt(out, win(k).indirect(lst(k, n, 16 * h, 16 * h + 16)), buf(src, k)[:, hs[h]], A.max, keys(k) + [bk(src, k, h)], [key])
+                return
+            b = 4 + k
+            tt(buf("ma", k)[:], bank(b)[:], buf("gb", k)[:], A.max, ["bank%d" % b, bk("gb", k)], [bk("ma", k)])
+            tt(buf("mb", k)[:], win(k).indirect(lst(k, 2)), buf("ma", k)[:], A.max, keys(k) + [bk("ma", k)], [bk("mb", k)])
+            for h in range(2):
+                out, key = target(k, h)
+                tt(out, win(k).indirect(lst(k, 3, 16 * h, 16 * h + 16)), buf("mb", k)[:, hs[h]], A.max, keys(k) + [bk("mb", k)], [key])
+        return scalar, vector
+
+    def slots1(k):
+        act(T.snd1[:, k, :], T.win1[:, 1024 * k:1024 * k + 512].indirect(T.ls1[:]), ["f1%d0" % k, "f1%d1" % k, "ls1"], ["snd1%d" % k])
+        c0 = 1024 * k + 8 * (64 + 16 * r)
+        for j, d in enumerate(dests):
+            send(d, T.win1[:, c0:c0 + 128], T.snd1[:, k, 128 * j:128 * j + 128], "arr1k%d" % k, ["snd1%d" % k])
+
+    s0, v0 = rounds(0)
+    s1, v1 = rounds(1)
+    s0(0)
+    s0(1)
+    v0(0)
+    slots1(0)
+    v0(1)
+    s0(2)
+    slots1(1)
+    v0(2)
+    slots1(2)
+    for k in range(3):
+        s1(k)
+        v1(k)
+    act(T.yo[:, 0:768], T.n1a[:].indirect(T.lf[:, 0:48]), lfk + ["n10%d" % k for k in range(3)], ["yo0"])
+    op("Y", lambda: g.sync.dma_start(T.y[:, 0:768], T.yo[:, 0:768]), ["yo0"], [], "st0", 16)
+    n1k = ["n11%d" % k for k in range(3)]
+    vcopy(T.yo[:, 768:1152], T.n1b[:].indirect(T.lf[:, 48:72]), lfk + n1k, ["yo1"])
+    act(T.yo[:, 1152:1536], T.n1b[:].indirect(T.lf[:, 72:96]), lfk + n1k, ["yo2"])
+    op("Y", lambda: g.sync.dma_start(T.y[:, 768:1152], T.yo[:, 768:1152]), ["yo1"], [], "st1", 16)
+    op("S", lambda: s.dma_start(T.y[:, 1152:1536], T.yo[:, 1152:1536]), ["yo2"], [], "st2", 16)
+    for name in sorted(cnt):
+        wait("Y", name, cnt[name])
+    wait("G", "sent", 4 * sum(nen.values()))

@@ -160,9 +160,9 @@ def rank_program(g, core, T, topo):
     def col(name):
         return T.cc[:, ccn[name]:ccn[name] + 1]
 
-    def mkcol(name, src, m, a, reads=("cf",)):
+    def mkcol(name, src, m, a):
         ccn[name] = len(ccn)
-        ts(col(name), src, float(m), float(a), A.mult, A.add, list(reads), ["c_" + name])
+        ts(col(name), src, float(m), float(a), A.mult, A.add, ["cf"], ["c_" + name])
     ts(T.gm[:], T.cq[:, 0:8], gc, None, A.is_equal, None, ["cq", "cf"], ["gm"])
     ts(T.m16[:], T.cq[:, 0:16], pc, None, A.is_equal, None, ["cq", "cf"], ["m16"])
     ts(T.sg[:], T.cqg[:], gc, None, A.is_equal, None, ["cqg", "cf"], ["sg"])
@@ -246,54 +246,55 @@ def rank_program(g, core, T, topo):
         c0 = 24 * (64 + 16 * r)
         send(d, T.win0[:, c0:c0 + 384], T.snd0[:, 384 * j:384 * j + 384], "arr0", [["snd0a"], ["snd0b"], ["snd0c", "snd0d"]][j])
 
-    ts(T.c24[:, 32:64], T.c24[:, 32:64], hc, None, A.add, None, ["c24a", "cf"], ["c24h"]) if False else None
-    mkcol("h24", hc, 24, 0)
-    mkcol("h8", hc, 8, 0)
-    mkcol("big", hc, -100, 100)
-    ts(T.c24[:, 32:64], T.c24[:, 32:64], col("h24"), None, A.add, None, ["c24a", "c_h24"], ["c24b"])
-    ts(T.c24[:, 64:96], T.c24[:, 64:96], 24.0, None, A.add, None, ["c24a"], ["c24c"])
-    for u in range(4):
-        ts(T.spp[:, 16 * u:16 * u + 16], T.m16[:], T.f8[:, 4 + u:5 + u], None, A.mult, None, ["m16", "f8"], ["spp%d" % u])
-    mm(0, 0, 64, [(T.sg[:], T.spp[:], ["sg"] + ["spp%d" % u for u in range(4)])])
-    onehot(T.oh0, 0, 64, "oh0")
-    vcopy(T.pbs[:, 0, :], bank(0)[:, 0:64], ["bank0"], ["pbs0"])
-    ts(T.pbs[:, 1, :], bank(0)[:, 0:64], col("big"), None, A.add, None, ["bank0", "c_big"], ["pbs1"])
-
     def natural(b, oh, key):
         mm(b, 0, 32, look("E1", oh, 0, key))
         mm(b, 32, 32, look("U", oh, 0, key) + look("W", oh, 1, key))
         mm(b, 64, 32, look("E2", oh, 1, key))
+
+    def tile(name, o1, s1, key, reads, s2=None):
+        ts(o1, T.cq[:] if name == "q" else T.cqh[:], s1, s2, A.is_equal, A.mult if s2 is not None else None, ["c" + ("q" if name == "q" else "qh")] + reads, [key])
+    for u in range(4):
+        ts(T.spp[:, 16 * u:16 * u + 16], T.m16[:], T.f8[:, 4 + u:5 + u], None, A.mult, None, ["m16", "f8"], ["spp%d" % u])
+    mm(0, 0, 64, [(T.sg[:], T.spp[:], ["sg"] + ["spp%d" % u for u in range(4)])])
+    mkcol("h24", hc, 24, 0)
+    mkcol("big", hc, -100, 100)
+    ts(T.c24[:, 32:64], T.c24[:, 32:64], col("h24"), None, A.add, None, ["c24a", "c_h24"], ["c24b"])
+    ts(T.c24[:, 64:96], T.c24[:, 64:96], 24.0, None, A.add, None, ["c24a"], ["c24c"])
+    onehot(T.oh0, 0, 64, "oh0")
     natural(2, T.oh0, "oh0")
+    mm(3, 0, 64, [(rt(y, "E1"), T.oh0[:, y, :], ["rt%d" % y, "oh0%d" % y]) for y in range(2)])
+    mm(3, 64, 64, [(rt(y, "E2"), T.oh0[:, y, :], ["rt%d" % y, "oh0%d" % y]) for y in range(2)])
+    vcopy(T.f20[:], T.ian[:], ["ianA", "ianB"], ["f20"])
+    for u in range(4):
+        ts(T.spa[:, 16 * u:16 * u + 16], T.m16[:], T.f20[:, u:u + 1], None, A.mult, None, ["m16", "f20"], ["spa%d" % u])
+    mm(1, 0, 64, [(T.sg[:], T.spa[:], ["sg"] + ["spa%d" % u for u in range(4)])])
+    for j in range(16):
+        act(T.spn[:, 16 * j:16 * j + 16], T.m16[:], ["m16", "f20"], ["spn%d" % j], T.f20[:, 4 + j:5 + j])
+    snk = ["spn%d" % j for j in range(16)]
     tt(T.l0f[:], bank(2)[:, 0:96], T.c24[:], A.add, ["bank2", "c24a", "c24b", "c24c"], ["l0f"])
     for c in range(3):
         vcopy(T.l0[:, c::3], T.l0f[:, 32 * c:32 * c + 32], ["l0f"], ["l0%d" % c])
     l0k = ["l00", "l01", "l02", "xs"]
     act(T.win0[:, 768:1536], T.xs[:].indirect(T.l0[:, 48:96]), l0k, ["win0b"])
-
-    vcopy(T.f20[:], T.ian[:], ["ianA", "ianB"], ["f20"])
-    for u in range(4):
-        ts(T.spa[:, 16 * u:16 * u + 16], T.m16[:], T.f20[:, u:u + 1], None, A.mult, None, ["m16", "f20"], ["spa%d" % u])
-    mm(1, 0, 64, [(T.sg[:], T.spa[:], ["sg"] + ["spa%d" % u for u in range(4)])])
-    mm(3, 0, 64, [(rt(y, "E1"), T.oh0[:, y, :], ["rt%d" % y, "oh0%d" % y]) for y in range(2)])
-    mm(3, 64, 64, [(rt(y, "E2"), T.oh0[:, y, :], ["rt%d" % y, "oh0%d" % y]) for y in range(2)])
+    vcopy(T.pbs[:, 0, :], bank(0)[:, 0:64], ["bank0"], ["pbs0"])
+    ts(T.pbs[:, 1, :], bank(0)[:, 0:64], col("big"), None, A.add, None, ["bank0", "c_big"], ["pbs1"])
     vcopy(T.mbs[:, 0, :], bank(1)[:, 0:64], ["bank1"], ["mbs0"])
     ts(T.mbs[:, 1, :], bank(1)[:, 0:64], col("big"), None, A.add, None, ["bank1", "c_big"], ["mbs1"])
     for x in range(2):
         tt(T.oha[:, x, :], bank(3)[:, 64 * x:64 * x + 64], T.mbs[:, x, :], A.is_equal, ["bank3", "mbs%d" % x], ["oha%d" % x])
     for y in range(2):
         mm(4, 64 * y, 64, [(T.bd[:, 2 * x + y, :], T.oha[:, x, :], bdk + ["oha%d" % x]) for x in range(2)])
-    ts(c5[:, 384:512], T.cq[:], colP, col("nh"), A.is_equal, A.mult, ["cq", "colP", "c_nh"], ["t5l"])
-    ts(c5[:, 512:640], T.cq[:], colP, hc, A.is_equal, A.mult, ["cq", "colP", "cf"], ["t5h"])
+    tile("q", c5[:, 384:512], colP, "t5l", ["colP", "c_nh"], col("nh"))
+    tile("q", c5[:, 512:640], colP, "t5h", ["colP", "cf"], hc)
     for y in range(2):
         for x in range(2):
             mm(5 + y, 256 * x, 256, [(T.bd[:, 2 * x + y, :], c5[:, 384:640], bdk + ["t5l", "t5h"])])
         act(T.rm[:, y, :], bank(5 + y)[:], ["bank%d" % (5 + y)], ["rm%d" % y])
-    vcopy(T.win0[:, 0:768], T.xs[:].indirect(T.l0[:, 0:48]), l0k, ["win0a"])
     for y in range(2):
         tt(T.ohd[:, y, :], bank(4)[:, 64 * y:64 * y + 64], T.pbs[:, y, :], A.is_equal, ["bank4", "pbs%d" % y], ["ohd%d" % y])
-    for j in range(16):
-        act(T.spn[:, 16 * j:16 * j + 16], T.m16[:], ["m16", "f20"], ["spn%d" % j], T.f20[:, 4 + j:5 + j])
-    snk = ["spn%d" % j for j in range(16)]
+    nev, nod = T.spn[:, 0::2], T.spn[:, 1::2]
+    mm(7, 0, 128, [(T.tgl[:], nev, ["tgl"] + snk), (T.tgh[:], nod, ["tgh"] + snk)])
+    vcopy(T.win0[:, 0:768], T.xs[:].indirect(T.l0[:, 0:48]), l0k, ["win0a"])
     tiles = [("M", 0, "R", "W"), ("M", 2, "M", 1), ("R", "U", "M", 3)]
 
     def half(y, kind, name):
@@ -305,44 +306,50 @@ def rank_program(g, core, T, topo):
                 t, key = half(y, kind, name)
                 parts.append((t, T.ohd[:, y, par::2], [key, "ohd%d" % y]))
         mm(2, 32 * k, 32, parts)
+    tile("h", T.sgl[:], col("g2"), "sgl", ["c_g2"])
+    tile("h", T.sgh[:], col("g21"), "sgh", ["c_g21"])
+    tile("q", T.idf[:], colP, "idf", ["colP"])
+    mm(1, 0, 24, [(T.sgl[:], ev, ["sgl"] + spk), (T.sgh[:], od, ["sgh"] + spk)])
+    mm(0, 0, 128, [(T.sgl[:], nev, ["sgl"] + snk), (T.sgh[:], nod, ["sgh"] + snk)])
     vcopy(T.pfs[:], bank(2)[:, 0:96], ["bank2"], ["pfs"])
-    nev, nod = T.spn[:, 0::2], T.spn[:, 1::2]
-    mm(7, 0, 128, [(T.tgl[:], nev, ["tgl"] + snk), (T.tgh[:], nod, ["tgh"] + snk)])
     for k in range(3):
         for n in range(4):
             c = 128 * k + 32 * n
             tt(T.lrf[:, c:c + 32], bank(7)[:, 32 * n:32 * n + 32], T.pfs[:, 32 * k:32 * k + 32], A.add, ["bank7", "pfs"], ["lrf%d%d" % (k, n)])
-    for k in range(3):
         vcopy(T.lr0[:, 128 * k:128 * k + 128], T.lrf[:, 128 * k:128 * k + 128], ["lrf%d%d" % (k, n) for n in range(4)], ["lr0%d" % k])
-    ts(T.sgl[:], T.cqh[:], col("g2"), None, A.is_equal, None, ["cqh", "c_g2"], ["sgl"])
-    ts(T.sgh[:], T.cqh[:], col("g21"), None, A.is_equal, None, ["cqh", "c_g21"], ["sgh"])
-    ts(T.idf[:], T.cq[:], colP, None, A.is_equal, None, ["cq", "colP"], ["idf"])
-    mm(1, 0, 24, [(T.sgl[:], ev, ["sgl"] + spk), (T.sgh[:], od, ["sgh"] + spk)])
-    mm(0, 0, 128, [(T.sgl[:], nev, ["sgl"] + snk), (T.sgh[:], nod, ["sgh"] + snk)])
     ts(T.ls1[:], bank(1)[:, 0:24], 8.0, k8, A.mult, A.add, ["bank1", "cf"], ["ls1"])
     ts(T.lr1[:], bank(0)[:, 0:128], 8.0, k8, A.mult, A.add, ["bank0", "cf"], ["lr1"])
-    tt(T.dg[:], T.rn4[:, 0, :], T.m16[:], A.mult, ["rn40", "m16"], ["dg"])
-    op("V", lambda: v.tensor_reduce(T.ecol[:], T.dg[:], AxisListType.X, A.add), ["dg"], ["ecol"])
-    ts(T.ohe[:, 0:1], T.cf[:, 1:2], T.ecol[:], None, A.is_equal, None, ["cf", "ecol"], ["ohe0"])
-    ts(T.ohe[:, 1:2], col("p8"), T.ecol[:], hc, A.is_equal, A.mult, ["cf", "c_p8", "ecol"], ["ohe1"])
-    for x in range(2):
-        ts(T.sge[:, x, :], T.sg[:], T.ohe[:, x:x + 1], None, A.mult, None, ["sg", "ohe%d" % x], ["sge%d" % x])
-    for y in range(2):
-        mm(5, 128 * y, 128, [(T.bd[:, 2 * x + y, :], T.sge[:, x, :], bdk + ["sge%d" % x]) for x in range(2)])
-    vcopy(T.rte[:], bank(5)[:, 0:256], ["bank5"], ["rte"])
-    mm(6, 0, 64, [(T.rte[:, 128 * y:128 * y + 128], T.oha[:, y, :], ["rte", "oha%d" % y]) for y in range(2)])
-    onehot(T.ohb, 6, 64, "ohb")
-    natural(3, T.ohb, "ohb")
-    vcopy(T.lfi[:], bank(3)[:, 0:96], ["bank3"], ["lfi"])
-    op("V", lambda: v.tensor_scalar(T.lfh[:], T.lfi[:], 3, None, A.arith_shift_right), ["lfi"], ["lfh"])
-    ts(T.c8[:, 32:64], T.c8[:, 32:64], col("h8"), None, A.add, None, ["c8a", "c_h8"], ["c8b"])
-    ts(T.c8[:, 64:96], T.c8[:, 64:96], 8.0, None, A.add, None, ["c8a"], ["c8c"])
-    ts(T.lft[:], T.lfh[:], 248.0, None, A.mult, None, ["lfh"], ["lft"])
-    tt(T.lfu[:], T.lfi[:], T.c8[:], A.add, ["lfi", "c8a", "c8b", "c8c"], ["lfu"])
-    tt(T.lfv[:], T.lft[:], T.lfu[:], A.add, ["lft", "lfu"], ["lfv"])
-    for c in range(3):
-        vcopy(T.lf[:, c::3], T.lfv[:, 32 * c:32 * c + 32], ["lfv"], ["lf%d" % c])
+
+    def last1():
+        tt(T.dg[:], T.rn4[:, 0, :], T.m16[:], A.mult, ["rn40", "m16"], ["dg"])
+        mkcol("h8", hc, 8, 0)
+        op("V", lambda: v.tensor_reduce(T.ecol[:], T.dg[:], AxisListType.X, A.add), ["dg"], ["ecol"])
+        ts(T.c8[:, 32:64], T.c8[:, 32:64], col("h8"), None, A.add, None, ["c8a", "c_h8"], ["c8b"])
+        ts(T.c8[:, 64:96], T.c8[:, 64:96], 8.0, None, A.add, None, ["c8a"], ["c8c"])
+        ts(T.ohe[:, 0:1], pc, T.ecol[:], None, A.is_equal, None, ["cf", "ecol"], ["ohe0"])
+        ts(T.ohe[:, 1:2], col("p8"), T.ecol[:], hc, A.is_equal, A.mult, ["cf", "c_p8", "ecol"], ["ohe1"])
+        for x in range(2):
+            ts(T.sge[:, x, :], T.sg[:], T.ohe[:, x:x + 1], None, A.mult, None, ["sg", "ohe%d" % x], ["sge%d" % x])
+        for y in range(2):
+            mm(7, 128 * y, 128, [(T.bd[:, 2 * x + y, :], T.sge[:, x, :], bdk + ["sge%d" % x]) for x in range(2)])
+        vcopy(T.rte[:], bank(7)[:, 0:256], ["bank7"], ["rte"])
+        mm(0, 0, 64, [(T.rte[:, 128 * y:128 * y + 128], T.oha[:, y, :], ["rte", "oha%d" % y]) for y in range(2)])
+
+    def last2():
+        onehot(T.ohb, 0, 64, "ohb")
+        natural(3, T.ohb, "ohb")
+
+    def last3():
+        vcopy(T.lfi[:], bank(3)[:, 0:96], ["bank3"], ["lfi"])
+        op("V", lambda: v.tensor_scalar(T.lfh[:], T.lfi[:], 3, None, A.arith_shift_right), ["lfi"], ["lfh"])
+        tt(T.lfu[:], T.lfi[:], T.c8[:], A.add, ["lfi", "c8a", "c8b", "c8c"], ["lfu"])
+        ts(T.lft[:], T.lfh[:], 248.0, None, A.mult, None, ["lfh"], ["lft"])
+        tt(T.lfv[:], T.lft[:], T.lfu[:], A.add, ["lft", "lfu"], ["lfv"])
+        for c in range(3):
+            vcopy(T.lf[:, c::3], T.lfv[:, 32 * c:32 * c + 32], ["lfv"], ["lf%d" % c])
     lfk = ["lf0", "lf1", "lf2"]
+
+    hs = [slice(256 * h, 256 * h + 256) for h in range(2)]
 
     def rounds(t):
         def win(k):
@@ -356,10 +363,7 @@ def rank_program(g, core, T, topo):
             return ["win0a", "win0b", "lr0%d" % k] if t == 0 else ["f1%d0" % k, "f1%d1" % k, "lr1"]
 
         def arrived(e, k):
-            if t == 0:
-                wait(e, "arr0", nin)
-            else:
-                wait(e, "arr1k%d" % k, nin)
+            wait(e, "arr0" if t == 0 else "arr1k%d" % k, nin)
 
         def buf(n, k):
             return T["%s%d%d" % (n, t, k)]
@@ -376,28 +380,33 @@ def rank_program(g, core, T, topo):
             arrived("S", k)
             if k == 0:
                 for h in range(2):
-                    act(buf("ga", k)[:, 256 * h:256 * h + 256], win(k).indirect(lst(k, 0, 16 * h, 16 * h + 16)), keys(k), [bk("ga", k, h)])
+                    act(buf("ga", k)[:, hs[h]], win(k).indirect(lst(k, 0, 16 * h, 16 * h + 16)), keys(k), [bk("ga", k, h)])
                 return
             act(buf("ga", k)[:], win(k).indirect(lst(k, 0)), keys(k), [bk("ga", k)])
-            b = 4 + k + 2 * (t == 0) - 2 * (t == 0)
-            mm(b, 0, 512, [(T.idf[:], buf("ga", k)[:], ["idf", bk("ga", k)])])
+            mm(4 + k, 0, 512, [(T.idf[:], buf("ga", k)[:], ["idf", bk("ga", k)])])
             act(buf("gb", k)[:], win(k).indirect(lst(k, 1)), keys(k), [bk("gb", k)])
+
+        def part(k, n, h, src, skey, dst):
+            out, key = (buf(dst, k)[:, hs[h]], bk(dst, k, h)) if dst else target(k, h)
+            tt(out, win(k).indirect(lst(k, n, 16 * h, 16 * h + 16)), buf(src, k)[:, hs[h]], A.max, keys(k) + [skey], [key])
 
         def vector(k):
             arrived("V", k)
-            hs = [slice(256 * h, 256 * h + 256) for h in range(2)]
             if k == 0:
                 for n, (src, dst) in enumerate((("ga", "ma"), ("ma", "mb"), ("mb", None)), 1):
                     for h in range(2):
-                        out, key = (buf(dst, k)[:, hs[h]], bk(dst, k, h)) if dst else target(k, h)
-                        tt(out, win(k).indirect(lst(k, n, 16 * h, 16 * h + 16)), buf(src, k)[:, hs[h]], A.max, keys(k) + [bk(src, k, h)], [key])
+                        part(k, n, h, src, bk(src, k, h), dst)
                 return
             b = 4 + k
             tt(buf("ma", k)[:], bank(b)[:], buf("gb", k)[:], A.max, ["bank%d" % b, bk("gb", k)], [bk("ma", k)])
+            if t == 1 and k == 2:
+                for h in range(2):
+                    part(k, 2, h, "ma", bk("ma", k), "mb")
+                    part(k, 3, h, "mb", bk("mb", k, h), None)
+                return
             tt(buf("mb", k)[:], win(k).indirect(lst(k, 2)), buf("ma", k)[:], A.max, keys(k) + [bk("ma", k)], [bk("mb", k)])
             for h in range(2):
-                out, key = target(k, h)
-                tt(out, win(k).indirect(lst(k, 3, 16 * h, 16 * h + 16)), buf("mb", k)[:, hs[h]], A.max, keys(k) + [bk("mb", k)], [key])
+                part(k, 3, h, "mb", bk("mb", k), None)
         return scalar, vector
 
     def slots1(k):
@@ -417,16 +426,28 @@ def rank_program(g, core, T, topo):
     slots1(1)
     v0(2)
     slots1(2)
-    for k in range(3):
-        s1(k)
-        v1(k)
-    act(T.yo[:, 0:768], T.n1a[:].indirect(T.lf[:, 0:48]), lfk + ["n10%d" % k for k in range(3)], ["yo0"])
-    op("Y", lambda: g.sync.dma_start(T.y[:, 0:768], T.yo[:, 0:768]), ["yo0"], [], "st0", 16)
-    n1k = ["n11%d" % k for k in range(3)]
-    vcopy(T.yo[:, 768:1152], T.n1b[:].indirect(T.lf[:, 48:72]), lfk + n1k, ["yo1"])
-    act(T.yo[:, 1152:1536], T.n1b[:].indirect(T.lf[:, 72:96]), lfk + n1k, ["yo2"])
-    op("Y", lambda: g.sync.dma_start(T.y[:, 768:1152], T.yo[:, 768:1152]), ["yo1"], [], "st1", 16)
-    op("S", lambda: s.dma_start(T.y[:, 1152:1536], T.yo[:, 1152:1536]), ["yo2"], [], "st2", 16)
+    last1()
+    s1(0)
+    s1(1)
+    v1(0)
+    last2()
+    s1(2)
+    v1(1)
+    last3()
+    v1(2)
+
+    def final(e, c, win, keys):
+        out, src = T.yo[:, 384 * c:384 * c + 384], T[win][:].indirect(T.lf[:, 24 * c:24 * c + 24])
+        if e == "V":
+            vcopy(out, src, lfk + keys, ["yo%d" % c])
+        else:
+            act(out, src, lfk + keys, ["yo%d" % c])
+        op("Y", lambda: g.sync.dma_start(T.y[:, 384 * c:384 * c + 384], T.yo[:, 384 * c:384 * c + 384]), ["yo%d" % c], [], "st%d" % c, 16)
+    ka, kb = ["n10%d" % k for k in range(3)], ["n11%d" % k for k in range(3)]
+    final("S", 0, "n1a", ka)
+    final("S", 1, "n1a", ka)
+    final("V", 2, "n1b", kb)
+    final("S", 3, "n1b", kb)
     for name in sorted(cnt):
         wait("Y", name, cnt[name])
-    wait("G", "sent", 4 * sum(nen.values()))
+    wait("G", "sent", (1 + 3) * sum(nen.values()))

@@ -1,4 +1,5 @@
 import numpy as np
+from concourse.bass import DstId, RemoteDMATransfer
 from concourse.mybir import dt, AluOpType, AxisListType, ActivationFunctionType
 
 F, B, I, U = "float32", "bfloat16", "int32", "uint16"
@@ -9,19 +10,19 @@ def _s(cols, d):
 
 
 SCRATCH = {
-    "xs": _s(1536, F), "ish": _s(8, I), "ian": _s(20, I), "reln": _s([2, 24], I),
-    "pi": _s(1, I), "ci": _s(4, I), "cf": _s(4, F), "cc": _s(16, F), "pcols": _s(3, F),
+    "xs": _s(1536, F), "ish": _s(8, I), "iact": _s(4, I), "inbr": _s(16, I), "reln": _s([2, 24], I),
+    "pi": _s(1, I), "ci": _s(4, I), "cf": _s(4, F), "cc": _s(16, F), "pcols": _s(3, F), "one": _s(128, B), "onef": _s(128, F),
     "cq": _s(128, B), "cqg": _s(128, B), "cqh": _s(128, B), "c8": _s(96, F), "c24": _s(96, F),
-    "ct5": _s(640, B), "sg": _s(128, B), "sgl": _s(128, B), "sgh": _s(128, B), "tg": _s(128, B), "tgl": _s(128, B),
-    "tgh": _s(128, B), "idf": _s(128, F), "m16": _s(16, B), "gm": _s(8, F),
+    "ct5": _s(640, B), "sg": _s(128, B), "tg": _s(128, B), "tgl": _s(128, B), "tgh": _s(128, B), "sel": _s([8, 128], B),
+    "idf": _s(128, F), "m16": _s(16, B), "gm": _s(8, F),
     "rn4": _s([4, 16], F), "bd": _s([4, 128], B), "rt": _s([2, 512], B), "rm": _s([2, 512], B), "rte": _s(256, B),
-    "f8": _s(8, F), "f20": _s(20, F), "sps": _s(48, B), "spp": _s(64, B), "spa": _s(64, B), "spn": _s(256, B),
+    "f8": _s(8, F), "f4": _s(4, F), "sps": _s(48, B), "spp": _s(64, B), "spa": _s(64, B), "nb8": _s(16, B), "ns8": _s(8, B),
     "eq": _s([4, 48], B), "ohs": _s([2, 48], B), "oh0": _s([2, 64], B), "oha": _s([2, 64], B), "ohd": _s([2, 64], B),
     "ohb": _s([2, 64], B), "pbs": _s([2, 64], F), "mbs": _s([2, 64], F),
     "dg": _s(16, F), "ecol": _s(1, F), "ohe": _s(2, F), "sge": _s([2, 128], B),
-    "ls0": _s(72, U), "l0f": _s(96, F), "l0": _s(96, U), "pfs": _s(96, F), "lrf": _s(384, F), "lr0": _s(384, U),
-    "lr1": _s(128, U), "ls1": _s(24, U), "lfi": _s(96, I), "lfh": _s(96, I), "lft": _s(96, F), "lfu": _s(96, F),
-    "lfv": _s(96, F), "lf": _s(96, U),
+    "ls0": _s(72, U), "l0f": _s(96, F), "l0": _s(96, U), "pfs": _s(96, F), "lrf": _s(384, F),
+    "lr0": _s(384, U), "lr1": _s(128, U), "ls1": _s(24, U), "lfa": _s(96, F), "lfb": _s(96, F), "lfc": _s(96, F),
+    "lfd": _s(96, F), "lfe": _s(96, F), "lf": _s(96, U),
     "snd0": _s(1152, F), "snd1": _s([3, 384], F), "win0": _s(3072, F), "win1": _s(3072, F),
     "n1a": _s(768, F), "n1b": _s(768, F), "yo": _s(1536, F),
 }
@@ -32,7 +33,7 @@ for _t in range(2):
 for _b in range(8):
     SCRATCH["bank%d" % _b] = ("psum", [128, 512], F)
 SEMAPHORES = ["cv", "cs", "ctn", "cg", "arr0", "arr1k0", "arr1k1", "arr1k2", "sent"] + ["ld%d" % i for i in range(8)] + ["st%d" % i for i in range(4)]
-COPY = ActivationFunctionType.Copy
+COPY, IDENT = ActivationFunctionType.Copy, ActivationFunctionType.Identity
 A = AluOpType
 
 
@@ -98,8 +99,13 @@ def rank_program(g, core, T, topo):
     dests = [(r + 1 + j) % n_ranks for j in range(n_ranks - 1)]
     q, op, wait, cnt = _queues(g, T)
     v, s, te = g.vector, g.scalar, g.tensor
-    nen = {d: len(topo.engines(core, ranks[d])) for d in dests}
-    nin = sum(len(topo.engines(ranks[d], core)) for d in dests)
+
+    def share(a, b, j):
+        es = topo.engines(a, b)
+        h = len(es) // 2
+        return (es[:h], es[h:], es)[j]
+    nout = sum(len(share(core, ranks[d], j)) for j, d in enumerate(dests))
+    nin = sum(len(share(ranks[(r - 1 - j) % n_ranks], core, j)) for j in range(n_ranks - 1))
 
     def bank(b):
         return T["bank%d" % b]
@@ -116,24 +122,28 @@ def rank_program(g, core, T, topo):
     def vcopy(out, a, reads, writes):
         op("V", lambda: v.tensor_copy(out, a), reads, writes)
 
-    def act(out, a, reads, writes, scale=None):
-        if scale is None:
+    def act(out, a, reads, writes, scale=None, bias=None):
+        if bias is not None:
+            op("S", lambda: s.activation(out, a, IDENT, bias=bias), reads, writes)
+        elif scale is None:
             op("S", lambda: s.activation(out, a, COPY), reads, writes)
         else:
             op("S", lambda: s.activation(out, a, COPY, scale=scale), reads, writes)
 
-    def mm(b, c0, n, parts):
-        out = bank(b)[:, c0:c0 + n]
+    def mmo(b, out, parts, first=True, last=True):
         for i, (l, rh, keys) in enumerate(parts):
-            op("T", lambda: te.matmul(out, l, rh, i == 0, i == len(parts) - 1), keys, ["bank%d" % b])
+            op("T", lambda: te.matmul(out, l, rh, first and i == 0, last and i == len(parts) - 1), keys, ["bank%d" % b])
+
+    def mm(b, c0, n, parts, first=True, last=True):
+        mmo(b, bank(b)[:, c0:c0 + n], parts, first, last)
 
     op("Y", lambda: g.sync.dma_start(T.reln[:, 0, :], T.rel[:, 0:384]), [], ["relnA"], "ld0", 16)
     op("S", lambda: s.dma_start(T.ish[:, 0:4], T.shown[:]), [], ["ishA"], "ld1", 16)
     op("Y", lambda: g.sync.dma_start(T.reln[:, 1, :], T.rel[:, 192:576]), [], ["relnB"], "ld2", 16)
     op("S", lambda: s.dma_start(T.ish[:, 4:8], T.pose[:]), [], ["ishB"], "ld3", 16)
+    op("S", lambda: s.dma_start(T.iact[:], T.act[:]), [], ["iact"], "ld5", 16)
     op("Y", lambda: g.sync.dma_start(T.xs[:], T.x[:]), [], ["xs"], "ld4", 16)
-    op("Y", lambda: g.sync.dma_start(T.ian[:, 0:4], T.act[:]), [], ["ianA"], "ld5", 16)
-    op("Y", lambda: g.sync.dma_start(T.ian[:, 4:20], T.nbr[:]), [], ["ianB"], "ld6", 16)
+    op("Y", lambda: g.sync.dma_start(T.inbr[:], T.nbr[:]), [], ["inbr"], "ld6", 16)
 
     def iota(out, pat, base, cm, key, flag=True):
         if flag:
@@ -143,12 +153,17 @@ def rank_program(g, core, T, topo):
     iota(T.pi[:], [[1, 1]], 0, 1, "pi", False)
     iota(T.cq[:], [[1, 128]], 0, 0, "cq")
     iota(T.cqg[:], [[1, 8], [0, 16]], 0, 0, "cqg")
-    iota(T.pcols[:, 0:1], [[1, 1]], 0, 1, "colP")
-    iota(T.pcols[:, 1:2], [[1, 1]], 8, 1, "colPp8")
-    iota(T.pcols[:, 2:3], [[1, 1]], -8, 1, "colPm8")
     iota(T.cqh[:], [[1, 16], [0, 8]], 0, 0, "cqh")
-    iota(T.c24[:], [[0, 3], [48, 32]], 0, 0, "c24a")
-    iota(T.c8[:], [[0, 3], [0, 2], [16, 16]], 0, 0, "c8a")
+    iota(T.pcols[:, 1:2], [[1, 1]], 8, 1, "colPp8")
+    iota(T.pcols[:, 0:1], [[1, 1]], 0, 1, "colP")
+    iota(T.pcols[:, 2:3], [[1, 1]], -8, 1, "colPm8")
+    iota(T.c24[:], [[48, 32], [0, 3]], 0, 0, "c24a")
+    iota(T.c8[:], [[0, 2], [16, 16], [0, 3]], 0, 0, "c8a")
+    iota(T.one[:], [[0, 128]], 1, 0, "one")
+    for m in range(8):
+        op("G", lambda: g.affine_select(T.sel[:, m, :], T.one[:], [[16, 8], [1, 2], [0, 8]], A.is_equal, 0.0, 2 * m, -1), ["one"], ["sel%d" % m])
+    iota(T.onef[:], [[0, 128]], 1, 0, "onef")
+    op("G", lambda: g.affine_select(T.idf[:], T.onef[:], [[1, 128]], A.is_equal, 0.0, 0, -1), ["onef"], ["idf"])
     op("V", lambda: v.tensor_scalar(T.ci[:, 0:1], T.pi[:], 4, None, A.arith_shift_right), ["pi"], ["ci0"])
     op("V", lambda: v.tensor_scalar(T.ci[:, 1:2], T.pi[:], 15, None, A.bitwise_and), ["pi"], ["ci1"])
     op("V", lambda: v.tensor_scalar(T.ci[:, 2:3], T.pi[:], 3, 1, A.arith_shift_right, A.bitwise_and), ["pi"], ["ci2"])
@@ -165,24 +180,35 @@ def rank_program(g, core, T, topo):
         ts(col(name), src, float(m), float(a), A.mult, A.add, ["cf"], ["c_" + name])
     ts(T.gm[:], T.cq[:, 0:8], gc, None, A.is_equal, None, ["cq", "cf"], ["gm"])
     ts(T.m16[:], T.cq[:, 0:16], pc, None, A.is_equal, None, ["cq", "cf"], ["m16"])
-    ts(T.sg[:], T.cqg[:], gc, None, A.is_equal, None, ["cqg", "cf"], ["sg"])
     mkcol("nh", hc, -1, 1)
+    mkcol("g2", gc, 2, 0)
+    mkcol("g21", gc, 2, 1)
+    ts(T.sg[:], T.cqg[:], gc, None, A.is_equal, None, ["cqg", "cf"], ["sg"])
     mkcol("p8", pc, 1, 8)
     for u in range(1, 4):
         mkcol("v%d" % u, pc, 1, 16 * u)
-    mkcol("g2", gc, 2, 0)
-    mkcol("g21", gc, 2, 1)
     colP, colPp8, colPm8 = (T.pcols[:, j:j + 1] for j in range(3))
     c5 = T.ct5
-    ts(c5[:, 0:128], T.cq[:], colPp8, col("nh"), A.is_equal, A.mult, ["cq", "colPp8", "c_nh"], ["t5b"])
-    ts(c5[:, 128:256], T.cq[:], colP, None, A.is_equal, None, ["cq", "colP"], ["t5i"])
-    ts(c5[:, 256:384], T.cq[:], colPm8, hc, A.is_equal, A.mult, ["cq", "colPm8", "cf"], ["t5a"])
-    ts(T.tg[:], T.cqg[:], gc, 24.0, A.is_equal, A.mult, ["cqg", "cf"], ["tg"])
-    ts(T.tgl[:], T.cqh[:], col("g2"), 24.0, A.is_equal, A.mult, ["cqh", "c_g2"], ["tgl"])
-    ts(T.tgh[:], T.cqh[:], col("g21"), 24.0, A.is_equal, A.mult, ["cqh", "c_g21"], ["tgh"])
 
+    def tile(o1, src, s1, key, reads, s2=None):
+        ts(o1, T[src][:], s1, s2, A.is_equal, A.mult if s2 is not None else None, [src] + reads, [key])
+    tile(T.tg[:], "cqg", gc, "tg", ["cf"], 24.0)
+    tile(T.tgl[:], "cqh", col("g2"), "tgl", ["c_g2"], 24.0)
+    tile(T.tgh[:], "cqh", col("g21"), "tgh", ["c_g21"], 24.0)
+    tile(c5[:, 0:128], "cq", colPp8, "t5b", ["colPp8", "c_nh"], col("nh"))
+    tile(c5[:, 128:256], "cq", colP, "t5i", ["colP"])
+    tile(c5[:, 256:384], "cq", colPm8, "t5a", ["colPm8", "cf"], hc)
+    mkcol("h24", hc, 24, 0)
+    mkcol("big", hc, -100, 100)
+    tile(c5[:, 384:512], "cq", colP, "t5l", ["colP", "c_nh"], col("nh"))
+    tile(c5[:, 512:640], "cq", colP, "t5h", ["colP", "cf"], hc)
+
+    vcopy(T.f8[:], T.ish[:], ["ishA", "ishB"], ["f8"])
     for y in range(2):
         vcopy(T.rn4[:, y::2, :], T.reln[:, :, 8 * y:8 * y + 16], ["relnA", "relnB"], ["rn4%d" % y])
+    for j, d in enumerate(dests):
+        ts(T.sps[:, 16 * j:16 * j + 16], T.m16[:], T.f8[:, d:d + 1], None, A.mult, None, ["m16", "f8"], ["sps%d" % j])
+    spk = ["sps0", "sps1", "sps2"]
     for j in range(8):
         out, sc = T.bd[:, :, 16 * j:16 * j + 16], T.gm[:, j:j + 1]
         if j % 2:
@@ -190,6 +216,16 @@ def rank_program(g, core, T, topo):
         else:
             ts(out, T.rn4[:], sc, None, A.mult, None, ["rn40", "rn41", "gm"], ["bd%d" % j])
     bdk = ["bd%d" % j for j in range(8)]
+    vcopy(T.f4[:], T.iact[:], ["iact"], ["f4"])
+    for u in range(4):
+        act(T.spp[:, 16 * u:16 * u + 16], T.m16[:], ["m16", "f8"], ["spp%d" % u], T.f8[:, 4 + u:5 + u])
+    for u in range(4):
+        act(T.spa[:, 16 * u:16 * u + 16], T.m16[:], ["m16", "f4"], ["spa%d" % u], T.f4[:, u:u + 1])
+    ev, od = T.sps[:, 0::2], T.sps[:, 1::2]
+    mm(0, 0, 48, [(T.sg[:], T.sps[:], ["sg"] + spk)])
+    mm(2, 0, 24, [(T.tg[:], ev, ["tg"] + spk)], last=False)
+    mm(3, 0, 24, [(T.tgl[:], ev, ["tgl"] + spk), (T.tgh[:], od, ["tgh"] + spk)], last=False)
+    mm(4, 0, 24, [(T.tg[:], od, ["tg"] + spk)], last=False)
     for y in range(2):
         mm(5 + y, 0, 256, [(T.bd[:, y, :], c5[:, 0:256], bdk + ["t5b", "t5i"])])
         mm(5 + y, 256, 256, [(T.bd[:, 2 + y, :], c5[:, 128:384], bdk + ["t5i", "t5a"])])
@@ -205,25 +241,35 @@ def rank_program(g, core, T, topo):
     def look(name, oh, par, key):
         return [(rt(y, name), oh[:, y, par::2], ["rt%d" % y, key + str(y)]) for y in range(2)]
 
-    vcopy(T.f8[:], T.ish[:], ["ishA", "ishB"], ["f8"])
-    for j, d in enumerate(dests):
-        ts(T.sps[:, 16 * j:16 * j + 16], T.m16[:], T.f8[:, d:d + 1], None, A.mult, None, ["m16", "f8"], ["sps%d" % j])
-    spk = ["sps0", "sps1", "sps2"]
-    mm(0, 0, 48, [(T.sg[:], T.sps[:], ["sg"] + spk)])
     vc = [pc] + [col("v%d" % u) for u in range(1, 4)]
     vk = ["cf", "c_v1", "c_v2", "c_v3"]
     for u in range(4):
         ts(T.eq[:, u, :], bank(0)[:, 0:48], vc[u], T.f8[:, 4 + u:5 + u], A.is_equal, A.mult, ["bank0", vk[u], "f8"], ["eq%d" % u])
     mm(1, 0, 48, [(T.sg[:], T.eq[:, u, :], ["sg", "eq%d" % u]) for u in range(4)])
+    mm(7, 0, 64, [(T.sg[:], T.spp[:], ["sg"] + ["spp%d" % u for u in range(4)])])
+    mm(0, 0, 64, [(T.sg[:], T.spa[:], ["sg"] + ["spa%d" % u for u in range(4)])])
+    for t, b in (("pbs", 7), ("mbs", 0)):
+        act(T[t][:, 0, :], bank(b)[:, 0:64], ["bank%d" % b], [t + "0"])
+        act(T[t][:, 1, :], bank(b)[:, 0:64], ["bank%d" % b, "c_big"], [t + "1"], bias=col("big"))
+    tt(T.dg[:], T.rn4[:, 0, :], T.m16[:], A.mult, ["rn40", "m16"], ["dg"])
+    ts(T.c24[:, 1::3], T.c24[:, 1::3], col("h24"), None, A.add, None, ["c24a", "c_h24"], ["c24b"])
+    ts(T.c24[:, 2::3], T.c24[:, 2::3], 24.0, None, A.add, None, ["c24a"], ["c24c"])
+    op("V", lambda: v.tensor_reduce(T.ecol[:], T.dg[:], AxisListType.X, A.add), ["dg"], ["ecol"])
+    for j in range(2):
+        ts(T.ns8[:, 4 * j:4 * j + 4], T.f8[:, 0:4], 8.0, None, A.mult, None, ["f8"], ["ns8%d" % j])
+    ts(T.ohe[:, 0:1], pc, T.ecol[:], None, A.is_equal, None, ["cf", "ecol"], ["ohe0"])
+    ts(T.ohe[:, 1:2], col("p8"), T.ecol[:], hc, A.is_equal, A.mult, ["cf", "c_p8", "ecol"], ["ohe1"])
 
     def onehot(dst, b, n, key):
         ts(dst[:, 0, :], bank(b)[:, 0:n], pc, None, A.is_equal, None, ["bank%d" % b, "cf"], [key + "0"])
         ts(dst[:, 1, :], bank(b)[:, 0:n], col("p8"), hc, A.is_equal, A.mult, ["bank%d" % b, "cf", "c_p8"], [key + "1"])
     onehot(T.ohs, 1, 48, "ohs")
-    ev, od = T.sps[:, 0::2], T.sps[:, 1::2]
-    mm(2, 0, 24, [(T.tg[:], ev, ["tg"] + spk)] + look("E1", T.ohs, 0, "ohs"))
-    mm(3, 0, 24, [(T.tgl[:], ev, ["tgl"] + spk), (T.tgh[:], od, ["tgh"] + spk)] + look("U", T.ohs, 0, "ohs") + look("W", T.ohs, 1, "ohs"))
-    mm(4, 0, 24, [(T.tg[:], od, ["tg"] + spk)] + look("E2", T.ohs, 1, "ohs"))
+    mm(2, 0, 24, look("E1", T.ohs, 0, "ohs"), first=False)
+    mm(3, 0, 24, look("U", T.ohs, 0, "ohs") + look("W", T.ohs, 1, "ohs"), first=False)
+    mm(4, 0, 24, look("E2", T.ohs, 1, "ohs"), first=False)
+    onehot(T.oh0, 7, 64, "oh0")
+    for x in range(2):
+        ts(T.sge[:, x, :], T.sg[:], T.ohe[:, x:x + 1], None, A.mult, None, ["sg", "ohe%d" % x], ["sge%d" % x])
     for c in range(3):
         vcopy(T.ls0[:, c::3], bank(2 + c)[:, 0:24], ["bank%d" % (2 + c)], ["ls0%d" % c])
     lsk = ["ls00", "ls01", "ls02", "xs"]
@@ -239,62 +285,44 @@ def rank_program(g, core, T, topo):
     slot0("V", 48, 60, "snd0c")
     slot0("S", 60, 72, "snd0d")
 
-    def send(d, out, src, sem, keys):
-        rid, pid = topo.addr(ranks[d])[:2]
-        op("G", lambda: g.remote_dma(out, src, T.sem[sem], T.sem.sent, pid, rid, topo.mask(core, ranks[d])), keys, [], signal=False)
-    for j, d in enumerate(dests):
-        c0 = 24 * (64 + 16 * r)
-        send(d, T.win0[:, c0:c0 + 384], T.snd0[:, 384 * j:384 * j + 384], "arr0", [["snd0a"], ["snd0b"], ["snd0c", "snd0d"]][j])
+    def send(out, srcs, sem, keys):
+        mask = [sum(1 << e for e in share(core, ranks[d], j)) for j, d in enumerate(dests)]
+        at = [topo.addr(ranks[d])[:2] for d in dests]
+        two = [RemoteDMATransfer(dst_ids=[DstId(rid=at[j][0], pnc=at[j][1])], dma_engine_mask=mask[j], remote_sem=T.sem[sem], srcs=[srcs[j]], dsts=[out], alu_op=0) for j in range(2)]
+        op("G", lambda: g.remote_dma_fused(two, local_sem=T.sem.sent), keys[0] + keys[1], [], signal=False)
+        op("G", lambda: g.remote_dma(out, srcs[2], T.sem[sem], T.sem.sent, at[2][1], at[2][0], mask[2]), keys[2], [], signal=False)
+    c0 = 24 * (64 + 16 * r)
+    send(T.win0[:, c0:c0 + 384], [T.snd0[:, 384 * j:384 * j + 384] for j in range(3)], "arr0", [["snd0a"], ["snd0b"], ["snd0c", "snd0d"]])
 
     def natural(b, oh, key):
-        mm(b, 0, 32, look("E1", oh, 0, key))
-        mm(b, 32, 32, look("U", oh, 0, key) + look("W", oh, 1, key))
-        mm(b, 64, 32, look("E2", oh, 1, key))
+        for c, parts in enumerate((look("E1", oh, 0, key), look("U", oh, 0, key) + look("W", oh, 1, key), look("E2", oh, 1, key))):
+            mmo(b, bank(b)[:, c:96:3], parts)
 
-    def tile(name, o1, s1, key, reads, s2=None):
-        ts(o1, T.cq[:] if name == "q" else T.cqh[:], s1, s2, A.is_equal, A.mult if s2 is not None else None, ["c" + ("q" if name == "q" else "qh")] + reads, [key])
-    for u in range(4):
-        ts(T.spp[:, 16 * u:16 * u + 16], T.m16[:], T.f8[:, 4 + u:5 + u], None, A.mult, None, ["m16", "f8"], ["spp%d" % u])
-    mm(0, 0, 64, [(T.sg[:], T.spp[:], ["sg"] + ["spp%d" % u for u in range(4)])])
-    mkcol("h24", hc, 24, 0)
-    mkcol("big", hc, -100, 100)
-    ts(T.c24[:, 32:64], T.c24[:, 32:64], col("h24"), None, A.add, None, ["c24a", "c_h24"], ["c24b"])
-    ts(T.c24[:, 64:96], T.c24[:, 64:96], 24.0, None, A.add, None, ["c24a"], ["c24c"])
-    onehot(T.oh0, 0, 64, "oh0")
-    natural(2, T.oh0, "oh0")
-    mm(3, 0, 64, [(rt(y, "E1"), T.oh0[:, y, :], ["rt%d" % y, "oh0%d" % y]) for y in range(2)])
-    mm(3, 64, 64, [(rt(y, "E2"), T.oh0[:, y, :], ["rt%d" % y, "oh0%d" % y]) for y in range(2)])
-    vcopy(T.f20[:], T.ian[:], ["ianA", "ianB"], ["f20"])
-    for u in range(4):
-        ts(T.spa[:, 16 * u:16 * u + 16], T.m16[:], T.f20[:, u:u + 1], None, A.mult, None, ["m16", "f20"], ["spa%d" % u])
-    mm(1, 0, 64, [(T.sg[:], T.spa[:], ["sg"] + ["spa%d" % u for u in range(4)])])
-    for j in range(16):
-        act(T.spn[:, 16 * j:16 * j + 16], T.m16[:], ["m16", "f20"], ["spn%d" % j], T.f20[:, 4 + j:5 + j])
-    snk = ["spn%d" % j for j in range(16)]
-    tt(T.l0f[:], bank(2)[:, 0:96], T.c24[:], A.add, ["bank2", "c24a", "c24b", "c24c"], ["l0f"])
-    for c in range(3):
-        vcopy(T.l0[:, c::3], T.l0f[:, 32 * c:32 * c + 32], ["l0f"], ["l0%d" % c])
-    l0k = ["l00", "l01", "l02", "xs"]
-    act(T.win0[:, 768:1536], T.xs[:].indirect(T.l0[:, 48:96]), l0k, ["win0b"])
-    vcopy(T.pbs[:, 0, :], bank(0)[:, 0:64], ["bank0"], ["pbs0"])
-    ts(T.pbs[:, 1, :], bank(0)[:, 0:64], col("big"), None, A.add, None, ["bank0", "c_big"], ["pbs1"])
-    vcopy(T.mbs[:, 0, :], bank(1)[:, 0:64], ["bank1"], ["mbs0"])
-    ts(T.mbs[:, 1, :], bank(1)[:, 0:64], col("big"), None, A.add, None, ["bank1", "c_big"], ["mbs1"])
+    def selected(b, c0, n, rhs, keys):
+        for m in range(8):
+            mmo(b, bank(b)[:, c0 + m:c0 + 8 * n:8], [(T.sel[:, m, :], rhs, keys + ["sel%d" % m])])
+    for x, name in enumerate(("E1", "E2")):
+        mm(2, 64 * x, 64, [(rt(y, name), T.oh0[:, y, :], ["rt%d" % y, "oh0%d" % y]) for y in range(2)])
+    natural(0, T.oh0, "oh0")
     for x in range(2):
-        tt(T.oha[:, x, :], bank(3)[:, 64 * x:64 * x + 64], T.mbs[:, x, :], A.is_equal, ["bank3", "mbs%d" % x], ["oha%d" % x])
-    for y in range(2):
-        mm(4, 64 * y, 64, [(T.bd[:, 2 * x + y, :], T.oha[:, x, :], bdk + ["oha%d" % x]) for x in range(2)])
-    tile("q", c5[:, 384:512], colP, "t5l", ["colP", "c_nh"], col("nh"))
-    tile("q", c5[:, 512:640], colP, "t5h", ["colP", "cf"], hc)
+        tt(T.oha[:, x, :], bank(2)[:, 64 * x:64 * x + 64], T.mbs[:, x, :], A.is_equal, ["bank2", "mbs%d" % x], ["oha%d" % x])
+    tt(T.l0f[:], bank(0)[:, 0:96], T.c24[:], A.add, ["bank0", "c24a", "c24b", "c24c"], ["l0f"])
+    ts(T.nb8[:], T.inbr[:], 8.0, None, A.mult, None, ["inbr"], ["nb8"])
+    vcopy(T.l0[:], T.l0f[:], ["l0f"], ["l0"])
+    l0k = ["l0", "xs"]
     for y in range(2):
         for x in range(2):
             mm(5 + y, 256 * x, 256, [(T.bd[:, 2 * x + y, :], c5[:, 384:640], bdk + ["t5l", "t5h"])])
         act(T.rm[:, y, :], bank(5 + y)[:], ["bank%d" % (5 + y)], ["rm%d" % y])
     for y in range(2):
+        mm(4, 64 * y, 64, [(T.bd[:, 2 * x + y, :], T.oha[:, x, :], bdk + ["oha%d" % x]) for x in range(2)])
+    selected(7, 0, 16, T.nb8[:], ["nb8"])
+    for k in range(3):
+        act(bank(0)[:, 128 * k:128 * k + 128], bank(7)[:, 0:128], ["bank7"], ["bank0"], 3.0)
+    act(T.win0[:, 768:1536], T.xs[:].indirect(T.l0[:, 48:96]), l0k, ["win0c"])
+    vcopy(T.win0[:, 0:384], T.xs[:].indirect(T.l0[:, 0:24]), l0k, ["win0a"])
+    for y in range(2):
         tt(T.ohd[:, y, :], bank(4)[:, 64 * y:64 * y + 64], T.pbs[:, y, :], A.is_equal, ["bank4", "pbs%d" % y], ["ohd%d" % y])
-    nev, nod = T.spn[:, 0::2], T.spn[:, 1::2]
-    mm(7, 0, 128, [(T.tgl[:], nev, ["tgl"] + snk), (T.tgh[:], nod, ["tgh"] + snk)])
-    vcopy(T.win0[:, 0:768], T.xs[:].indirect(T.l0[:, 0:48]), l0k, ["win0a"])
     tiles = [("M", 0, "R", "W"), ("M", 2, "M", 1), ("R", "U", "M", 3)]
 
     def half(y, kind, name):
@@ -305,49 +333,35 @@ def rank_program(g, core, T, topo):
             for y in range(2):
                 t, key = half(y, kind, name)
                 parts.append((t, T.ohd[:, y, par::2], [key, "ohd%d" % y]))
-        mm(2, 32 * k, 32, parts)
-    tile("h", T.sgl[:], col("g2"), "sgl", ["c_g2"])
-    tile("h", T.sgh[:], col("g21"), "sgh", ["c_g21"])
-    tile("q", T.idf[:], colP, "idf", ["colP"])
-    mm(1, 0, 24, [(T.sgl[:], ev, ["sgl"] + spk), (T.sgh[:], od, ["sgh"] + spk)])
-    mm(0, 0, 128, [(T.sgl[:], nev, ["sgl"] + snk), (T.sgh[:], nod, ["sgh"] + snk)])
-    vcopy(T.pfs[:], bank(2)[:, 0:96], ["bank2"], ["pfs"])
+        mm(3, 32 * k, 32, parts)
+    vcopy(T.win0[:, 384:768], T.xs[:].indirect(T.l0[:, 24:48]), l0k, ["win0b"])
+    for y in range(2):
+        mm(1, 128 * y, 128, [(T.bd[:, 2 * x + y, :], T.sge[:, x, :], bdk + ["sge%d" % x]) for x in range(2)])
+    act(T.rte[:], bank(1)[:, 0:256], ["bank1"], ["rte"])
+    selected(2, 128, 3, T.ns8[:, r + 1:r + 4], ["ns80", "ns81"])
+    mm(2, 0, 64, [(T.rte[:, 128 * y:128 * y + 128], T.oha[:, y, :], ["rte", "oha%d" % y]) for y in range(2)])
+    vcopy(T.pfs[:], bank(3)[:, 0:96], ["bank3"], ["pfs"])
+    ts(T.lr1[:], bank(7)[:, 0:128], k8, None, A.add, None, ["bank7", "cf"], ["lr1"])
     for k in range(3):
         for n in range(4):
             c = 128 * k + 32 * n
-            tt(T.lrf[:, c:c + 32], bank(7)[:, 32 * n:32 * n + 32], T.pfs[:, 32 * k:32 * k + 32], A.add, ["bank7", "pfs"], ["lrf%d%d" % (k, n)])
+            tt(T.lrf[:, c:c + 32], bank(0)[:, c:c + 32], T.pfs[:, 32 * k:32 * k + 32], A.add, ["bank0", "pfs"], ["lrf%d%d" % (k, n)])
+    for k in range(3):
         vcopy(T.lr0[:, 128 * k:128 * k + 128], T.lrf[:, 128 * k:128 * k + 128], ["lrf%d%d" % (k, n) for n in range(4)], ["lr0%d" % k])
-    ts(T.ls1[:], bank(1)[:, 0:24], 8.0, k8, A.mult, A.add, ["bank1", "cf"], ["ls1"])
-    ts(T.lr1[:], bank(0)[:, 0:128], 8.0, k8, A.mult, A.add, ["bank0", "cf"], ["lr1"])
+    ts(T.ls1[:], bank(2)[:, 128:152], k8, None, A.add, None, ["bank2", "cf"], ["ls1"])
+    onehot(T.ohb, 2, 64, "ohb")
+    natural(4, T.ohb, "ohb")
 
-    def last1():
-        tt(T.dg[:], T.rn4[:, 0, :], T.m16[:], A.mult, ["rn40", "m16"], ["dg"])
+    def last():
         mkcol("h8", hc, 8, 0)
-        op("V", lambda: v.tensor_reduce(T.ecol[:], T.dg[:], AxisListType.X, A.add), ["dg"], ["ecol"])
-        ts(T.c8[:, 32:64], T.c8[:, 32:64], col("h8"), None, A.add, None, ["c8a", "c_h8"], ["c8b"])
-        ts(T.c8[:, 64:96], T.c8[:, 64:96], 8.0, None, A.add, None, ["c8a"], ["c8c"])
-        ts(T.ohe[:, 0:1], pc, T.ecol[:], None, A.is_equal, None, ["cf", "ecol"], ["ohe0"])
-        ts(T.ohe[:, 1:2], col("p8"), T.ecol[:], hc, A.is_equal, A.mult, ["cf", "c_p8", "ecol"], ["ohe1"])
-        for x in range(2):
-            ts(T.sge[:, x, :], T.sg[:], T.ohe[:, x:x + 1], None, A.mult, None, ["sg", "ohe%d" % x], ["sge%d" % x])
-        for y in range(2):
-            mm(7, 128 * y, 128, [(T.bd[:, 2 * x + y, :], T.sge[:, x, :], bdk + ["sge%d" % x]) for x in range(2)])
-        vcopy(T.rte[:], bank(7)[:, 0:256], ["bank7"], ["rte"])
-        mm(0, 0, 64, [(T.rte[:, 128 * y:128 * y + 128], T.oha[:, y, :], ["rte", "oha%d" % y]) for y in range(2)])
-
-    def last2():
-        onehot(T.ohb, 0, 64, "ohb")
-        natural(3, T.ohb, "ohb")
-
-    def last3():
-        vcopy(T.lfi[:], bank(3)[:, 0:96], ["bank3"], ["lfi"])
-        op("V", lambda: v.tensor_scalar(T.lfh[:], T.lfi[:], 3, None, A.arith_shift_right), ["lfi"], ["lfh"])
-        tt(T.lfu[:], T.lfi[:], T.c8[:], A.add, ["lfi", "c8a", "c8b", "c8c"], ["lfu"])
-        ts(T.lft[:], T.lfh[:], 248.0, None, A.mult, None, ["lfh"], ["lft"])
-        tt(T.lfv[:], T.lft[:], T.lfu[:], A.add, ["lft", "lfu"], ["lfv"])
-        for c in range(3):
-            vcopy(T.lf[:, c::3], T.lfv[:, 32 * c:32 * c + 32], ["lfv"], ["lf%d" % c])
-    lfk = ["lf0", "lf1", "lf2"]
+        ts(T.lfa[:], bank(4)[:, 0:96], 8.0, 248.0, A.is_ge, A.mult, ["bank4"], ["lfa"])
+        ts(T.c8[:, 1::3], T.c8[:, 1::3], col("h8"), None, A.add, None, ["c8a", "c_h8"], ["c8b"])
+        ts(T.c8[:, 2::3], T.c8[:, 2::3], 8.0, None, A.add, None, ["c8a"], ["c8c"])
+        ts(T.lfb[:], bank(4)[:, 0:96], 16.0, 248.0, A.is_ge, A.mult, ["bank4"], ["lfb"])
+        tt(T.lfc[:], bank(4)[:, 0:96], T.c8[:], A.add, ["bank4", "c8a", "c8b", "c8c"], ["lfc"])
+        tt(T.lfd[:], T.lfa[:], T.lfb[:], A.add, ["lfa", "lfb"], ["lfd"])
+        tt(T.lfe[:], T.lfc[:], T.lfd[:], A.add, ["lfc", "lfd"], ["lfe"])
+        vcopy(T.lf[:], T.lfe[:], ["lfe"], ["lf"])
 
     hs = [slice(256 * h, 256 * h + 256) for h in range(2)]
 
@@ -356,11 +370,11 @@ def rank_program(g, core, T, topo):
             return T.win0[:] if t == 0 else T.win1[:, 1024 * k:1024 * k + 1024]
 
         def lst(k, n, a=0, b=32):
-            c = 128 * k + 32 * n
-            return T.lr0[:, c + a:c + b] if t == 0 else T.lr1[:, 32 * n + a:32 * n + b]
+            c = 128 * k + 32 * n if t == 0 else 32 * n
+            return T.lr0[:, c + a:c + b] if t == 0 else T.lr1[:, c + a:c + b]
 
         def keys(k):
-            return ["win0a", "win0b", "lr0%d" % k] if t == 0 else ["f1%d0" % k, "f1%d1" % k, "lr1"]
+            return ["win0a", "win0b", "win0c", "lr0%d" % k] if t == 0 else ["f1%d0" % k, "f1%d1" % k, "lr1"]
 
         def arrived(e, k):
             wait(e, "arr0" if t == 0 else "arr1k%d" % k, nin)
@@ -368,86 +382,81 @@ def rank_program(g, core, T, topo):
         def buf(n, k):
             return T["%s%d%d" % (n, t, k)]
 
-        def bk(n, k, h=None):
-            return "%s%d%d" % (n, t, k) + ("" if h is None else "h%d" % h)
+        def bk(n, k, h):
+            return "%s%d%dh%d" % (n, t, k, h)
 
         def target(k, h):
             if t == 0:
                 return T.win1[:, 1024 * k + 256 * h:1024 * k + 256 * h + 256], "f1%d%d" % (k, h)
             return T["n1" + "ab"[h]][:, 256 * k:256 * k + 256], "n1%d%d" % (h, k)
 
-        def scalar(k):
+        def halves(k):
             arrived("S", k)
-            if k == 0:
-                for h in range(2):
-                    act(buf("ga", k)[:, hs[h]], win(k).indirect(lst(k, 0, 16 * h, 16 * h + 16)), keys(k), [bk("ga", k, h)])
-                return
-            act(buf("ga", k)[:], win(k).indirect(lst(k, 0)), keys(k), [bk("ga", k)])
-            mm(4 + k, 0, 512, [(T.idf[:], buf("ga", k)[:], ["idf", bk("ga", k)])])
-            act(buf("gb", k)[:], win(k).indirect(lst(k, 1)), keys(k), [bk("gb", k)])
-
-        def part(k, n, h, src, skey, dst):
-            out, key = (buf(dst, k)[:, hs[h]], bk(dst, k, h)) if dst else target(k, h)
-            tt(out, win(k).indirect(lst(k, n, 16 * h, 16 * h + 16)), buf(src, k)[:, hs[h]], A.max, keys(k) + [skey], [key])
-
-        def vector(k):
-            arrived("V", k)
-            if k == 0:
-                for n, (src, dst) in enumerate((("ga", "ma"), ("ma", "mb"), ("mb", None)), 1):
-                    for h in range(2):
-                        part(k, n, h, src, bk(src, k, h), dst)
-                return
-            b = 4 + k
-            tt(buf("ma", k)[:], bank(b)[:], buf("gb", k)[:], A.max, ["bank%d" % b, bk("gb", k)], [bk("ma", k)])
-            if t == 1 and k == 2:
-                for h in range(2):
-                    part(k, 2, h, "ma", bk("ma", k), "mb")
-                    part(k, 3, h, "mb", bk("mb", k, h), None)
-                return
-            tt(buf("mb", k)[:], win(k).indirect(lst(k, 2)), buf("ma", k)[:], A.max, keys(k) + [bk("ma", k)], [bk("mb", k)])
             for h in range(2):
-                part(k, 3, h, "mb", bk("mb", k), None)
-        return scalar, vector
+                act(buf("ga", k)[:, hs[h]], win(k).indirect(lst(k, 0, 16 * h, 16 * h + 16)), keys(k), [bk("ga", k, h)])
+
+        def gathera(k):
+            arrived("S", k)
+            act(buf("ga", k)[:], win(k).indirect(lst(k, 0)), keys(k), [bk("ga", k, 0), bk("ga", k, 1)])
+            for h in range(2):
+                mm(4 + k, 256 * h, 256, [(T.idf[:], buf("ga", k)[:, hs[h]], ["idf", bk("ga", k, h)])])
+
+        def gatherb(k):
+            act(buf("gb", k)[:], win(k).indirect(lst(k, 1)), keys(k), [bk("gb", k, 0), bk("gb", k, 1)])
+
+        def part(k, n, h, src, dst):
+            out, key = (buf(dst, k)[:, hs[h]], bk(dst, k, h)) if dst else target(k, h)
+            tt(out, win(k).indirect(lst(k, n, 16 * h, 16 * h + 16)), buf(src, k)[:, hs[h]], A.max, keys(k) + [bk(src, k, h)], [key])
+
+        def vector(k, moved):
+            arrived("V", k)
+            b = 4 + k
+            for h in range(2):
+                if moved:
+                    tt(buf("ma", k)[:, hs[h]], bank(b)[:, hs[h]], buf("gb", k)[:, hs[h]], A.max, ["bank%d" % b, bk("gb", k, h)], [bk("ma", k, h)])
+                else:
+                    part(k, 1, h, "ga", "ma")
+            for h in range(2):
+                part(k, 2, h, "ma", "mb")
+            for h in range(2):
+                part(k, 3, h, "mb", None)
+        return halves, gathera, gatherb, vector
 
     def slots1(k):
         act(T.snd1[:, k, :], T.win1[:, 1024 * k:1024 * k + 512].indirect(T.ls1[:]), ["f1%d0" % k, "f1%d1" % k, "ls1"], ["snd1%d" % k])
         c0 = 1024 * k + 8 * (64 + 16 * r)
-        for j, d in enumerate(dests):
-            send(d, T.win1[:, c0:c0 + 128], T.snd1[:, k, 128 * j:128 * j + 128], "arr1k%d" % k, ["snd1%d" % k])
+        send(T.win1[:, c0:c0 + 128], [T.snd1[:, k, 128 * j:128 * j + 128] for j in range(3)], "arr1k%d" % k, [["snd1%d" % k]] * 3)
 
-    s0, v0 = rounds(0)
-    s1, v1 = rounds(1)
-    s0(0)
-    s0(1)
-    v0(0)
+    halves0, gathera0, gatherb0, vector0 = rounds(0)
+    halves1, _, _, vector1 = rounds(1)
+    halves0(0)
+    gathera0(1)
+    gatherb0(1)
+    vector0(0, False)
+    gathera0(2)
     slots1(0)
-    v0(1)
-    s0(2)
+    vector0(1, True)
+    gatherb0(2)
     slots1(1)
-    v0(2)
+    vector0(2, True)
     slots1(2)
-    last1()
-    s1(0)
-    s1(1)
-    v1(0)
-    last2()
-    s1(2)
-    v1(1)
-    last3()
-    v1(2)
+    last()
+    for k in range(3):
+        halves1(k)
+        vector1(k, False)
 
     def final(e, c, win, keys):
         out, src = T.yo[:, 384 * c:384 * c + 384], T[win][:].indirect(T.lf[:, 24 * c:24 * c + 24])
         if e == "V":
-            vcopy(out, src, lfk + keys, ["yo%d" % c])
+            vcopy(out, src, ["lf"] + keys, ["yo%d" % c])
         else:
-            act(out, src, lfk + keys, ["yo%d" % c])
+            act(out, src, ["lf"] + keys, ["yo%d" % c])
         op("Y", lambda: g.sync.dma_start(T.y[:, 384 * c:384 * c + 384], T.yo[:, 384 * c:384 * c + 384]), ["yo%d" % c], [], "st%d" % c, 16)
     ka, kb = ["n10%d" % k for k in range(3)], ["n11%d" % k for k in range(3)]
     final("S", 0, "n1a", ka)
-    final("S", 1, "n1a", ka)
     final("V", 2, "n1b", kb)
-    final("S", 3, "n1b", kb)
+    final("S", 1, "n1a", ka)
+    final("V", 3, "n1b", kb)
     for name in sorted(cnt):
         wait("Y", name, cnt[name])
-    wait("G", "sent", (1 + 3) * sum(nen.values()))
+    wait("G", "sent", (1 + 3) * nout)

@@ -11,18 +11,18 @@ def _s(cols, d):
 
 SCRATCH = {
     "xs": _s(1536, F), "ish": _s(8, I), "iact": _s(4, I), "inbr": _s(16, I), "reln": _s([2, 24], I),
-    "pi": _s(1, I), "ci": _s(4, I), "cf": _s(4, F), "cc": _s(16, F), "pcols": _s(3, F), "one": _s(128, B), "onef": _s(128, F),
-    "cq": _s(128, B), "cqg": _s(128, B), "cqh": _s(128, B), "c8": _s(96, F), "c24": _s(96, F),
+    "pi": _s(1, I), "ci": _s(4, I), "cf": _s(4, F), "cc": _s(16, F), "pcols": _s(3, F), "pm2": _s(8, F), "bcol": _s(2, F),
+    "cqz": _s(128, B),
+    "cq": _s(128, B), "cqg": _s(128, B), "cqh": _s(128, B), "c8": _s(96, B), "c24": _s(96, B), "id124": _s(128, B),
     "ct5": _s(640, B), "sg": _s(128, B), "tg": _s(128, B), "tgl": _s(128, B), "tgh": _s(128, B), "sel": _s([8, 128], B),
     "idf": _s(128, F), "m16": _s(16, B), "gm": _s(8, F),
     "rn4": _s([4, 16], F), "bd": _s([4, 128], B), "rt": _s([2, 512], B), "rm": _s([2, 512], B), "rte": _s(256, B),
-    "f8": _s(8, F), "f4": _s(4, F), "sps": _s(48, B), "spp": _s(64, B), "spa": _s(64, B), "nb8": _s(16, B), "ns8": _s(8, B),
-    "eq": _s([4, 48], B), "ohs": _s([2, 48], B), "oh0": _s([2, 64], B), "oha": _s([2, 64], B), "ohd": _s([2, 64], B),
-    "ohb": _s([2, 64], B), "pbs": _s([2, 64], F), "mbs": _s([2, 64], F),
+    "f8": _s(8, F), "f4": _s(4, F), "sps": _s(64, B), "spp": _s(64, B), "spa": _s(64, B), "nb8": _s(16, B), "ns8": _s(8, B),
+    "ohs": _s([2, 64], B), "oh0": _s([2, 64], B), "oha": _s([2, 64], B), "ohd": _s([2, 64], B),
+    "ohb": _s([2, 64], B), "a0f": _s(64, F), "a0g": _s(64, F), "pg": _s(64, F), "shu": _s(4, U), "mbs": _s([2, 64], F),
     "dg": _s(16, F), "ecol": _s(1, F), "ohe": _s(2, F), "sge": _s([2, 128], B),
-    "ls0": _s(72, U), "l0f": _s(96, F), "l0": _s(96, U), "pfs": _s(96, F), "lrf": _s(384, F),
-    "lr0": _s(384, U), "lr1": _s(128, U), "ls1": _s(24, U), "lfa": _s(96, F), "lfb": _s(96, F), "lfc": _s(96, F),
-    "lfd": _s(96, F), "lfe": _s(96, F), "lf": _s(96, U),
+    "ls0": _s(96, U), "l0": _s(96, U), "pfs": _s(96, F), "lrf": _s(384, F),
+    "lr0": _s(384, U), "lr1": _s(128, U), "ls1": _s(24, U), "kb": _s(96, B), "k1": _s(96, B), "k2": _s(96, B), "lf": _s(96, U),
     "snd0": _s(1152, F), "snd1": _s([3, 384], F), "win0": _s(3072, F), "win1": _s(3072, F),
     "n1a": _s(768, F), "n1b": _s(768, F), "yo": _s(1536, F),
 }
@@ -32,8 +32,9 @@ for _t in range(2):
             SCRATCH["%s%d%d" % (_n, _t, _k)] = _s(512, F)
 for _b in range(8):
     SCRATCH["bank%d" % _b] = ("psum", [128, 512], F)
-SEMAPHORES = ["cv", "cs", "ctn", "cg", "arr0", "arr1k0", "arr1k1", "arr1k2", "sent"] + ["ld%d" % i for i in range(8)] + ["st%d" % i for i in range(4)]
-COPY, IDENT = ActivationFunctionType.Copy, ActivationFunctionType.Identity
+SEMAPHORES = ["cv", "cs", "ctn", "cg", "arr0", "arr1k0", "arr1k1", "arr1k2", "sent"] + ["ld%d" % i for i in range(8)] + ["st%d" % i for i in range(8)]
+AF = ActivationFunctionType
+COPY, IDENT, SIGN = AF.Copy, AF.Identity, AF.Sign
 A = AluOpType
 
 
@@ -100,10 +101,10 @@ def rank_program(g, core, T, topo):
     q, op, wait, cnt = _queues(g, T)
     v, s, te = g.vector, g.scalar, g.tensor
 
-    def share(a, b, j):
+    def share(a, b, i):
         es = topo.engines(a, b)
         h = len(es) // 2
-        return (es[:h], es[h:], es)[j]
+        return (es[:h], es[h:], es)[i]
     nout = sum(len(share(core, ranks[d], j)) for j, d in enumerate(dests))
     nin = sum(len(share(ranks[(r - 1 - j) % n_ranks], core, j)) for j in range(n_ranks - 1))
 
@@ -141,9 +142,9 @@ def rank_program(g, core, T, topo):
     op("S", lambda: s.dma_start(T.ish[:, 0:4], T.shown[:]), [], ["ishA"], "ld1", 16)
     op("Y", lambda: g.sync.dma_start(T.reln[:, 1, :], T.rel[:, 192:576]), [], ["relnB"], "ld2", 16)
     op("S", lambda: s.dma_start(T.ish[:, 4:8], T.pose[:]), [], ["ishB"], "ld3", 16)
-    op("S", lambda: s.dma_start(T.iact[:], T.act[:]), [], ["iact"], "ld5", 16)
     op("Y", lambda: g.sync.dma_start(T.xs[:], T.x[:]), [], ["xs"], "ld4", 16)
-    op("Y", lambda: g.sync.dma_start(T.inbr[:], T.nbr[:]), [], ["inbr"], "ld6", 16)
+    op("S", lambda: s.dma_start(T.iact[:], T.act[:]), [], ["iact"], "ld5", 16)
+    op("S", lambda: s.dma_start(T.inbr[:], T.nbr[:]), [], ["inbr"], "ld6", 16)
 
     def iota(out, pat, base, cm, key, flag=True):
         if flag:
@@ -153,17 +154,11 @@ def rank_program(g, core, T, topo):
     iota(T.pi[:], [[1, 1]], 0, 1, "pi", False)
     iota(T.cq[:], [[1, 128]], 0, 0, "cq")
     iota(T.cqg[:], [[1, 8], [0, 16]], 0, 0, "cqg")
+    iota(T.pcols[:], [[8, 3]], -8, 1, "pcols")
     iota(T.cqh[:], [[1, 16], [0, 8]], 0, 0, "cqh")
-    iota(T.pcols[:, 1:2], [[1, 1]], 8, 1, "colPp8")
-    iota(T.pcols[:, 0:1], [[1, 1]], 0, 1, "colP")
-    iota(T.pcols[:, 2:3], [[1, 1]], -8, 1, "colPm8")
+    iota(T.cqz[:], [[16, 8], [1, 2], [0, 8]], 0, 0, "cqz")
+    iota(T.pm2[:], [[-2, 8]], 0, 1, "pm2")
     iota(T.c24[:], [[48, 32], [0, 3]], 0, 0, "c24a")
-    iota(T.c8[:], [[0, 2], [16, 16], [0, 3]], 0, 0, "c8a")
-    iota(T.one[:], [[0, 128]], 1, 0, "one")
-    for m in range(8):
-        op("G", lambda: g.affine_select(T.sel[:, m, :], T.one[:], [[16, 8], [1, 2], [0, 8]], A.is_equal, 0.0, 2 * m, -1), ["one"], ["sel%d" % m])
-    iota(T.onef[:], [[0, 128]], 1, 0, "onef")
-    op("G", lambda: g.affine_select(T.idf[:], T.onef[:], [[1, 128]], A.is_equal, 0.0, 0, -1), ["onef"], ["idf"])
     op("V", lambda: v.tensor_scalar(T.ci[:, 0:1], T.pi[:], 4, None, A.arith_shift_right), ["pi"], ["ci0"])
     op("V", lambda: v.tensor_scalar(T.ci[:, 1:2], T.pi[:], 15, None, A.bitwise_and), ["pi"], ["ci1"])
     op("V", lambda: v.tensor_scalar(T.ci[:, 2:3], T.pi[:], 3, 1, A.arith_shift_right, A.bitwise_and), ["pi"], ["ci2"])
@@ -177,38 +172,32 @@ def rank_program(g, core, T, topo):
 
     def mkcol(name, src, m, a):
         ccn[name] = len(ccn)
-        ts(col(name), src, float(m), float(a), A.mult, A.add, ["cf"], ["c_" + name])
+        op("S", lambda: s.activation(col(name), src, COPY, bias=float(a), scale=float(m)), ["cf"], ["c_" + name])
     ts(T.gm[:], T.cq[:, 0:8], gc, None, A.is_equal, None, ["cq", "cf"], ["gm"])
     ts(T.m16[:], T.cq[:, 0:16], pc, None, A.is_equal, None, ["cq", "cf"], ["m16"])
     mkcol("nh", hc, -1, 1)
+    mkcol("p8", pc, 1, 8)
     mkcol("g2", gc, 2, 0)
     mkcol("g21", gc, 2, 1)
+    mkcol("h24", hc, 24, 0)
+    mkcol("big", hc, -100, 100)
+    mkcol("h8", hc, 8, -4)
+    mkcol("p24", hc, 0, 24)
     ts(T.sg[:], T.cqg[:], gc, None, A.is_equal, None, ["cqg", "cf"], ["sg"])
-    mkcol("p8", pc, 1, 8)
-    for u in range(1, 4):
-        mkcol("v%d" % u, pc, 1, 16 * u)
-    colP, colPp8, colPm8 = (T.pcols[:, j:j + 1] for j in range(3))
+    colPm8, colP, colPp8 = (T.pcols[:, j:j + 1] for j in range(3))
     c5 = T.ct5
 
     def tile(o1, src, s1, key, reads, s2=None):
         ts(o1, T[src][:], s1, s2, A.is_equal, A.mult if s2 is not None else None, [src] + reads, [key])
     tile(T.tg[:], "cqg", gc, "tg", ["cf"], 24.0)
-    tile(T.tgl[:], "cqh", col("g2"), "tgl", ["c_g2"], 24.0)
-    tile(T.tgh[:], "cqh", col("g21"), "tgh", ["c_g21"], 24.0)
-    tile(c5[:, 0:128], "cq", colPp8, "t5b", ["colPp8", "c_nh"], col("nh"))
-    tile(c5[:, 128:256], "cq", colP, "t5i", ["colP"])
-    tile(c5[:, 256:384], "cq", colPm8, "t5a", ["colPm8", "cf"], hc)
-    mkcol("h24", hc, 24, 0)
-    mkcol("big", hc, -100, 100)
-    tile(c5[:, 384:512], "cq", colP, "t5l", ["colP", "c_nh"], col("nh"))
-    tile(c5[:, 512:640], "cq", colP, "t5h", ["colP", "cf"], hc)
+    tile(c5[:, 0:128], "cq", colPp8, "t5b", ["pcols", "c_nh"], col("nh"))
+    tile(c5[:, 128:256], "cq", colP, "t5i", ["pcols"])
+    tile(c5[:, 256:384], "cq", colPm8, "t5a", ["pcols", "cf"], hc)
+    idb = c5[:, 128:256]
 
     vcopy(T.f8[:], T.ish[:], ["ishA", "ishB"], ["f8"])
     for y in range(2):
         vcopy(T.rn4[:, y::2, :], T.reln[:, :, 8 * y:8 * y + 16], ["relnA", "relnB"], ["rn4%d" % y])
-    for j, d in enumerate(dests):
-        ts(T.sps[:, 16 * j:16 * j + 16], T.m16[:], T.f8[:, d:d + 1], None, A.mult, None, ["m16", "f8"], ["sps%d" % j])
-    spk = ["sps0", "sps1", "sps2"]
     for j in range(8):
         out, sc = T.bd[:, :, 16 * j:16 * j + 16], T.gm[:, j:j + 1]
         if j % 2:
@@ -216,117 +205,152 @@ def rank_program(g, core, T, topo):
         else:
             ts(out, T.rn4[:], sc, None, A.mult, None, ["rn40", "rn41", "gm"], ["bd%d" % j])
     bdk = ["bd%d" % j for j in range(8)]
-    vcopy(T.f4[:], T.iact[:], ["iact"], ["f4"])
     for u in range(4):
         act(T.spp[:, 16 * u:16 * u + 16], T.m16[:], ["m16", "f8"], ["spp%d" % u], T.f8[:, 4 + u:5 + u])
-    for u in range(4):
-        act(T.spa[:, 16 * u:16 * u + 16], T.m16[:], ["m16", "f4"], ["spa%d" % u], T.f4[:, u:u + 1])
+    tb = [5, 6, 7, 4]
+
+    def tables(y, x):
+        l, c = T.bd[:, 2 * x + y, :], (c5[:, 0:256], c5[:, 128:384])[x]
+        mm(tb[2 * y + x], 0, 256, [(l, c, bdk + ["t5b", "t5i", "t5a"])])
+
+    def table_copy(y, x):
+        out, b, key = T.rt[:, y, 256 * x:256 * x + 256], tb[2 * y + x], ["rt%d%d" % (y, x)]
+        (act, vcopy)[y](out, bank(b)[:, 0:256], ["bank%d" % b], key)
+    tables(0, 0)
+    tables(1, 0)
+    mm(1, 0, 64, [(T.sg[:], T.spp[:], ["sg"] + ["spp%d" % u for u in range(4)])])
+    tables(0, 1)
+    tables(1, 1)
+    for p in range(n_ranks):
+        ts(T.sps[:, 16 * p:16 * p + 16], T.m16[:], T.f8[:, p:p + 1], None, A.mult, None, ["m16", "f8"], ["sps%d" % p])
+    spk = ["sps%d" % p for p in range(n_ranks)]
+    vcopy(T.shu[:], T.ish[:, 0:4], ["ishA"], ["shu"])
     ev, od = T.sps[:, 0::2], T.sps[:, 1::2]
-    mm(0, 0, 48, [(T.sg[:], T.sps[:], ["sg"] + spk)])
-    mm(2, 0, 24, [(T.tg[:], ev, ["tg"] + spk)], last=False)
-    mm(3, 0, 24, [(T.tgl[:], ev, ["tgl"] + spk), (T.tgh[:], od, ["tgh"] + spk)], last=False)
-    mm(4, 0, 24, [(T.tg[:], od, ["tg"] + spk)], last=False)
-    for y in range(2):
-        mm(5 + y, 0, 256, [(T.bd[:, y, :], c5[:, 0:256], bdk + ["t5b", "t5i"])])
-        mm(5 + y, 256, 256, [(T.bd[:, 2 + y, :], c5[:, 128:384], bdk + ["t5i", "t5a"])])
-        act(T.rt[:, y, :], bank(5 + y)[:], ["bank%d" % (5 + y)], ["rt%d" % y])
+    table_copy(0, 0)
+    act(T.a0f[:], bank(1)[:, 0:64], ["bank1"], ["a0f"])
+    table_copy(1, 0)
+    table_copy(0, 1)
 
     def rt(y, name):
         j = {"W": 0, "E1": 1, "E2": 2, "U": 3}[name]
         return T.rt[:, y, 128 * j:128 * j + 128]
 
+    def rk(y, name):
+        return "rt%d%d" % (y, {"W": 0, "E1": 0, "E2": 1, "U": 1}[name])
+
     def rm(y, j):
         return T.rm[:, y, 128 * j:128 * j + 128]
 
     def look(name, oh, par, key):
-        return [(rt(y, name), oh[:, y, par::2], ["rt%d" % y, key + str(y)]) for y in range(2)]
+        return [(rt(y, name), oh[:, y, par::2], [rk(y, name), key + str(y)]) for y in range(2)]
 
-    vc = [pc] + [col("v%d" % u) for u in range(1, 4)]
-    vk = ["cf", "c_v1", "c_v2", "c_v3"]
+    def onehot(dst, src, keys, key):
+        ts(dst[:, 0, :], src, pc, None, A.is_equal, None, keys + ["cf"], [key + "0"])
+        ts(dst[:, 1, :], src, col("p8"), hc, A.is_equal, A.mult, keys + ["cf", "c_p8"], [key + "1"])
+    vcopy(T.pg[:], T.a0f[:].indirect(T.shu[:]), ["a0f", "shu"], ["pg"])
+    tile(T.tgl[:], "cqh", col("g2"), "tgl", ["c_g2"], 24.0)
+    tile(T.tgh[:], "cqh", col("g21"), "tgh", ["c_g21"], 24.0)
+    onehot(T.ohs, T.pg[:], ["pg"], "ohs")
+    table_copy(1, 1)
+    onehot(T.oh0, T.a0f[:], ["a0f"], "oh0")
+    vcopy(T.f4[:], T.iact[:], ["iact"], ["f4"])
+    mm(2, 0, 32, [(T.tg[:], ev, ["tg"] + spk)], last=False)
+    mm(3, 0, 32, [(T.tgl[:], ev, ["tgl"] + spk), (T.tgh[:], od, ["tgh"] + spk)], last=False)
+    mm(2, 0, 32, look("E1", T.ohs, 0, "ohs"), first=False)
+    mm(4, 0, 32, [(T.tg[:], od, ["tg"] + spk)], last=False)
+    mm(3, 0, 32, look("W", T.ohs, 1, "ohs"), first=False, last=False)
+    mm(4, 0, 32, look("E2", T.ohs, 1, "ohs"), first=False)
+    mm(3, 0, 32, look("U", T.ohs, 0, "ohs"), first=False)
+    act(T.c24[:, 1::3], T.c24[:, 1::3], ["c24a", "c_h24"], ["c24b"], bias=col("h24"))
+    act(T.c24[:, 2::3], T.c24[:, 2::3], ["c24a", "c_p24"], ["c24c"], bias=col("p24"))
     for u in range(4):
-        ts(T.eq[:, u, :], bank(0)[:, 0:48], vc[u], T.f8[:, 4 + u:5 + u], A.is_equal, A.mult, ["bank0", vk[u], "f8"], ["eq%d" % u])
-    mm(1, 0, 48, [(T.sg[:], T.eq[:, u, :], ["sg", "eq%d" % u]) for u in range(4)])
-    mm(7, 0, 64, [(T.sg[:], T.spp[:], ["sg"] + ["spp%d" % u for u in range(4)])])
-    mm(0, 0, 64, [(T.sg[:], T.spa[:], ["sg"] + ["spa%d" % u for u in range(4)])])
-    for t, b in (("pbs", 7), ("mbs", 0)):
-        act(T[t][:, 0, :], bank(b)[:, 0:64], ["bank%d" % b], [t + "0"])
-        act(T[t][:, 1, :], bank(b)[:, 0:64], ["bank%d" % b, "c_big"], [t + "1"], bias=col("big"))
-    tt(T.dg[:], T.rn4[:, 0, :], T.m16[:], A.mult, ["rn40", "m16"], ["dg"])
-    ts(T.c24[:, 1::3], T.c24[:, 1::3], col("h24"), None, A.add, None, ["c24a", "c_h24"], ["c24b"])
-    ts(T.c24[:, 2::3], T.c24[:, 2::3], 24.0, None, A.add, None, ["c24a"], ["c24c"])
-    op("V", lambda: v.tensor_reduce(T.ecol[:], T.dg[:], AxisListType.X, A.add), ["dg"], ["ecol"])
-    for j in range(2):
-        ts(T.ns8[:, 4 * j:4 * j + 4], T.f8[:, 0:4], 8.0, None, A.mult, None, ["f8"], ["ns8%d" % j])
-    ts(T.ohe[:, 0:1], pc, T.ecol[:], None, A.is_equal, None, ["cf", "ecol"], ["ohe0"])
-    ts(T.ohe[:, 1:2], col("p8"), T.ecol[:], hc, A.is_equal, A.mult, ["cf", "c_p8", "ecol"], ["ohe1"])
-
-    def onehot(dst, b, n, key):
-        ts(dst[:, 0, :], bank(b)[:, 0:n], pc, None, A.is_equal, None, ["bank%d" % b, "cf"], [key + "0"])
-        ts(dst[:, 1, :], bank(b)[:, 0:n], col("p8"), hc, A.is_equal, A.mult, ["bank%d" % b, "cf", "c_p8"], [key + "1"])
-    onehot(T.ohs, 1, 48, "ohs")
-    mm(2, 0, 24, look("E1", T.ohs, 0, "ohs"), first=False)
-    mm(3, 0, 24, look("U", T.ohs, 0, "ohs") + look("W", T.ohs, 1, "ohs"), first=False)
-    mm(4, 0, 24, look("E2", T.ohs, 1, "ohs"), first=False)
-    onehot(T.oh0, 7, 64, "oh0")
-    for x in range(2):
-        ts(T.sge[:, x, :], T.sg[:], T.ohe[:, x:x + 1], None, A.mult, None, ["sg", "ohe%d" % x], ["sge%d" % x])
-    for c in range(3):
-        vcopy(T.ls0[:, c::3], bank(2 + c)[:, 0:24], ["bank%d" % (2 + c)], ["ls0%d" % c])
+        act(T.spa[:, 16 * u:16 * u + 16], T.m16[:], ["m16", "f4"], ["spa%d" % u], T.f4[:, u:u + 1])
+    for c in (0, 2, 1):
+        vcopy(T.ls0[:, c::3], bank(2 + c)[:, 0:32], ["bank%d" % (2 + c)], ["ls0%d" % c])
     lsk = ["ls00", "ls01", "ls02", "xs"]
 
-    def slot0(e, a, b, key):
-        src, out = T.xs[:].indirect(T.ls0[:, a:b]), T.snd0[:, 16 * a:16 * b]
+    def slot0(e, j, a, b, key):
+        c = 24 * dests[j]
+        src, out = T.xs[:].indirect(T.ls0[:, c + a:c + b]), T.snd0[:, 384 * j + 16 * a:384 * j + 16 * b]
         if e == "V":
             vcopy(out, src, lsk, [key])
         else:
             act(out, src, lsk, [key])
-    slot0("V", 0, 24, "snd0a")
-    slot0("S", 24, 48, "snd0b")
-    slot0("V", 48, 60, "snd0c")
-    slot0("S", 60, 72, "snd0d")
+    slot0("V", 0, 0, 12, "snd0a")
+    slot0("S", 0, 12, 24, "snd0b")
+    slot0("V", 1, 0, 24, "snd0c")
+    slot0("S", 2, 0, 24, "snd0d")
 
-    def send(out, srcs, sem, keys):
-        mask = [sum(1 << e for e in share(core, ranks[d], j)) for j, d in enumerate(dests)]
+    def send(out, srcs, sem, keys, pair):
         at = [topo.addr(ranks[d])[:2] for d in dests]
-        two = [RemoteDMATransfer(dst_ids=[DstId(rid=at[j][0], pnc=at[j][1])], dma_engine_mask=mask[j], remote_sem=T.sem[sem], srcs=[srcs[j]], dsts=[out], alu_op=0) for j in range(2)]
-        op("G", lambda: g.remote_dma_fused(two, local_sem=T.sem.sent), keys[0] + keys[1], [], signal=False)
-        op("G", lambda: g.remote_dma(out, srcs[2], T.sem[sem], T.sem.sent, at[2][1], at[2][0], mask[2]), keys[2], [], signal=False)
-    c0 = 24 * (64 + 16 * r)
-    send(T.win0[:, c0:c0 + 384], [T.snd0[:, 384 * j:384 * j + 384] for j in range(3)], "arr0", [["snd0a"], ["snd0b"], ["snd0c", "snd0d"]])
 
-    def natural(b, oh, key):
+        def mask(j, i):
+            return sum(1 << e for e in share(core, ranks[dests[j]], i))
+        alone = 3 - sum(pair)
+        two = [RemoteDMATransfer(dst_ids=[DstId(rid=at[j][0], pnc=at[j][1])], dma_engine_mask=mask(j, i), remote_sem=T.sem[sem], srcs=[srcs[j]], dsts=[out], alu_op=0) for i, j in enumerate(pair)]
+
+        def fused():
+            op("G", lambda: g.remote_dma_fused(two, local_sem=T.sem.sent), keys[pair[0]] + keys[pair[1]], [], signal=False)
+
+        def single():
+            op("G", lambda: g.remote_dma(out, srcs[alone], T.sem[sem], T.sem.sent, at[alone][1], at[alone][0], mask(alone, 2)), keys[alone], [], signal=False)
+        for f in ((single, fused) if alone == 0 else (fused, single)):
+            f()
+    c0 = 24 * (64 + 16 * r)
+    send(T.win0[:, c0:c0 + 384], [T.snd0[:, 384 * j:384 * j + 384] for j in range(3)], "arr0", [["snd0a", "snd0b"], ["snd0c"], ["snd0d"]], (1, 2))
+    iota(T.bcol[:], [[-16, 2]], -15, 0, "bcol")
+    iota(T.c8[:], [[0, 2], [16, 16], [4, 3]], 248, 0, "c8a")
+
+    def natural(b, oh, key, add=None):
         for c, parts in enumerate((look("E1", oh, 0, key), look("U", oh, 0, key) + look("W", oh, 1, key), look("E2", oh, 1, key))):
-            mmo(b, bank(b)[:, c:96:3], parts)
+            more = [(idb, T.c24[:, c::3], ["t5i", "c24a", "c24b", "c24c"])] if add else []
+            mmo(b, bank(b)[:, c:96:3], parts + more)
 
     def selected(b, c0, n, rhs, keys):
         for m in range(8):
             mmo(b, bank(b)[:, c0 + m:c0 + 8 * n:8], [(T.sel[:, m, :], rhs, keys + ["sel%d" % m])])
+    mm(0, 0, 64, [(T.sg[:], T.spa[:], ["sg"] + ["spa%d" % u for u in range(4)])])
+    act(T.mbs[:, 0, :], bank(0)[:, 0:64], ["bank0"], ["mbs0"])
+    act(T.mbs[:, 1, :], bank(0)[:, 0:64], ["bank0", "c_big"], ["mbs1"], bias=col("big"))
+    act(T.a0g[:], T.a0f[:], ["a0f", "c_big"], ["a0g"], bias=col("big"))
     for x, name in enumerate(("E1", "E2")):
-        mm(2, 64 * x, 64, [(rt(y, name), T.oh0[:, y, :], ["rt%d" % y, "oh0%d" % y]) for y in range(2)])
-    natural(0, T.oh0, "oh0")
+        mm(2, 64 * x, 64, [(rt(y, name), T.oh0[:, y, :], [rk(y, name), "oh0%d" % y]) for y in range(2)])
+    natural(0, T.oh0, "oh0", True)
+    tile(c5[:, 384:512], "cq", colP, "t5l", ["pcols", "c_nh"], col("nh"))
+    tile(c5[:, 512:640], "cq", colP, "t5h", ["pcols", "cf"], hc)
+    tt(T.dg[:], T.rn4[:, 0, :], T.m16[:], A.mult, ["rn40", "m16"], ["dg"])
     for x in range(2):
         tt(T.oha[:, x, :], bank(2)[:, 64 * x:64 * x + 64], T.mbs[:, x, :], A.is_equal, ["bank2", "mbs%d" % x], ["oha%d" % x])
-    tt(T.l0f[:], bank(0)[:, 0:96], T.c24[:], A.add, ["bank0", "c24a", "c24b", "c24c"], ["l0f"])
     ts(T.nb8[:], T.inbr[:], 8.0, None, A.mult, None, ["inbr"], ["nb8"])
-    vcopy(T.l0[:], T.l0f[:], ["l0f"], ["l0"])
+    vcopy(T.l0[:], bank(0)[:, 0:96], ["bank0"], ["l0"])
+    for m in range(8):
+        tile(T.sel[:, m, :], "cqz", T.pm2[:, m:m + 1], "sel%d" % m, ["pm2"])
     l0k = ["l0", "xs"]
+    for y in range(2):
+        mm(4, 64 * y, 64, [(T.bd[:, 2 * x + y, :], T.oha[:, x, :], bdk + ["oha%d" % x]) for x in range(2)])
     for y in range(2):
         for x in range(2):
             mm(5 + y, 256 * x, 256, [(T.bd[:, 2 * x + y, :], c5[:, 384:640], bdk + ["t5l", "t5h"])])
-        act(T.rm[:, y, :], bank(5 + y)[:], ["bank%d" % (5 + y)], ["rm%d" % y])
-    for y in range(2):
-        mm(4, 64 * y, 64, [(T.bd[:, 2 * x + y, :], T.oha[:, x, :], bdk + ["oha%d" % x]) for x in range(2)])
+    act(T.win0[:, 1152:1536], T.xs[:].indirect(T.l0[:, 72:96]), l0k, ["win0c"])
+    act(T.rm[:, 0, :], bank(5)[:], ["bank5"], ["rm0"])
     selected(7, 0, 16, T.nb8[:], ["nb8"])
+    op("V", lambda: v.tensor_reduce(T.ecol[:], T.dg[:], AxisListType.X, A.add), ["dg"], ["ecol"])
     for k in range(3):
         act(bank(0)[:, 128 * k:128 * k + 128], bank(7)[:, 0:128], ["bank7"], ["bank0"], 3.0)
-    act(T.win0[:, 768:1536], T.xs[:].indirect(T.l0[:, 48:96]), l0k, ["win0c"])
-    vcopy(T.win0[:, 0:384], T.xs[:].indirect(T.l0[:, 0:24]), l0k, ["win0a"])
+    for j in range(2):
+        act(T.ns8[:, 4 * j:4 * j + 4], T.f8[:, 0:4], ["f8"], ["ns8%d" % j], 8.0)
+    act(T.idf[:], idb, ["t5i"], ["idf"])
+    act(T.id124[:], idb, ["t5i"], ["id124"], 124.0)
+    act(T.c8[:, 1::3], T.c8[:, 1::3], ["c8a", "c_h8"], ["c8b"], bias=col("h8"))
+    vcopy(T.win0[:, 0:288], T.xs[:].indirect(T.l0[:, 0:18]), l0k, ["win0a"])
     for y in range(2):
-        tt(T.ohd[:, y, :], bank(4)[:, 64 * y:64 * y + 64], T.pbs[:, y, :], A.is_equal, ["bank4", "pbs%d" % y], ["ohd%d" % y])
+        tt(T.ohd[:, y, :], bank(4)[:, 64 * y:64 * y + 64], (T.a0f, T.a0g)[y][:], A.is_equal, ["bank4", ("a0f", "a0g")[y]], ["ohd%d" % y])
+    vcopy(T.rm[:, 1, :], bank(6)[:], ["bank6"], ["rm1"])
+    vcopy(T.win0[:, 288:672], T.xs[:].indirect(T.l0[:, 18:42]), l0k, ["win0d"])
     tiles = [("M", 0, "R", "W"), ("M", 2, "M", 1), ("R", "U", "M", 3)]
 
     def half(y, kind, name):
-        return (rt(y, name), "rt%d" % y) if kind == "R" else (rm(y, name), "rm%d" % y)
+        return (rt(y, name), rk(y, name)) if kind == "R" else (rm(y, name), "rm%d" % y)
     for k, (ka, na, kb, nb) in enumerate(tiles):
         parts = []
         for par, kind, name in ((0, ka, na), (1, kb, nb)):
@@ -334,129 +358,157 @@ def rank_program(g, core, T, topo):
                 t, key = half(y, kind, name)
                 parts.append((t, T.ohd[:, y, par::2], [key, "ohd%d" % y]))
         mm(3, 32 * k, 32, parts)
-    vcopy(T.win0[:, 384:768], T.xs[:].indirect(T.l0[:, 24:48]), l0k, ["win0b"])
+    ts(T.ohe[:, 0:1], pc, T.ecol[:], None, A.is_equal, None, ["cf", "ecol"], ["ohe0"])
+    ts(T.ohe[:, 1:2], col("p8"), T.ecol[:], hc, A.is_equal, A.mult, ["cf", "c_p8", "ecol"], ["ohe1"])
+    for x in range(2):
+        act(T.sge[:, x, :], T.sg[:], ["sg", "ohe%d" % x], ["sge%d" % x], T.ohe[:, x:x + 1])
     for y in range(2):
         mm(1, 128 * y, 128, [(T.bd[:, 2 * x + y, :], T.sge[:, x, :], bdk + ["sge%d" % x]) for x in range(2)])
     act(T.rte[:], bank(1)[:, 0:256], ["bank1"], ["rte"])
+    act(T.win0[:, 672:1152], T.xs[:].indirect(T.l0[:, 42:72]), l0k, ["win0b"])
     selected(2, 128, 3, T.ns8[:, r + 1:r + 4], ["ns80", "ns81"])
     mm(2, 0, 64, [(T.rte[:, 128 * y:128 * y + 128], T.oha[:, y, :], ["rte", "oha%d" % y]) for y in range(2)])
     vcopy(T.pfs[:], bank(3)[:, 0:96], ["bank3"], ["pfs"])
-    ts(T.lr1[:], bank(7)[:, 0:128], k8, None, A.add, None, ["bank7", "cf"], ["lr1"])
     for k in range(3):
         for n in range(4):
             c = 128 * k + 32 * n
             tt(T.lrf[:, c:c + 32], bank(0)[:, c:c + 32], T.pfs[:, 32 * k:32 * k + 32], A.add, ["bank0", "pfs"], ["lrf%d%d" % (k, n)])
+    ts(T.lr1[:], bank(7)[:, 0:128], k8, None, A.add, None, ["bank7", "cf"], ["lr1"])
     for k in range(3):
         vcopy(T.lr0[:, 128 * k:128 * k + 128], T.lrf[:, 128 * k:128 * k + 128], ["lrf%d%d" % (k, n) for n in range(4)], ["lr0%d" % k])
     ts(T.ls1[:], bank(2)[:, 128:152], k8, None, A.add, None, ["bank2", "cf"], ["ls1"])
-    onehot(T.ohb, 2, 64, "ohb")
+    onehot(T.ohb, bank(2)[:, 0:64], ["bank2"], "ohb")
     natural(4, T.ohb, "ohb")
 
     def last():
-        mkcol("h8", hc, 8, 0)
-        ts(T.lfa[:], bank(4)[:, 0:96], 8.0, 248.0, A.is_ge, A.mult, ["bank4"], ["lfa"])
-        ts(T.c8[:, 1::3], T.c8[:, 1::3], col("h8"), None, A.add, None, ["c8a", "c_h8"], ["c8b"])
-        ts(T.c8[:, 2::3], T.c8[:, 2::3], 8.0, None, A.add, None, ["c8a"], ["c8c"])
-        ts(T.lfb[:], bank(4)[:, 0:96], 16.0, 248.0, A.is_ge, A.mult, ["bank4"], ["lfb"])
-        tt(T.lfc[:], bank(4)[:, 0:96], T.c8[:], A.add, ["bank4", "c8a", "c8b", "c8c"], ["lfc"])
-        tt(T.lfd[:], T.lfa[:], T.lfb[:], A.add, ["lfa", "lfb"], ["lfd"])
-        tt(T.lfe[:], T.lfc[:], T.lfd[:], A.add, ["lfc", "lfd"], ["lfe"])
-        vcopy(T.lf[:], T.lfe[:], ["lfe"], ["lf"])
+        act(T.kb[:], bank(4)[:, 0:96], ["bank4"], ["kb"])
+        for j in range(2):
+            out, b, key = T["k%d" % (j + 1)], T.bcol[:, j:j + 1], "k%d" % (j + 1)
+            op("S", lambda: s.activation(out[:], bank(4)[:, 0:96], SIGN, bias=b, scale=2.0), ["bank4", "bcol"], [key])
+        mm(2, 0, 96, [(idb, T.c8[:], ["t5i", "c8a", "c8b"]), (idb, T.kb[:], ["kb"])] + [(T.id124[:], T[k][:], ["id124", k]) for k in ("k1", "k2")])
 
     hs = [slice(256 * h, 256 * h + 256) for h in range(2)]
+    pb = {(0, 0): 5, (0, 1): 6, (0, 2): 7, (1, 0): 0, (1, 1): 1, (1, 2): 3}
 
-    def rounds(t):
-        def win(k):
-            return T.win0[:] if t == 0 else T.win1[:, 1024 * k:1024 * k + 1024]
+    def win(t, k):
+        return T.win0[:] if t == 0 else T.win1[:, 1024 * k:1024 * k + 1024]
 
-        def lst(k, n, a=0, b=32):
-            c = 128 * k + 32 * n if t == 0 else 32 * n
-            return T.lr0[:, c + a:c + b] if t == 0 else T.lr1[:, c + a:c + b]
+    def lst(t, k, n, a=0, b=32):
+        c = 128 * k + 32 * n if t == 0 else 32 * n
+        return T.lr0[:, c + a:c + b] if t == 0 else T.lr1[:, c + a:c + b]
 
-        def keys(k):
-            return ["win0a", "win0b", "win0c", "lr0%d" % k] if t == 0 else ["f1%d0" % k, "f1%d1" % k, "lr1"]
+    def keys(t, k):
+        return ["win0a", "win0b", "win0c", "win0d", "lr0%d" % k] if t == 0 else ["f1%d0" % k, "f1%d1" % k, "lr1"]
 
-        def arrived(e, k):
-            wait(e, "arr0" if t == 0 else "arr1k%d" % k, nin)
+    def arrived(e, t, k):
+        wait(e, "arr0" if t == 0 else "arr1k%d" % k, nin)
 
-        def buf(n, k):
-            return T["%s%d%d" % (n, t, k)]
+    def buf(n, t, k):
+        return T["%s%d%d" % (n, t, k)]
 
-        def bk(n, k, h):
-            return "%s%d%dh%d" % (n, t, k, h)
+    def bk(n, t, k, h):
+        return "%s%d%dh%d" % (n, t, k, h)
 
-        def target(k, h):
-            if t == 0:
-                return T.win1[:, 1024 * k + 256 * h:1024 * k + 256 * h + 256], "f1%d%d" % (k, h)
-            return T["n1" + "ab"[h]][:, 256 * k:256 * k + 256], "n1%d%d" % (h, k)
+    def first(e, t, k, h):
+        arrived(e, t, k)
+        out, src, ky = buf("ga", t, k)[:, hs[h]], win(t, k).indirect(lst(t, k, 0, 16 * h, 16 * h + 16)), keys(t, k)
+        if e == "V":
+            vcopy(out, src, ky, [bk("ga", t, k, h)])
+        else:
+            act(out, src, ky, [bk("ga", t, k, h)])
 
-        def halves(k):
-            arrived("S", k)
+    def gather(t, k, n, halves=(0, 1)):
+        arrived("S", t, k)
+        nm = "g" + "ab"[n]
+        whole = t == 0 and k > 0
+        if whole:
+            act(buf(nm, t, k)[:], win(t, k).indirect(lst(t, k, n)), keys(t, k), [bk(nm, t, k, 0), bk(nm, t, k, 1)])
+        for h in halves:
+            if not whole:
+                act(buf(nm, t, k)[:, hs[h]], win(t, k).indirect(lst(t, k, n, 16 * h, 16 * h + 16)), keys(t, k), [bk(nm, t, k, h)])
+            if n == 1:
+                mm(pb[t, k], 256 * h, 256, [(T.idf[:], buf(nm, t, k)[:, hs[h]], ["idf", bk(nm, t, k, h)])])
+
+    def result(t, k, h):
+        if t == 0:
+            return T.win1[:, 1024 * k + 256 * h:1024 * k + 256 * h + 256], "f1%d%d" % (k, h)
+        return T["n1" + "ab"[h]][:, 256 * k:256 * k + 256], "n1%d%d" % (h, k)
+
+    def part(t, k, n, h):
+        arrived("V", t, k)
+        src, dst = {2: ("ga", "ma"), 3: ("ma", "mb"), 1: ("mb", "")}[n]
+        out, key = result(t, k, h) if n == 1 else (buf(dst, t, k)[:, hs[h]], bk(dst, t, k, h))
+        tt(out, win(t, k).indirect(lst(t, k, n, 16 * h, 16 * h + 16)), buf(src, t, k)[:, hs[h]], A.max, keys(t, k) + [bk(src, t, k, h)], [key])
+
+    def join(t, k, h):
+        out, key = result(t, k, h)
+        tt(out, bank(pb[t, k])[:, hs[h]], buf("mb", t, k)[:, hs[h]], A.max, ["bank%d" % pb[t, k], bk("mb", t, k, h)], [key])
+
+    def vector(t, k, moved):
+        for n in (2, 3):
             for h in range(2):
-                act(buf("ga", k)[:, hs[h]], win(k).indirect(lst(k, 0, 16 * h, 16 * h + 16)), keys(k), [bk("ga", k, h)])
-
-        def gathera(k):
-            arrived("S", k)
-            act(buf("ga", k)[:], win(k).indirect(lst(k, 0)), keys(k), [bk("ga", k, 0), bk("ga", k, 1)])
-            for h in range(2):
-                mm(4 + k, 256 * h, 256, [(T.idf[:], buf("ga", k)[:, hs[h]], ["idf", bk("ga", k, h)])])
-
-        def gatherb(k):
-            act(buf("gb", k)[:], win(k).indirect(lst(k, 1)), keys(k), [bk("gb", k, 0), bk("gb", k, 1)])
-
-        def part(k, n, h, src, dst):
-            out, key = (buf(dst, k)[:, hs[h]], bk(dst, k, h)) if dst else target(k, h)
-            tt(out, win(k).indirect(lst(k, n, 16 * h, 16 * h + 16)), buf(src, k)[:, hs[h]], A.max, keys(k) + [bk(src, k, h)], [key])
-
-        def vector(k, moved):
-            arrived("V", k)
-            b = 4 + k
-            for h in range(2):
-                if moved:
-                    tt(buf("ma", k)[:, hs[h]], bank(b)[:, hs[h]], buf("gb", k)[:, hs[h]], A.max, ["bank%d" % b, bk("gb", k, h)], [bk("ma", k, h)])
-                else:
-                    part(k, 1, h, "ga", "ma")
-            for h in range(2):
-                part(k, 2, h, "ma", "mb")
-            for h in range(2):
-                part(k, 3, h, "mb", None)
-        return halves, gathera, gatherb, vector
+                part(t, k, n, h)
+        for h in range(2):
+            if h in moved:
+                join(t, k, h)
+            else:
+                part(t, k, 1, h)
 
     def slots1(k):
-        act(T.snd1[:, k, :], T.win1[:, 1024 * k:1024 * k + 512].indirect(T.ls1[:]), ["f1%d0" % k, "f1%d1" % k, "ls1"], ["snd1%d" % k])
-        c0 = 1024 * k + 8 * (64 + 16 * r)
-        send(T.win1[:, c0:c0 + 128], [T.snd1[:, k, 128 * j:128 * j + 128] for j in range(3)], "arr1k%d" % k, [["snd1%d" % k]] * 3)
-
-    halves0, gathera0, gatherb0, vector0 = rounds(0)
-    halves1, _, _, vector1 = rounds(1)
-    halves0(0)
-    gathera0(1)
-    gatherb0(1)
-    vector0(0, False)
-    gathera0(2)
-    slots1(0)
-    vector0(1, True)
-    gatherb0(2)
-    slots1(1)
-    vector0(2, True)
-    slots1(2)
-    last()
-    for k in range(3):
-        halves1(k)
-        vector1(k, False)
-
-    def final(e, c, win, keys):
-        out, src = T.yo[:, 384 * c:384 * c + 384], T[win][:].indirect(T.lf[:, 24 * c:24 * c + 24])
-        if e == "V":
-            vcopy(out, src, ["lf"] + keys, ["yo%d" % c])
+        w, ky = T.win1[:, 1024 * k:1024 * k + 512], ["f1%d0" % k, "f1%d1" % k, "ls1"]
+        if k < 2:
+            act(T.snd1[:, k, :], w.indirect(T.ls1[:]), ky, ["snd1%d" % k])
+            kk = [["snd1%d" % k]] * 3
         else:
-            act(out, src, ["lf"] + keys, ["yo%d" % c])
-        op("Y", lambda: g.sync.dma_start(T.y[:, 384 * c:384 * c + 384], T.yo[:, 384 * c:384 * c + 384]), ["yo%d" % c], [], "st%d" % c, 16)
-    ka, kb = ["n10%d" % k for k in range(3)], ["n11%d" % k for k in range(3)]
-    final("S", 0, "n1a", ka)
-    final("V", 2, "n1b", kb)
-    final("S", 1, "n1a", ka)
-    final("V", 3, "n1b", kb)
+            act(T.snd1[:, k, 0:128], w.indirect(T.ls1[:, 0:8]), ky, ["snd12a"])
+            for j, key in ((1, "snd12b"), (2, "snd12c")):
+                vcopy(T.snd1[:, k, 128 * j:128 * j + 128], w.indirect(T.ls1[:, 8 * j:8 * j + 8]), ky, [key])
+            kk = [["snd12a"], ["snd12b"], ["snd12c"]]
+        c0 = 1024 * k + 8 * (64 + 16 * r)
+        send(T.win1[:, c0:c0 + 128], [T.snd1[:, k, 128 * j:128 * j + 128] for j in range(3)], "arr1k%d" % k, kk, (0, 1))
+
+    both, one = (0, 1), (1,)
+    first("S", 0, 0, 0)
+    first("V", 0, 0, 1)
+    gather(0, 0, 1, one)
+    gather(0, 1, 1)
+    gather(0, 1, 0)
+    gather(0, 2, 1)
+    vector(0, 0, one)
+    slots1(0)
+    gather(0, 2, 0)
+    vector(0, 1, both)
+    slots1(1)
+    last()
+    vector(0, 2, both)
+    slots1(2)
+    vcopy(T.lf[:], bank(2)[:, 0:96], ["bank2"], ["lf"])
+    first("V", 1, 0, 1)
+    first("S", 1, 0, 0)
+    gather(1, 0, 1, one)
+    for k in range(1, 3):
+        gather(1, k, 0)
+        gather(1, k, 1, one)
+    for k in range(3):
+        vector(1, k, one)
+
+    nst = [0]
+
+    def final(e, a, b):
+        h = 0 if b <= 48 else 1
+        out, src = T.yo[:, 16 * a:16 * b], T["n1" + "ab"[h]][:].indirect(T.lf[:, a:b])
+        ky = ["lf"] + ["n1%d%d" % (h, k) for k in range(3)]
+        if e == "V":
+            vcopy(out, src, ky, ["yo%d" % a])
+        else:
+            act(out, src, ky, ["yo%d" % a])
+        op("Y", lambda: g.sync.dma_start(T.y[:, 16 * a:16 * b], T.yo[:, 16 * a:16 * b]), ["yo%d" % a], [], "st%d" % nst[0], 16)
+        nst[0] += 1
+    final("S", 0, 24)
+    final("V", 48, 64)
+    final("S", 24, 48)
+    final("V", 64, 84)
+    final("S", 84, 96)
     for name in sorted(cnt):
         wait("Y", name, cnt[name])
     wait("G", "sent", (1 + 3) * nout)

@@ -10,19 +10,18 @@ def _s(cols, d):
 
 
 SCRATCH = {
-    "xs": _s(1536, F), "ish": _s(8, I), "iact": _s(4, I), "inbr": _s(16, I), "reln": _s([2, 24], I),
-    "pi": _s(1, I), "ci": _s(4, I), "cf": _s(4, F), "cc": _s(16, F), "pcols": _s(3, F), "pm2": _s(8, F), "bcol": _s(2, F),
-    "cqz": _s(128, B),
-    "cq": _s(128, B), "cqg": _s(128, B), "cqh": _s(128, B), "c8": _s(96, B), "c24": _s(96, B), "id124": _s(128, B),
-    "ct5": _s(640, B), "sg": _s(128, B), "tg": _s(128, B), "tgl": _s(128, B), "tgh": _s(128, B), "sel": _s([8, 128], B),
-    "idf": _s(128, F), "m16": _s(16, B), "gm": _s(8, F),
-    "rn4": _s([4, 16], F), "bd": _s([4, 128], B), "rt": _s([2, 512], B), "rm": _s([2, 512], B), "rte": _s(256, B),
-    "f8": _s(8, F), "f4": _s(4, F), "sps": _s(64, B), "spp": _s(64, B), "spa": _s(64, B), "nb8": _s(16, B), "ns8": _s(8, B),
-    "ohs": _s([2, 64], B), "oh0": _s([2, 64], B), "oha": _s([2, 64], B), "ohd": _s([2, 64], B),
-    "ohb": _s([2, 64], B), "a0f": _s(64, F), "a0g": _s(64, F), "pg": _s(64, F), "shu": _s(4, U), "mbs": _s([2, 64], F),
-    "dg": _s(16, F), "ecol": _s(1, F), "ohe": _s(2, F), "sge": _s([2, 128], B),
-    "ls0": _s(96, U), "l0": _s(96, U), "pfs": _s(96, F), "lrf": _s(384, F),
-    "lr0": _s(384, U), "lr1": _s(128, U), "ls1": _s(24, U), "kb": _s(96, B), "k1": _s(96, B), "k2": _s(96, B), "lf": _s(96, U),
+    "xs": _s(1536, F), "ipo": _s(4, I), "ish": _s(4, I), "iact": _s(4, I), "inbr": _s(16, I), "reln": _s(48, I),
+    "ctn": _s([2, 24], I),
+    "pi": _s(1, I), "ci": _s(4, I), "cf": _s(4, F), "cc": _s(16, F), "pcols": _s(3, F), "bcol": _s(2, F),
+    "cq": _s(128, B), "cqg": _s(128, B), "c48": _s(48, B), "i24": _s(128, F), "c8": _s(96, B), "id124": _s(128, B),
+    "c5": _s(640, B), "sgx": _s([2, 128], B), "w3": _s([2, 128], B), "gm": _s(8, F),
+    "idf": _s(128, F), "sd32": _s(128, F), "su32": _s(128, F),
+    "pu": _s(8, U), "mu": _s(8, U), "shu": _s(4, U), "nbu": _s(16, U),
+    "X": _s(128, F), "xs0": _s(64, F), "xs1": _s(64, F), "cp": _s(48, F), "cfb": _s([4, 16], B), "bd": _s([4, 128], B),
+    "a0s": _s(128, F), "ms": _s(128, F), "cpo": _s(128, F), "ohw": _s(128, B), "ohz": _s(128, B), "oha": _s(128, B),
+    "rd": _s([2, 128], B), "ya": _s(128, B), "ns8": _s(256, B), "ss8": _s(64, B),
+    "ls0": _s(96, U), "l0": _s(96, U), "lr0": _s(384, U), "lr1": _s(128, U), "ls1": _s(24, U),
+    "kb": _s(96, B), "k1": _s(96, B), "k2": _s(96, B), "lf": _s(96, U),
     "snd0": _s(1152, F), "snd1": _s([3, 384], F), "win0": _s(3072, F), "win1": _s(3072, F),
     "n1a": _s(768, F), "n1b": _s(768, F), "yo": _s(1536, F),
 }
@@ -31,8 +30,8 @@ for _t in range(2):
         for _n in ("ga", "gb", "ma", "mb"):
             SCRATCH["%s%d%d" % (_n, _t, _k)] = _s(512, F)
 for _b in range(8):
-    SCRATCH["bank%d" % _b] = ("psum", [128, 512], F)
-SEMAPHORES = ["cv", "cs", "ctn", "cg", "arr0", "arr1k0", "arr1k1", "arr1k2", "sent"] + ["ld%d" % i for i in range(8)] + ["st%d" % i for i in range(8)]
+    SCRATCH["bank%d" % _b] = ("psum", [128, 8, 64] if _b == 3 else [128, 512], F)
+SEMAPHORES = ["cv", "cs", "cte", "cg", "arr0", "arr1k0", "arr1k1", "arr1k2", "sent"] + ["ld%d" % i for i in range(10)] + ["st%d" % i for i in range(8)]
 AF = ActivationFunctionType
 COPY, IDENT, SIGN = AF.Copy, AF.Identity, AF.Sign
 A = AluOpType
@@ -40,7 +39,7 @@ A = AluOpType
 
 def _queues(g, T):
     q = {"V": g.vector, "S": g.scalar, "T": g.tensor, "G": g, "Y": g.sync}
-    csem = {"V": "cv", "S": "cs", "T": "ctn", "G": "cg"}
+    csem = {"V": "cv", "S": "cs", "T": "cte", "G": "cg"}
     cnt = {}
     known = {e: {} for e in q}
     wrote, read = {}, {}
@@ -138,13 +137,16 @@ def rank_program(g, core, T, topo):
     def mm(b, c0, n, parts, first=True, last=True):
         mmo(b, bank(b)[:, c0:c0 + n], parts, first, last)
 
-    op("Y", lambda: g.sync.dma_start(T.reln[:, 0, :], T.rel[:, 0:384]), [], ["relnA"], "ld0", 16)
-    op("S", lambda: s.dma_start(T.ish[:, 0:4], T.shown[:]), [], ["ishA"], "ld1", 16)
-    op("Y", lambda: g.sync.dma_start(T.reln[:, 1, :], T.rel[:, 192:576]), [], ["relnB"], "ld2", 16)
-    op("S", lambda: s.dma_start(T.ish[:, 4:8], T.pose[:]), [], ["ishB"], "ld3", 16)
+    op("Y", lambda: g.sync.dma_start(T.reln[:, 0:24], T.rel[:, 0:384]), [], ["relA"], "ld0", 16)
+    op("S", lambda: s.dma_start(T.ipo[:], T.pose[:]), [], ["ipo"], "ld1", 16)
+    op("Y", lambda: g.sync.dma_start(T.reln[:, 24:48], T.rel[:, 192:576]), [], ["relB"], "ld2", 16)
+    op("S", lambda: s.dma_start(T.ish[:], T.shown[:]), [], ["ish"], "ld3", 16)
     op("Y", lambda: g.sync.dma_start(T.xs[:], T.x[:]), [], ["xs"], "ld4", 16)
-    op("S", lambda: s.dma_start(T.iact[:], T.act[:]), [], ["iact"], "ld5", 16)
-    op("S", lambda: s.dma_start(T.inbr[:], T.nbr[:]), [], ["inbr"], "ld6", 16)
+    op("Y", lambda: g.sync.dma_start(T.iact[:], T.act[:]), [], ["iact"], "ld5", 16)
+    for y in range(2):
+        op("Y", lambda: g.sync.dma_start(T.ctn[:, y, :], T.ct[:, 192 * y:192 * y + 384]), [], ["ctn%d" % y], "ld%d" % (6 + y), 16)
+    op("Y", lambda: g.sync.dma_start(T.inbr[:], T.nbr[:]), [], ["inbr"], "ld8", 16)
+    relk, ctk = ["relA", "relB"], ["ctn0", "ctn1"]
 
     def iota(out, pat, base, cm, key, flag=True):
         if flag:
@@ -152,13 +154,11 @@ def rank_program(g, core, T, topo):
         else:
             op("G", lambda: g.iota(out, pat, base, cm), [], [key])
     iota(T.pi[:], [[1, 1]], 0, 1, "pi", False)
-    iota(T.cq[:], [[1, 128]], 0, 0, "cq")
-    iota(T.cqg[:], [[1, 8], [0, 16]], 0, 0, "cqg")
     iota(T.pcols[:], [[8, 3]], -8, 1, "pcols")
-    iota(T.cqh[:], [[1, 16], [0, 8]], 0, 0, "cqh")
-    iota(T.cqz[:], [[16, 8], [1, 2], [0, 8]], 0, 0, "cqz")
-    iota(T.pm2[:], [[-2, 8]], 0, 1, "pm2")
-    iota(T.c24[:], [[48, 32], [0, 3]], 0, 0, "c24a")
+    iota(T.cq[:], [[1, 128]], 0, 0, "cq")
+    iota(T.i24[:], [[0, 2], [24, 64]], 0, 0, "i24")
+    iota(T.c48[:], [[0, 2], [1, 24]], 0, 0, "c48")
+    iota(T.cqg[:], [[1, 8], [0, 16]], 0, 0, "cqg")
     op("V", lambda: v.tensor_scalar(T.ci[:, 0:1], T.pi[:], 4, None, A.arith_shift_right), ["pi"], ["ci0"])
     op("V", lambda: v.tensor_scalar(T.ci[:, 1:2], T.pi[:], 15, None, A.bitwise_and), ["pi"], ["ci1"])
     op("V", lambda: v.tensor_scalar(T.ci[:, 2:3], T.pi[:], 3, 1, A.arith_shift_right, A.bitwise_and), ["pi"], ["ci2"])
@@ -173,101 +173,45 @@ def rank_program(g, core, T, topo):
     def mkcol(name, src, m, a):
         ccn[name] = len(ccn)
         op("S", lambda: s.activation(col(name), src, COPY, bias=float(a), scale=float(m)), ["cf"], ["c_" + name])
-    ts(T.gm[:], T.cq[:, 0:8], gc, None, A.is_equal, None, ["cq", "cf"], ["gm"])
-    ts(T.m16[:], T.cq[:, 0:16], pc, None, A.is_equal, None, ["cq", "cf"], ["m16"])
     mkcol("nh", hc, -1, 1)
     mkcol("p8", pc, 1, 8)
-    mkcol("g2", gc, 2, 0)
-    mkcol("g21", gc, 2, 1)
-    mkcol("h24", hc, 24, 0)
     mkcol("big", hc, -100, 100)
     mkcol("h8", hc, 8, -4)
-    mkcol("p24", hc, 0, 24)
-    ts(T.sg[:], T.cqg[:], gc, None, A.is_equal, None, ["cqg", "cf"], ["sg"])
     colPm8, colP, colPp8 = (T.pcols[:, j:j + 1] for j in range(3))
-    c5 = T.ct5
 
     def tile(o1, src, s1, key, reads, s2=None):
         ts(o1, T[src][:], s1, s2, A.is_equal, A.mult if s2 is not None else None, [src] + reads, [key])
-    tile(T.tg[:], "cqg", gc, "tg", ["cf"], 24.0)
-    tile(c5[:, 0:128], "cq", colPp8, "t5b", ["pcols", "c_nh"], col("nh"))
-    tile(c5[:, 128:256], "cq", colP, "t5i", ["pcols"])
-    tile(c5[:, 256:384], "cq", colPm8, "t5a", ["pcols", "cf"], hc)
-    idb = c5[:, 128:256]
+    down, same, up, low, high = (T.c5[:, 128 * j:128 * j + 128] for j in range(5))
+    tile(down, "cq", colPm8, "down", ["pcols", "cf"], hc)
+    tile(same, "cq", colP, "same", ["pcols"])
+    tile(up, "cq", colPp8, "up", ["pcols", "c_nh"], col("nh"))
+    act(T.sd32[:], down, ["down"], ["sd32"])
+    act(T.idf[:], same, ["same"], ["idf"])
+    act(T.su32[:], up, ["up"], ["su32"])
 
-    vcopy(T.f8[:], T.ish[:], ["ishA", "ishB"], ["f8"])
-    for y in range(2):
-        vcopy(T.rn4[:, y::2, :], T.reln[:, :, 8 * y:8 * y + 16], ["relnA", "relnB"], ["rn4%d" % y])
-    for j in range(8):
-        out, sc = T.bd[:, :, 16 * j:16 * j + 16], T.gm[:, j:j + 1]
-        if j % 2:
-            act(out, T.rn4[:], ["rn40", "rn41", "gm"], ["bd%d" % j], sc)
-        else:
-            ts(out, T.rn4[:], sc, None, A.mult, None, ["rn40", "rn41", "gm"], ["bd%d" % j])
-    bdk = ["bd%d" % j for j in range(8)]
-    for u in range(4):
-        act(T.spp[:, 16 * u:16 * u + 16], T.m16[:], ["m16", "f8"], ["spp%d" % u], T.f8[:, 4 + u:5 + u])
-    tb = [5, 6, 7, 4]
+    vcopy(T.pu[:, 0:4], T.ipo[:], ["ipo"], ["pua"])
+    ts(T.pu[:, 4:8], T.ipo[:], 24.0, None, A.add, None, ["ipo"], ["pub"])
+    vcopy(T.shu[:], T.ish[:], ["ish"], ["shu"])
+    puk = ["pua", "pub"]
+    tt(T.X[:], T.reln[:].indirect(T.pu[:]), T.i24[:], A.add, relk + puk + ["i24"], ["X"])
+    vcopy(T.xs0[:], T.X[:, 0:64].indirect(T.shu[:]), ["X", "shu"], ["xs0"])
+    act(T.xs1[:], T.X[:, 64:128].indirect(T.shu[:]), ["X", "shu"], ["xs1"])
+    act(T.a0s[:], T.c48[:].indirect(T.pu[:]), puk + ["c48"], ["a0s"])
 
-    def tables(y, x):
-        l, c = T.bd[:, 2 * x + y, :], (c5[:, 0:256], c5[:, 128:384])[x]
-        mm(tb[2 * y + x], 0, 256, [(l, c, bdk + ["t5b", "t5i", "t5a"])])
-
-    def table_copy(y, x):
-        out, b, key = T.rt[:, y, 256 * x:256 * x + 256], tb[2 * y + x], ["rt%d%d" % (y, x)]
-        (act, vcopy)[y](out, bank(b)[:, 0:256], ["bank%d" % b], key)
-    tables(0, 0)
-    tables(1, 0)
-    mm(1, 0, 64, [(T.sg[:], T.spp[:], ["sg"] + ["spp%d" % u for u in range(4)])])
-    tables(0, 1)
-    tables(1, 1)
-    for p in range(n_ranks):
-        ts(T.sps[:, 16 * p:16 * p + 16], T.m16[:], T.f8[:, p:p + 1], None, A.mult, None, ["m16", "f8"], ["sps%d" % p])
-    spk = ["sps%d" % p for p in range(n_ranks)]
-    vcopy(T.shu[:], T.ish[:, 0:4], ["ishA"], ["shu"])
-    ev, od = T.sps[:, 0::2], T.sps[:, 1::2]
-    table_copy(0, 0)
-    act(T.a0f[:], bank(1)[:, 0:64], ["bank1"], ["a0f"])
-    table_copy(1, 0)
-    table_copy(0, 1)
-
-    def rt(y, name):
-        j = {"W": 0, "E1": 1, "E2": 2, "U": 3}[name]
-        return T.rt[:, y, 128 * j:128 * j + 128]
-
-    def rk(y, name):
-        return "rt%d%d" % (y, {"W": 0, "E1": 0, "E2": 1, "U": 1}[name])
-
-    def rm(y, j):
-        return T.rm[:, y, 128 * j:128 * j + 128]
-
-    def look(name, oh, par, key):
-        return [(rt(y, name), oh[:, y, par::2], [rk(y, name), key + str(y)]) for y in range(2)]
-
-    def onehot(dst, src, keys, key):
-        ts(dst[:, 0, :], src, pc, None, A.is_equal, None, keys + ["cf"], [key + "0"])
-        ts(dst[:, 1, :], src, col("p8"), hc, A.is_equal, A.mult, keys + ["cf", "c_p8"], [key + "1"])
-    vcopy(T.pg[:], T.a0f[:].indirect(T.shu[:]), ["a0f", "shu"], ["pg"])
-    tile(T.tgl[:], "cqh", col("g2"), "tgl", ["c_g2"], 24.0)
-    tile(T.tgh[:], "cqh", col("g21"), "tgh", ["c_g21"], 24.0)
-    onehot(T.ohs, T.pg[:], ["pg"], "ohs")
-    table_copy(1, 1)
-    onehot(T.oh0, T.a0f[:], ["a0f"], "oh0")
-    vcopy(T.f4[:], T.iact[:], ["iact"], ["f4"])
-    mm(2, 0, 32, [(T.tg[:], ev, ["tg"] + spk)], last=False)
-    mm(3, 0, 32, [(T.tgl[:], ev, ["tgl"] + spk), (T.tgh[:], od, ["tgh"] + spk)], last=False)
-    mm(2, 0, 32, look("E1", T.ohs, 0, "ohs"), first=False)
-    mm(4, 0, 32, [(T.tg[:], od, ["tg"] + spk)], last=False)
-    mm(3, 0, 32, look("W", T.ohs, 1, "ohs"), first=False, last=False)
-    mm(4, 0, 32, look("E2", T.ohs, 1, "ohs"), first=False)
-    mm(3, 0, 32, look("U", T.ohs, 0, "ohs"), first=False)
-    act(T.c24[:, 1::3], T.c24[:, 1::3], ["c24a", "c_h24"], ["c24b"], bias=col("h24"))
-    act(T.c24[:, 2::3], T.c24[:, 2::3], ["c24a", "c_p24"], ["c24c"], bias=col("p24"))
-    for u in range(4):
-        act(T.spa[:, 16 * u:16 * u + 16], T.m16[:], ["m16", "f4"], ["spa%d" % u], T.f4[:, u:u + 1])
-    for c in (0, 2, 1):
-        vcopy(T.ls0[:, c::3], bank(2 + c)[:, 0:32], ["bank%d" % (2 + c)], ["ls0%d" % c])
+    def middle(b, out, d, u):
+        mmo(b, out, [d, u])
+    middle(0, bank(0)[:, 0:32], (T.sd32[:], T.xs1[:, 0::2], ["sd32", "xs1"]), (T.su32[:], T.xs0[:, 1::2], ["su32", "xs0"]))
+    mmo(1, bank(1)[:, 0:96:3], [(T.idf[:], T.X[:, 0:64:2], ["idf", "X"])])
+    middle(1, bank(1)[:, 1:96:3], (T.sd32[:], T.X[:, 64:128:2], ["sd32", "X"]), (T.su32[:], T.X[:, 1:64:2], ["su32", "X"]))
+    mmo(1, bank(1)[:, 2:96:3], [(T.idf[:], T.X[:, 65:128:2], ["idf", "X"])])
+    vcopy(T.ls0[:, 0::3], T.xs0[:, 0::2], ["xs0"], ["ls00"])
+    vcopy(T.ls0[:, 2::3], T.xs1[:, 1::2], ["xs1"], ["ls02"])
+    tile(low, "cq", colP, "low", ["pcols", "c_nh"], col("nh"))
+    tile(high, "cq", colP, "high", ["pcols", "cf"], hc)
+    ts(T.gm[:], T.cq[:, 0:8], gc, None, A.is_equal, None, ["cq", "cf"], ["gm"])
+    vcopy(T.ls0[:, 1::3], bank(0)[:, 0:32], ["bank0"], ["ls01"])
     lsk = ["ls00", "ls01", "ls02", "xs"]
+    l0k = ["l0", "xs"]
 
     def slot0(e, j, a, b, key):
         c = 24 * dests[j]
@@ -301,94 +245,90 @@ def rank_program(g, core, T, topo):
     iota(T.bcol[:], [[-16, 2]], -15, 0, "bcol")
     iota(T.c8[:], [[0, 2], [16, 16], [4, 3]], 248, 0, "c8a")
 
-    def natural(b, oh, key, add=None):
-        for c, parts in enumerate((look("E1", oh, 0, key), look("U", oh, 0, key) + look("W", oh, 1, key), look("E2", oh, 1, key))):
-            more = [(idb, T.c24[:, c::3], ["t5i", "c24a", "c24b", "c24c"])] if add else []
-            mmo(b, bank(b)[:, c:96:3], parts + more)
+    def own(e, a, b, key):
+        src, out = T.xs[:].indirect(T.l0[:, a:b]), T.win0[:, 16 * a:16 * b]
+        if e == "V":
+            vcopy(out, src, l0k, [key])
+        else:
+            act(out, src, l0k, [key])
+    vcopy(T.l0[:], bank(1)[:, 0:96], ["bank1"], ["l0"])
+    tile(T.sgx[:, 0, :], "cqg", gc, "sgx0", ["cf"], pc)
+    tile(T.sgx[:, 1, :], "cqg", gc, "sgx1", ["cf", "c_p8"], col("p8"))
+    act(T.w3[:, 0, :], low, ["low"], ["w3l"], 3.0)
+    act(T.w3[:, 1, :], high, ["high"], ["w3h"], 3.0)
+    own("V", 0, 8, "win0a")
+    own("S", 72, 96, "win0b")
+    vcopy(T.mu[:, 0:4], T.iact[:], ["iact"], ["mua"])
+    ts(T.mu[:, 4:8], T.iact[:], 24.0, None, A.add, None, ["iact"], ["mub"])
+    vcopy(T.cp[:, 0:24], T.ctn[:, 0, :], ["ctn0"], ["cpa"])
+    ts(T.cp[:, 24:48], T.ctn[:, 1, :], col("big"), None, A.add, None, ["ctn1", "c_big"], ["cpb"])
+    muk, cpk = ["mua", "mub"], ["cpa", "cpb"]
+    tt(T.ohw[:], T.cp[:].indirect(T.mu[:]), T.a0s[:], A.is_equal, cpk + muk + ["a0s"], ["ohw"])
+    act(T.cpo[:], T.cp[:].indirect(T.pu[:]), cpk + puk, ["cpo"])
+    for y in range(2):
+        vcopy(T.cfb[:, y::2, :], T.ctn[:, :, 8 * y:8 * y + 16], ctk, ["cf%d" % y])
+    vcopy(T.nbu[:], T.inbr[:], ["inbr"], ["nbu"])
+    for c in range(2):
+        mm(2, 64 * c, 64, [(T.sgx[:, x, :], T.ohw[:, 64 * x:64 * x + 64], ["sgx%d" % x, "ohw"]) for x in range(2)])
+    for j in range(8):
+        out, sc = T.bd[:, :, 16 * j:16 * j + 16], T.gm[:, j:j + 1]
+        if j % 2:
+            ts(out, T.cfb[:], sc, None, A.mult, None, ["cf0", "cf1", "gm"], ["bd%d" % j])
+        else:
+            act(out, T.cfb[:], ["cf0", "cf1", "gm"], ["bd%d" % j], sc)
+    bdk = ["bd%d" % j for j in range(8)]
+    tt(T.ohz[:], T.cpo[:], bank(2)[:, 0:128], A.is_equal, ["cpo", "bank2"], ["ohz"])
+    own("V", 8, 40, "win0c")
 
-    def selected(b, c0, n, rhs, keys):
-        for m in range(8):
-            mmo(b, bank(b)[:, c0 + m:c0 + 8 * n:8], [(T.sel[:, m, :], rhs, keys + ["sel%d" % m])])
-    mm(0, 0, 64, [(T.sg[:], T.spa[:], ["sg"] + ["spa%d" % u for u in range(4)])])
-    act(T.mbs[:, 0, :], bank(0)[:, 0:64], ["bank0"], ["mbs0"])
-    act(T.mbs[:, 1, :], bank(0)[:, 0:64], ["bank0", "c_big"], ["mbs1"], bias=col("big"))
-    act(T.a0g[:], T.a0f[:], ["a0f", "c_big"], ["a0g"], bias=col("big"))
-    for x, name in enumerate(("E1", "E2")):
-        mm(2, 64 * x, 64, [(rt(y, name), T.oh0[:, y, :], [rk(y, name), "oh0%d" % y]) for y in range(2)])
-    natural(0, T.oh0, "oh0", True)
-    tile(c5[:, 384:512], "cq", colP, "t5l", ["pcols", "c_nh"], col("nh"))
-    tile(c5[:, 512:640], "cq", colP, "t5h", ["pcols", "cf"], hc)
-    tt(T.dg[:], T.rn4[:, 0, :], T.m16[:], A.mult, ["rn40", "m16"], ["dg"])
-    for x in range(2):
-        tt(T.oha[:, x, :], bank(2)[:, 64 * x:64 * x + 64], T.mbs[:, x, :], A.is_equal, ["bank2", "mbs%d" % x], ["oha%d" % x])
-    ts(T.nb8[:], T.inbr[:], 8.0, None, A.mult, None, ["inbr"], ["nb8"])
-    vcopy(T.l0[:], bank(0)[:, 0:96], ["bank0"], ["l0"])
-    for m in range(8):
-        tile(T.sel[:, m, :], "cqz", T.pm2[:, m:m + 1], "sel%d" % m, ["pm2"])
-    l0k = ["l0", "xs"]
-    for y in range(2):
-        mm(4, 64 * y, 64, [(T.bd[:, 2 * x + y, :], T.oha[:, x, :], bdk + ["oha%d" % x]) for x in range(2)])
-    for y in range(2):
-        for x in range(2):
-            mm(5 + y, 256 * x, 256, [(T.bd[:, 2 * x + y, :], c5[:, 384:640], bdk + ["t5l", "t5h"])])
-    act(T.win0[:, 1152:1536], T.xs[:].indirect(T.l0[:, 72:96]), l0k, ["win0c"])
-    act(T.rm[:, 0, :], bank(5)[:], ["bank5"], ["rm0"])
-    selected(7, 0, 16, T.nb8[:], ["nb8"])
-    op("V", lambda: v.tensor_reduce(T.ecol[:], T.dg[:], AxisListType.X, A.add), ["dg"], ["ecol"])
+    def rows(b, oh, key):
+        for y in range(2):
+            out = bank(b)[:, y, :] if b == 3 else bank(b)[:, 64 * y:64 * y + 64]
+            mmo(b, out, [(T.bd[:, 2 * x + y, :], oh[:, 64 * x:64 * x + 64], bdk + [key]) for x in range(2)])
+    rows(3, T.ohz, "ohz")
+    act(T.ns8[:], T.cq[:].indirect(T.nbu[:]), ["cq", "nbu"], ["ns8"], 8.0)
+    for n in range(2):
+        act(T.rd[:, :, 64 * n:64 * n + 64], T.bank3[:, 0:2, :], ["bank3"], ["rd%d" % n])
+    rdk = ["rd%d" % n for n in range(2)]
+    own("S", 60, 72, "win0d")
+    act(T.ms[:, 0:64], T.c48[:].indirect(T.mu[:, 0:4]), ["c48", "mua"], ["ms0"])
+    act(T.ms[:, 64:128], T.c48[:].indirect(T.mu[:, 4:8]), ["c48", "mub", "c_big"], ["ms1"], bias=col("big"))
+    ev, od = T.ns8[:, 0::2], T.ns8[:, 1::2]
+    r1e, r1o, r2e, r2o = (T.rd[:, e, o::2] for e in range(2) for o in range(2))
+    turn = [((low, r1e, "low"), (up, r1o, "up")), ((low, r2e, "low"), (high, r1o, "high")), ((down, r2e, "down"), (high, r2o, "high"))]
     for k in range(3):
-        act(bank(0)[:, 128 * k:128 * k + 128], bank(7)[:, 0:128], ["bank7"], ["bank0"], 3.0)
-    for j in range(2):
-        act(T.ns8[:, 4 * j:4 * j + 4], T.f8[:, 0:4], ["f8"], ["ns8%d" % j], 8.0)
-    act(T.idf[:], idb, ["t5i"], ["idf"])
-    act(T.id124[:], idb, ["t5i"], ["id124"], 124.0)
+        mm(4 + k, 0, 128, [(T.w3[:, 0, :], ev, ["w3l", "ns8"])], last=False)
+        for n in range(2):
+            mm(4 + k, 64 * n, 64, [(t, rh, [key] + rdk) for t, rh, key in turn[k]], first=False, last=False)
+        mm(4 + k, 0, 128, [(T.w3[:, 1, :], od, ["w3h", "ns8"])], first=False)
+    own("V", 40, 60, "win0e")
+    act(T.id124[:], same, ["same"], ["id124"], 124.0)
     act(T.c8[:, 1::3], T.c8[:, 1::3], ["c8a", "c_h8"], ["c8b"], bias=col("h8"))
-    vcopy(T.win0[:, 0:288], T.xs[:].indirect(T.l0[:, 0:18]), l0k, ["win0a"])
-    for y in range(2):
-        tt(T.ohd[:, y, :], bank(4)[:, 64 * y:64 * y + 64], (T.a0f, T.a0g)[y][:], A.is_equal, ["bank4", ("a0f", "a0g")[y]], ["ohd%d" % y])
-    vcopy(T.rm[:, 1, :], bank(6)[:], ["bank6"], ["rm1"])
-    vcopy(T.win0[:, 288:672], T.xs[:].indirect(T.l0[:, 18:42]), l0k, ["win0d"])
-    tiles = [("M", 0, "R", "W"), ("M", 2, "M", 1), ("R", "U", "M", 3)]
-
-    def half(y, kind, name):
-        return (rt(y, name), rk(y, name)) if kind == "R" else (rm(y, name), "rm%d" % y)
-    for k, (ka, na, kb, nb) in enumerate(tiles):
-        parts = []
-        for par, kind, name in ((0, ka, na), (1, kb, nb)):
-            for y in range(2):
-                t, key = half(y, kind, name)
-                parts.append((t, T.ohd[:, y, par::2], [key, "ohd%d" % y]))
-        mm(3, 32 * k, 32, parts)
-    ts(T.ohe[:, 0:1], pc, T.ecol[:], None, A.is_equal, None, ["cf", "ecol"], ["ohe0"])
-    ts(T.ohe[:, 1:2], col("p8"), T.ecol[:], hc, A.is_equal, A.mult, ["cf", "c_p8", "ecol"], ["ohe1"])
-    for x in range(2):
-        act(T.sge[:, x, :], T.sg[:], ["sg", "ohe%d" % x], ["sge%d" % x], T.ohe[:, x:x + 1])
-    for y in range(2):
-        mm(1, 128 * y, 128, [(T.bd[:, 2 * x + y, :], T.sge[:, x, :], bdk + ["sge%d" % x]) for x in range(2)])
-    act(T.rte[:], bank(1)[:, 0:256], ["bank1"], ["rte"])
-    act(T.win0[:, 672:1152], T.xs[:].indirect(T.l0[:, 42:72]), l0k, ["win0b"])
-    selected(2, 128, 3, T.ns8[:, r + 1:r + 4], ["ns80", "ns81"])
-    mm(2, 0, 64, [(T.rte[:, 128 * y:128 * y + 128], T.oha[:, y, :], ["rte", "oha%d" % y]) for y in range(2)])
-    vcopy(T.pfs[:], bank(3)[:, 0:96], ["bank3"], ["pfs"])
+    act(T.ss8[:], T.cq[:].indirect(T.shu[:]), ["cq", "shu"], ["ss8"], 8.0)
+    mm(7, 0, 128, [(low, ev, ["low", "ns8"]), (high, od, ["high", "ns8"])])
+    for j, d in enumerate(dests):
+        mm(7, 128 + 8 * j, 8, [(low, T.ss8[:, 16 * d:16 * d + 16:2], ["low", "ss8"]), (high, T.ss8[:, 16 * d + 1:16 * d + 16:2], ["high", "ss8"])])
     for k in range(3):
-        for n in range(4):
-            c = 128 * k + 32 * n
-            tt(T.lrf[:, c:c + 32], bank(0)[:, c:c + 32], T.pfs[:, 32 * k:32 * k + 32], A.add, ["bank0", "pfs"], ["lrf%d%d" % (k, n)])
-    ts(T.lr1[:], bank(7)[:, 0:128], k8, None, A.add, None, ["bank7", "cf"], ["lr1"])
-    for k in range(3):
-        vcopy(T.lr0[:, 128 * k:128 * k + 128], T.lrf[:, 128 * k:128 * k + 128], ["lrf%d%d" % (k, n) for n in range(4)], ["lr0%d" % k])
-    ts(T.ls1[:], bank(2)[:, 128:152], k8, None, A.add, None, ["bank2", "cf"], ["ls1"])
-    onehot(T.ohb, bank(2)[:, 0:64], ["bank2"], "ohb")
-    natural(4, T.ohb, "ohb")
+        vcopy(T.lr0[:, 128 * k:128 * k + 128], bank(4 + k)[:, 0:128], ["bank%d" % (4 + k)], ["lr0%d" % k])
+        if k == 0:
+            tt(T.oha[:], T.reln[:].indirect(T.pu[:]), T.ms[:], A.is_equal, relk + puk + ["ms0", "ms1"], ["oha"])
+            rows(2, T.oha, "oha")
 
-    def last():
-        act(T.kb[:], bank(4)[:, 0:96], ["bank4"], ["kb"])
+    def last1():
+        act(T.ya[:], bank(2)[:, 0:128], ["bank2"], ["ya"])
+        mmo(5, bank(5)[:, 0:96:3], [(same, T.ya[:, 0:64:2], ["same", "ya"])])
+        middle(5, bank(5)[:, 1:96:3], (down, T.ya[:, 64:128:2], ["down", "ya"]), (up, T.ya[:, 1:64:2], ["up", "ya"]))
+        mmo(5, bank(5)[:, 2:96:3], [(same, T.ya[:, 65:128:2], ["same", "ya"])])
+
+    def last2():
+        act(T.kb[:], bank(5)[:, 0:96], ["bank5"], ["kb"])
         for j in range(2):
             out, b, key = T["k%d" % (j + 1)], T.bcol[:, j:j + 1], "k%d" % (j + 1)
-            op("S", lambda: s.activation(out[:], bank(4)[:, 0:96], SIGN, bias=b, scale=2.0), ["bank4", "bcol"], [key])
-        mm(2, 0, 96, [(idb, T.c8[:], ["t5i", "c8a", "c8b"]), (idb, T.kb[:], ["kb"])] + [(T.id124[:], T[k][:], ["id124", k]) for k in ("k1", "k2")])
+            op("S", lambda: s.activation(out[:], bank(5)[:, 0:96], SIGN, bias=b, scale=2.0), ["bank5", "bcol"], [key])
+        mm(6, 0, 96, [(same, T.c8[:], ["same", "c8a", "c8b"]), (same, T.kb[:], ["kb"])] + [(T.id124[:], T[k][:], ["id124", k]) for k in ("k1", "k2")])
 
     hs = [slice(256 * h, 256 * h + 256) for h in range(2)]
-    pb = {(0, 0): 5, (0, 1): 6, (0, 2): 7, (1, 0): 0, (1, 1): 1, (1, 2): 3}
+    pb = {(0, 0): 0, (0, 1): 1, (0, 2): 2, (1, 0): 4, (1, 1): 5, (1, 2): 6}
+    pcopy = {(1, 0, 0): 7, (1, 1, 0): 0}
 
     def win(t, k):
         return T.win0[:] if t == 0 else T.win1[:, 1024 * k:1024 * k + 1024]
@@ -398,7 +338,7 @@ def rank_program(g, core, T, topo):
         return T.lr0[:, c + a:c + b] if t == 0 else T.lr1[:, c + a:c + b]
 
     def keys(t, k):
-        return ["win0a", "win0b", "win0c", "win0d", "lr0%d" % k] if t == 0 else ["f1%d0" % k, "f1%d1" % k, "lr1"]
+        return ["win0a", "win0b", "win0c", "win0d", "win0e", "lr0%d" % k] if t == 0 else ["f1%d0" % k, "f1%d1" % k, "lr1"]
 
     def arrived(e, t, k):
         wait(e, "arr0" if t == 0 else "arr1k%d" % k, nin)
@@ -426,7 +366,10 @@ def rank_program(g, core, T, topo):
         for h in halves:
             if not whole:
                 act(buf(nm, t, k)[:, hs[h]], win(t, k).indirect(lst(t, k, n, 16 * h, 16 * h + 16)), keys(t, k), [bk(nm, t, k, h)])
-            if n == 1:
+            if n == 1 and (t, k, h) in pcopy:
+                b = pcopy[t, k, h]
+                act(bank(b)[:, hs[h]], buf(nm, t, k)[:, hs[h]], [bk(nm, t, k, h)], ["bank%d" % b])
+            elif n == 1:
                 mm(pb[t, k], 256 * h, 256, [(T.idf[:], buf(nm, t, k)[:, hs[h]], ["idf", bk(nm, t, k, h)])])
 
     def result(t, k, h):
@@ -442,17 +385,21 @@ def rank_program(g, core, T, topo):
 
     def join(t, k, h):
         out, key = result(t, k, h)
-        tt(out, bank(pb[t, k])[:, hs[h]], buf("mb", t, k)[:, hs[h]], A.max, ["bank%d" % pb[t, k], bk("mb", t, k, h)], [key])
+        b = pcopy.get((t, k, h), pb[t, k])
+        tt(out, bank(b)[:, hs[h]], buf("mb", t, k)[:, hs[h]], A.max, ["bank%d" % b, bk("mb", t, k, h)], [key])
 
-    def vector(t, k, moved):
-        for n in (2, 3):
-            for h in range(2):
-                part(t, k, n, h)
-        for h in range(2):
-            if h in moved:
+    both, one = (0, 1), (1,)
+    moved = {(0, 0): one, (0, 1): both, (0, 2): both, (1, 0): (1, 0), (1, 1): (1, 0), (1, 2): one}
+
+    def vector(t, order):
+        for k, n, h in order:
+            if n == 1 and h in moved[t, k]:
                 join(t, k, h)
             else:
-                part(t, k, 1, h)
+                part(t, k, n, h)
+
+    def block(k):
+        return [(k, n, h) for n in (2, 3, 1) for h in range(2)]
 
     def slots1(k):
         w, ky = T.win1[:, 1024 * k:1024 * k + 512], ["f1%d0" % k, "f1%d1" % k, "ls1"]
@@ -467,30 +414,32 @@ def rank_program(g, core, T, topo):
         c0 = 1024 * k + 8 * (64 + 16 * r)
         send(T.win1[:, c0:c0 + 128], [T.snd1[:, k, 128 * j:128 * j + 128] for j in range(3)], "arr1k%d" % k, kk, (0, 1))
 
-    both, one = (0, 1), (1,)
     first("S", 0, 0, 0)
     first("V", 0, 0, 1)
-    gather(0, 0, 1, one)
-    gather(0, 1, 1)
+    ts(T.lr1[:], bank(7)[:, 0:128], k8, None, A.add, None, ["bank7", "cf"], ["lr1"])
+    ts(T.ls1[:], bank(7)[:, 128:152], k8, None, A.add, None, ["bank7", "cf"], ["ls1"])
+    gather(0, 0, 1, moved[0, 0])
+    gather(0, 1, 1, moved[0, 1])
+    last1()
     gather(0, 1, 0)
-    gather(0, 2, 1)
-    vector(0, 0, one)
+    gather(0, 2, 1, moved[0, 2])
+    vector(0, block(0))
     slots1(0)
     gather(0, 2, 0)
-    vector(0, 1, both)
+    vector(0, block(1))
     slots1(1)
-    last()
-    vector(0, 2, both)
+    last2()
+    vector(0, block(2))
     slots1(2)
-    vcopy(T.lf[:], bank(2)[:, 0:96], ["bank2"], ["lf"])
+    vcopy(T.lf[:], bank(6)[:, 0:96], ["bank6"], ["lf"])
     first("V", 1, 0, 1)
     first("S", 1, 0, 0)
-    gather(1, 0, 1, one)
+    gather(1, 0, 1, moved[1, 0])
     for k in range(1, 3):
         gather(1, k, 0)
-        gather(1, k, 1, one)
-    for k in range(3):
-        vector(1, k, one)
+        gather(1, k, 1, moved[1, k])
+    vector(1, block(0))
+    vector(1, [(1, 2, 0), (1, 2, 1), (1, 3, 0), (1, 3, 1), (1, 1, 0), (2, 2, 0), (1, 1, 1), (2, 3, 0), (2, 1, 0), (2, 2, 1), (2, 3, 1), (2, 1, 1)])
 
     nst = [0]
 
@@ -505,10 +454,9 @@ def rank_program(g, core, T, topo):
         op("Y", lambda: g.sync.dma_start(T.y[:, 16 * a:16 * b], T.yo[:, 16 * a:16 * b]), ["yo%d" % a], [], "st%d" % nst[0], 16)
         nst[0] += 1
     final("S", 0, 24)
-    final("V", 48, 64)
     final("S", 24, 48)
-    final("V", 64, 84)
-    final("S", 84, 96)
+    final("V", 48, 72)
+    final("S", 72, 96)
     for name in sorted(cnt):
         wait("Y", name, cnt[name])
     wait("G", "sent", (1 + 3) * nout)

import numpy as np
from concourse.bass import DstId, RemoteDMATransfer
from concourse.mybir import dt, AluOpType, AxisListType, ActivationFunctionType

F, B, I, U = "float32", "bfloat16", "int32", "uint16"


def _s(cols, d):
    return ("sbuf", [128] + (cols if isinstance(cols, list) else [cols]), d)


SCRATCH = {
    "xs": _s(1536, F), "ipo": _s(4, I), "ish": _s(4, I), "iact": _s(4, I), "inbr": _s(16, I), "reln": _s(48, I),
    "ctn": _s([2, 24], I),
    "pi": _s(1, I), "ci": _s(4, I), "cf": _s(4, F), "cc": _s(16, F), "pcols": _s(3, F), "bcol": _s(2, F),
    "cq": _s(128, B), "cqg": _s(128, B), "c48": _s(48, B), "i24": _s(128, F), "c8": _s(96, B), "id124": _s(128, B),
    "c5": _s(640, B), "sgx": _s([2, 128], B), "w3": _s([2, 128], B), "gm": _s(8, F),
    "idf": _s(128, F), "sd32": _s(128, F), "su32": _s(128, F),
    "pu": _s(8, U), "mu": _s(8, U), "shu": _s(4, U), "nbu": _s(16, U),
    "X": _s(128, F), "xs0": _s(64, F), "xs1": _s(64, F), "cp": _s(48, F), "cfb": _s([4, 16], B), "bd": _s([4, 128], B),
    "a0s": _s(128, F), "ms": _s(128, F), "cpo": _s(128, F), "ohw": _s(128, B), "ohz": _s(128, B), "oha": _s(128, B),
    "rd": _s([2, 128], B), "ya": _s(128, B), "ns8": _s(256, B), "ss8": _s(64, B),
    "ls0": _s(96, U), "l0": _s(96, U), "lr0": _s(384, U), "lr1": _s(128, U), "ls1": _s(24, U),
    "kb": _s(96, B), "k1": _s(96, B), "k2": _s(96, B), "lf": _s(96, U),
    "snd0": _s(1152, F), "snd1": _s([3, 384], F), "win0": _s(3072, F), "win1": _s(3072, F),
    "n1a": _s(768, F), "n1b": _s(768, F), "yo": _s(1536, F),
}
for _t in range(2):
    for _k in range(3):
        for _n in ("ga", "gb", "ma", "mb"):
            SCRATCH["%s%d%d" % (_n, _t, _k)] = _s(512, F)
for _b in range(8):
    SCRATCH["bank%d" % _b] = ("psum", [128, 8, 64] if _b == 3 else [128, 512], F)
SEMAPHORES = ["cv", "cs", "cte", "cg", "arr0", "arr1k0", "arr1k1", "arr1k2", "sent"] + ["ld%d" % i for i in range(10)] + ["st%d" % i for i in range(8)]
AF = ActivationFunctionType
COPY, IDENT, SIGN = AF.Copy, AF.Identity, AF.Sign
A = AluOpType


def _queues(g, T):
    q = {"V": g.vector, "S": g.scalar, "T": g.tensor, "G": g, "Y": g.sync}
    csem = {"V": "cv", "S": "cs", "T": "cte", "G": "cg"}
    cnt = {}
    known = {e: {} for e in q}
    wrote, read = {}, {}

    def after(e, tok):
        sem, val, snap = tok[1], tok[2], tok[3]
        if known[e].get(sem, 0) < val:
            q[e].wait_ge(T.sem[sem], val)
            known[e][sem] = val
            for s, v in snap.items():
                if known[e].get(s, 0) < v:
                    known[e][s] = v

    def op(e, fn, reads=(), writes=(), sem=None, inc=1, signal=True):
        toks = []
        for k in reads:
            if k in wrote:
                toks.append(wrote[k])
            if k.startswith("bank"):
                toks += [t for t in read.get(k, []) if t[0] != e]
        for k in writes:
            if k in wrote and not (e == "T" and wrote[k][0] == "T"):
                toks.append(wrote[k])
            toks += [t for t in read.get(k, []) if t[0] != e]
        best = {}
        for t in toks:
            if t[1] not in best or best[t[1]][2] < t[2]:
                best[t[1]] = t
        for t in best.values():
            after(e, t)
        ins = fn()
        if not signal:
            return
        name = sem or csem[e]
        cnt[name] = cnt.get(name, 0) + inc
        ins.then_inc(T.sem[name], inc)
        tok = (e, name, cnt[name], dict(known[e]))
        for k in reads:
            read.setdefault(k, []).append(tok)
        for k in writes:
            wrote[k] = tok
            read[k] = []

    def wait(e, sem, val):
        if known[e].get(sem, 0) < val:
            q[e].wait_ge(T.sem[sem], val)
            known[e][sem] = val
    return q, op, wait, cnt


def rank_program(g, core, T, topo):
    r = T.rank_of(core)
    if r is None:
        return
    ranks = list(T.cores)
    n_ranks = len(ranks)
    dests = [(r + 1 + j) % n_ranks for j in range(n_ranks - 1)]
    q, op, wait, cnt = _queues(g, T)
    v, s, te = g.vector, g.scalar, g.tensor

    def share(a, b, i):
        es = topo.engines(a, b)
        h = len(es) // 2
        return (es[:h], es[h:], es)[i]
    nout = sum(len(share(core, ranks[d], j)) for j, d in enumerate(dests))
    nin = sum(len(share(ranks[(r - 1 - j) % n_ranks], core, j)) for j in range(n_ranks - 1))

    def bank(b):
        return T["bank%d" % b]

    def ts(out, in0, s1, s2, o0, o1, reads, writes):
        if o1 is None:
            op("V", lambda: v.tensor_scalar(out, in0, s1, None, o0), reads, writes)
        else:
            op("V", lambda: v.tensor_scalar(out, in0, s1, s2, o0, o1), reads, writes)

    def tt(out, a, b, o, reads, writes):
        op("V", lambda: v.tensor_tensor(out, a, b, o), reads, writes)

    def vcopy(out, a, reads, writes):
        op("V", lambda: v.tensor_copy(out, a), reads, writes)

    def act(out, a, reads, writes, scale=None, bias=None):
        if bias is not None:
            op("S", lambda: s.activation(out, a, IDENT, bias=bias), reads, writes)
        elif scale is None:
            op("S", lambda: s.activation(out, a, COPY), reads, writes)
        else:
            op("S", lambda: s.activation(out, a, COPY, scale=scale), reads, writes)

    def mmo(b, out, parts, first=True, last=True):
        for i, (l, rh, keys) in enumerate(parts):
            op("T", lambda: te.matmul(out, l, rh, first and i == 0, last and i == len(parts) - 1), keys, ["bank%d" % b])

    def mm(b, c0, n, parts, first=True, last=True):
        mmo(b, bank(b)[:, c0:c0 + n], parts, first, last)

    op("Y", lambda: g.sync.dma_start(T.reln[:, 0:24], T.rel[:, 0:384]), [], ["relA"], "ld0", 16)
    op("S", lambda: s.dma_start(T.ipo[:], T.pose[:]), [], ["ipo"], "ld1", 16)
    op("Y", lambda: g.sync.dma_start(T.reln[:, 24:48], T.rel[:, 192:576]), [], ["relB"], "ld2", 16)
    op("S", lambda: s.dma_start(T.ish[:], T.shown[:]), [], ["ish"], "ld3", 16)
    op("Y", lambda: g.sync.dma_start(T.xs[:], T.x[:]), [], ["xs"], "ld4", 16)
    op("Y", lambda: g.sync.dma_start(T.iact[:], T.act[:]), [], ["iact"], "ld5", 16)
    for y in range(2):
        op("Y", lambda: g.sync.dma_start(T.ctn[:, y, :], T.ct[:, 192 * y:192 * y + 384]), [], ["ctn%d" % y], "ld%d" % (6 + y), 16)
    op("Y", lambda: g.sync.dma_start(T.inbr[:], T.nbr[:]), [], ["inbr"], "ld8", 16)
    relk, ctk = ["relA", "relB"], ["ctn0", "ctn1"]

    def iota(out, pat, base, cm, key, flag=True):
        if flag:
            op("G", lambda: g.iota(out, pat, base, cm, allow_small_or_imprecise_dtypes=True), [], [key])
        else:
            op("G", lambda: g.iota(out, pat, base, cm), [], [key])
    iota(T.pi[:], [[1, 1]], 0, 1, "pi", False)
    iota(T.pcols[:], [[8, 3]], -8, 1, "pcols")
    iota(T.cq[:], [[1, 128]], 0, 0, "cq")
    iota(T.i24[:], [[0, 2], [24, 64]], 0, 0, "i24")
    iota(T.c48[:], [[0, 2], [1, 24]], 0, 0, "c48")
    iota(T.cqg[:], [[1, 8], [0, 16]], 0, 0, "cqg")
    op("V", lambda: v.tensor_scalar(T.ci[:, 0:1], T.pi[:], 4, None, A.arith_shift_right), ["pi"], ["ci0"])
    op("V", lambda: v.tensor_scalar(T.ci[:, 1:2], T.pi[:], 15, None, A.bitwise_and), ["pi"], ["ci1"])
    op("V", lambda: v.tensor_scalar(T.ci[:, 2:3], T.pi[:], 3, 1, A.arith_shift_right, A.bitwise_and), ["pi"], ["ci2"])
    op("V", lambda: v.tensor_scalar(T.ci[:, 3:4], T.pi[:], 7, None, A.bitwise_and), ["pi"], ["ci3"])
    vcopy(T.cf[:], T.ci[:], ["ci0", "ci1", "ci2", "ci3"], ["cf"])
    gc, pc, hc, k8 = (T.cf[:, j:j + 1] for j in range(4))
    ccn = {}

    def col(name):
        return T.cc[:, ccn[name]:ccn[name] + 1]

    def mkcol(name, src, m, a):
        ccn[name] = len(ccn)
        op("S", lambda: s.activation(col(name), src, COPY, bias=float(a), scale=float(m)), ["cf"], ["c_" + name])
    mkcol("nh", hc, -1, 1)
    mkcol("p8", pc, 1, 8)
    mkcol("big", hc, -100, 100)
    mkcol("h8", hc, 8, -4)
    colPm8, colP, colPp8 = (T.pcols[:, j:j + 1] for j in range(3))

    def tile(o1, src, s1, key, reads, s2=None):
        ts(o1, T[src][:], s1, s2, A.is_equal, A.mult if s2 is not None else None, [src] + reads, [key])
    down, same, up, low, high = (T.c5[:, 128 * j:128 * j + 128] for j in range(5))
    tile(down, "cq", colPm8, "down", ["pcols", "cf"], hc)
    tile(same, "cq", colP, "same", ["pcols"])
    tile(up, "cq", colPp8, "up", ["pcols", "c_nh"], col("nh"))
    act(T.sd32[:], down, ["down"], ["sd32"])
    act(T.idf[:], same, ["same"], ["idf"])
    act(T.su32[:], up, ["up"], ["su32"])

    vcopy(T.pu[:, 0:4], T.ipo[:], ["ipo"], ["pua"])
    ts(T.pu[:, 4:8], T.ipo[:], 24.0, None, A.add, None, ["ipo"], ["pub"])
    vcopy(T.shu[:], T.ish[:], ["ish"], ["shu"])
    puk = ["pua", "pub"]
    tt(T.X[:], T.reln[:].indirect(T.pu[:]), T.i24[:], A.add, relk + puk + ["i24"], ["X"])
    vcopy(T.xs0[:], T.X[:, 0:64].indirect(T.shu[:]), ["X", "shu"], ["xs0"])
    act(T.xs1[:], T.X[:, 64:128].indirect(T.shu[:]), ["X", "shu"], ["xs1"])
    act(T.a0s[:], T.c48[:].indirect(T.pu[:]), puk + ["c48"], ["a0s"])

    def middle(b, out, d, u):
        mmo(b, out, [d, u])
    middle(0, bank(0)[:, 0:32], (T.sd32[:], T.xs1[:, 0::2], ["sd32", "xs1"]), (T.su32[:], T.xs0[:, 1::2], ["su32", "xs0"]))
    mmo(1, bank(1)[:, 0:96:3], [(T.idf[:], T.X[:, 0:64:2], ["idf", "X"])])
    middle(1, bank(1)[:, 1:96:3], (T.sd32[:], T.X[:, 64:128:2], ["sd32", "X"]), (T.su32[:], T.X[:, 1:64:2], ["su32", "X"]))
    mmo(1, bank(1)[:, 2:96:3], [(T.idf[:], T.X[:, 65:128:2], ["idf", "X"])])
    vcopy(T.ls0[:, 0::3], T.xs0[:, 0::2], ["xs0"], ["ls00"])
    vcopy(T.ls0[:, 2::3], T.xs1[:, 1::2], ["xs1"], ["ls02"])
    tile(low, "cq", colP, "low", ["pcols", "c_nh"], col("nh"))
    tile(high, "cq", colP, "high", ["pcols", "cf"], hc)
    ts(T.gm[:], T.cq[:, 0:8], gc, None, A.is_equal, None, ["cq", "cf"], ["gm"])
    vcopy(T.ls0[:, 1::3], bank(0)[:, 0:32], ["bank0"], ["ls01"])
    lsk = ["ls00", "ls01", "ls02", "xs"]
    l0k = ["l0", "xs"]

    def slot0(e, j, a, b, key):
        c = 24 * dests[j]
        src, out = T.xs[:].indirect(T.ls0[:, c + a:c + b]), T.snd0[:, 384 * j + 16 * a:384 * j + 16 * b]
        if e == "V":
            vcopy(out, src, lsk, [key])
        else:
            act(out, src, lsk, [key])
    slot0("V", 0, 0, 12, "snd0a")
    slot0("S", 0, 12, 24, "snd0b")
    slot0("V", 1, 0, 24, "snd0c")
    slot0("S", 2, 0, 24, "snd0d")

    def send(out, srcs, sem, keys, pair):
        at = [topo.addr(ranks[d])[:2] for d in dests]

        def mask(j, i):
            return sum(1 << e for e in share(core, ranks[dests[j]], i))
        alone = 3 - sum(pair)
        two = [RemoteDMATransfer(dst_ids=[DstId(rid=at[j][0], pnc=at[j][1])], dma_engine_mask=mask(j, i), remote_sem=T.sem[sem], srcs=[srcs[j]], dsts=[out], alu_op=0) for i, j in enumerate(pair)]

        def fused():
            op("G", lambda: g.remote_dma_fused(two, local_sem=T.sem.sent), keys[pair[0]] + keys[pair[1]], [], signal=False)

        def single():
            op("G", lambda: g.remote_dma(out, srcs[alone], T.sem[sem], T.sem.sent, at[alone][1], at[alone][0], mask(alone, 2)), keys[alone], [], signal=False)
        for f in ((single, fused) if alone == 0 else (fused, single)):
            f()
    c0 = 24 * (64 + 16 * r)
    send(T.win0[:, c0:c0 + 384], [T.snd0[:, 384 * j:384 * j + 384] for j in range(3)], "arr0", [["snd0a", "snd0b"], ["snd0c"], ["snd0d"]], (1, 2))
    iota(T.bcol[:], [[-16, 2]], -15, 0, "bcol")
    iota(T.c8[:], [[0, 2], [16, 16], [4, 3]], 248, 0, "c8a")

    def own(e, a, b, key):
        src, out = T.xs[:].indirect(T.l0[:, a:b]), T.win0[:, 16 * a:16 * b]
        if e == "V":
            vcopy(out, src, l0k, [key])
        else:
            act(out, src, l0k, [key])
    vcopy(T.l0[:], bank(1)[:, 0:96], ["bank1"], ["l0"])
    tile(T.sgx[:, 0, :], "cqg", gc, "sgx0", ["cf"], pc)
    tile(T.sgx[:, 1, :], "cqg", gc, "sgx1", ["cf", "c_p8"], col("p8"))
    act(T.w3[:, 0, :], low, ["low"], ["w3l"], 3.0)
    act(T.w3[:, 1, :], high, ["high"], ["w3h"], 3.0)
    own("V", 0, 8, "win0a")
    own("S", 72, 96, "win0b")
    vcopy(T.mu[:, 0:4], T.iact[:], ["iact"], ["mua"])
    ts(T.mu[:, 4:8], T.iact[:], 24.0, None, A.add, None, ["iact"], ["mub"])
    vcopy(T.cp[:, 0:24], T.ctn[:, 0, :], ["ctn0"], ["cpa"])
    ts(T.cp[:, 24:48], T.ctn[:, 1, :], col("big"), None, A.add, None, ["ctn1", "c_big"], ["cpb"])
    muk, cpk = ["mua", "mub"], ["cpa", "cpb"]
    tt(T.ohw[:], T.cp[:].indirect(T.mu[:]), T.a0s[:], A.is_equal, cpk + muk + ["a0s"], ["ohw"])
    act(T.cpo[:], T.cp[:].indirect(T.pu[:]), cpk + puk, ["cpo"])
    for y in range(2):
        vcopy(T.cfb[:, y::2, :], T.ctn[:, :, 8 * y:8 * y + 16], ctk, ["cf%d" % y])
    vcopy(T.nbu[:], T.inbr[:], ["inbr"], ["nbu"])
    for c in range(2):
        mm(2, 64 * c, 64, [(T.sgx[:, x, :], T.ohw[:, 64 * x:64 * x + 64], ["sgx%d" % x, "ohw"]) for x in range(2)])
    for j in range(8):
        out, sc = T.bd[:, :, 16 * j:16 * j + 16], T.gm[:, j:j + 1]
        if j % 2:
            ts(out, T.cfb[:], sc, None, A.mult, None, ["cf0", "cf1", "gm"], ["bd%d" % j])
        else:
            act(out, T.cfb[:], ["cf0", "cf1", "gm"], ["bd%d" % j], sc)
    bdk = ["bd%d" % j for j in range(8)]
    tt(T.ohz[:], T.cpo[:], bank(2)[:, 0:128], A.is_equal, ["cpo", "bank2"], ["ohz"])
    own("V", 8, 40, "win0c")

    def rows(b, oh, key):
        for y in range(2):
            out = bank(b)[:, y, :] if b == 3 else bank(b)[:, 64 * y:64 * y + 64]
            mmo(b, out, [(T.bd[:, 2 * x + y, :], oh[:, 64 * x:64 * x + 64], bdk + [key]) for x in range(2)])
    rows(3, T.ohz, "ohz")
    act(T.ns8[:], T.cq[:].indirect(T.nbu[:]), ["cq", "nbu"], ["ns8"], 8.0)
    for n in range(2):
        act(T.rd[:, :, 64 * n:64 * n + 64], T.bank3[:, 0:2, :], ["bank3"], ["rd%d" % n])
    rdk = ["rd%d" % n for n in range(2)]
    own("S", 60, 72, "win0d")
    act(T.ms[:, 0:64], T.c48[:].indirect(T.mu[:, 0:4]), ["c48", "mua"], ["ms0"])
    act(T.ms[:, 64:128], T.c48[:].indirect(T.mu[:, 4:8]), ["c48", "mub", "c_big"], ["ms1"], bias=col("big"))
    ev, od = T.ns8[:, 0::2], T.ns8[:, 1::2]
    r1e, r1o, r2e, r2o = (T.rd[:, e, o::2] for e in range(2) for o in range(2))
    turn = [((low, r1e, "low"), (up, r1o, "up")), ((low, r2e, "low"), (high, r1o, "high")), ((down, r2e, "down"), (high, r2o, "high"))]
    for k in range(3):
        mm(4 + k, 0, 128, [(T.w3[:, 0, :], ev, ["w3l", "ns8"])], last=False)
        for n in range(2):
            mm(4 + k, 64 * n, 64, [(t, rh, [key] + rdk) for t, rh, key in turn[k]], first=False, last=False)
        mm(4 + k, 0, 128, [(T.w3[:, 1, :], od, ["w3h", "ns8"])], first=False)
    own("V", 40, 60, "win0e")
    act(T.id124[:], same, ["same"], ["id124"], 124.0)
    act(T.c8[:, 1::3], T.c8[:, 1::3], ["c8a", "c_h8"], ["c8b"], bias=col("h8"))
    act(T.ss8[:], T.cq[:].indirect(T.shu[:]), ["cq", "shu"], ["ss8"], 8.0)
    mm(7, 0, 128, [(low, ev, ["low", "ns8"]), (high, od, ["high", "ns8"])])
    for j, d in enumerate(dests):
        mm(7, 128 + 8 * j, 8, [(low, T.ss8[:, 16 * d:16 * d + 16:2], ["low", "ss8"]), (high, T.ss8[:, 16 * d + 1:16 * d + 16:2], ["high", "ss8"])])
    for k in range(3):
        vcopy(T.lr0[:, 128 * k:128 * k + 128], bank(4 + k)[:, 0:128], ["bank%d" % (4 + k)], ["lr0%d" % k])
        if k == 0:
            tt(T.oha[:], T.reln[:].indirect(T.pu[:]), T.ms[:], A.is_equal, relk + puk + ["ms0", "ms1"], ["oha"])
            rows(2, T.oha, "oha")

    def last1():
        act(T.ya[:], bank(2)[:, 0:128], ["bank2"], ["ya"])
        mmo(5, bank(5)[:, 0:96:3], [(same, T.ya[:, 0:64:2], ["same", "ya"])])
        middle(5, bank(5)[:, 1:96:3], (down, T.ya[:, 64:128:2], ["down", "ya"]), (up, T.ya[:, 1:64:2], ["up", "ya"]))
        mmo(5, bank(5)[:, 2:96:3], [(same, T.ya[:, 65:128:2], ["same", "ya"])])

    def last2():
        act(T.kb[:], bank(5)[:, 0:96], ["bank5"], ["kb"])
        for j in range(2):
            out, b, key = T["k%d" % (j + 1)], T.bcol[:, j:j + 1], "k%d" % (j + 1)
            op("S", lambda: s.activation(out[:], bank(5)[:, 0:96], SIGN, bias=b, scale=2.0), ["bank5", "bcol"], [key])
        mm(6, 0, 96, [(same, T.c8[:], ["same", "c8a", "c8b"]), (same, T.kb[:], ["kb"])] + [(T.id124[:], T[k][:], ["id124", k]) for k in ("k1", "k2")])

    hs = [slice(256 * h, 256 * h + 256) for h in range(2)]
    pb = {(0, 0): 0, (0, 1): 1, (0, 2): 2, (1, 0): 4, (1, 1): 5, (1, 2): 6}
    pcopy = {(1, 0, 0): 7, (1, 1, 0): 0}

    def win(t, k):
        return T.win0[:] if t == 0 else T.win1[:, 1024 * k:1024 * k + 1024]

    def lst(t, k, n, a=0, b=32):
        c = 128 * k + 32 * n if t == 0 else 32 * n
        return T.lr0[:, c + a:c + b] if t == 0 else T.lr1[:, c + a:c + b]

    def keys(t, k):
        return ["win0a", "win0b", "win0c", "win0d", "win0e", "lr0%d" % k] if t == 0 else ["f1%d0" % k, "f1%d1" % k, "lr1"]

    def arrived(e, t, k):
        wait(e, "arr0" if t == 0 else "arr1k%d" % k, nin)

    def buf(n, t, k):
        return T["%s%d%d" % (n, t, k)]

    def bk(n, t, k, h):
        return "%s%d%dh%d" % (n, t, k, h)

    def first(e, t, k, h):
        arrived(e, t, k)
        out, src, ky = buf("ga", t, k)[:, hs[h]], win(t, k).indirect(lst(t, k, 0, 16 * h, 16 * h + 16)), keys(t, k)
        if e == "V":
            vcopy(out, src, ky, [bk("ga", t, k, h)])
        else:
            act(out, src, ky, [bk("ga", t, k, h)])

    def gather(t, k, n, halves=(0, 1)):
        arrived("S", t, k)
        nm = "g" + "ab"[n]
        whole = t == 0 and k > 0
        if whole:
            act(buf(nm, t, k)[:], win(t, k).indirect(lst(t, k, n)), keys(t, k), [bk(nm, t, k, 0), bk(nm, t, k, 1)])
        for h in halves:
            if not whole:
                act(buf(nm, t, k)[:, hs[h]], win(t, k).indirect(lst(t, k, n, 16 * h, 16 * h + 16)), keys(t, k), [bk(nm, t, k, h)])
            if n == 1 and (t, k, h) in pcopy:
                b = pcopy[t, k, h]
                act(bank(b)[:, hs[h]], buf(nm, t, k)[:, hs[h]], [bk(nm, t, k, h)], ["bank%d" % b])
            elif n == 1:
                mm(pb[t, k], 256 * h, 256, [(T.idf[:], buf(nm, t, k)[:, hs[h]], ["idf", bk(nm, t, k, h)])])

    def result(t, k, h):
        if t == 0:
            return T.win1[:, 1024 * k + 256 * h:1024 * k + 256 * h + 256], "f1%d%d" % (k, h)
        return T["n1" + "ab"[h]][:, 256 * k:256 * k + 256], "n1%d%d" % (h, k)

    def part(t, k, n, h):
        arrived("V", t, k)
        src, dst = {2: ("ga", "ma"), 3: ("ma", "mb"), 1: ("mb", "")}[n]
        out, key = result(t, k, h) if n == 1 else (buf(dst, t, k)[:, hs[h]], bk(dst, t, k, h))
        tt(out, win(t, k).indirect(lst(t, k, n, 16 * h, 16 * h + 16)), buf(src, t, k)[:, hs[h]], A.max, keys(t, k) + [bk(src, t, k, h)], [key])

    def join(t, k, h):
        out, key = result(t, k, h)
        b = pcopy.get((t, k, h), pb[t, k])
        tt(out, bank(b)[:, hs[h]], buf("mb", t, k)[:, hs[h]], A.max, ["bank%d" % b, bk("mb", t, k, h)], [key])

    both, one = (0, 1), (1,)
    moved = {(0, 0): one, (0, 1): both, (0, 2): both, (1, 0): (1, 0), (1, 1): (1, 0), (1, 2): one}

    def vector(t, order):
        for k, n, h in order:
            if n == 1 and h in moved[t, k]:
                join(t, k, h)
            else:
                part(t, k, n, h)

    def block(k):
        return [(k, n, h) for n in (2, 3, 1) for h in range(2)]

    def slots1(k):
        w, ky = T.win1[:, 1024 * k:1024 * k + 512], ["f1%d0" % k, "f1%d1" % k, "ls1"]
        if k < 2:
            act(T.snd1[:, k, :], w.indirect(T.ls1[:]), ky, ["snd1%d" % k])
            kk = [["snd1%d" % k]] * 3
        else:
            act(T.snd1[:, k, 0:128], w.indirect(T.ls1[:, 0:8]), ky, ["snd12a"])
            for j, key in ((1, "snd12b"), (2, "snd12c")):
                vcopy(T.snd1[:, k, 128 * j:128 * j + 128], w.indirect(T.ls1[:, 8 * j:8 * j + 8]), ky, [key])
            kk = [["snd12a"], ["snd12b"], ["snd12c"]]
        c0 = 1024 * k + 8 * (64 + 16 * r)
        send(T.win1[:, c0:c0 + 128], [T.snd1[:, k, 128 * j:128 * j + 128] for j in range(3)], "arr1k%d" % k, kk, (0, 1))

    first("S", 0, 0, 0)
    first("V", 0, 0, 1)
    ts(T.lr1[:], bank(7)[:, 0:128], k8, None, A.add, None, ["bank7", "cf"], ["lr1"])
    ts(T.ls1[:], bank(7)[:, 128:152], k8, None, A.add, None, ["bank7", "cf"], ["ls1"])
    gather(0, 0, 1, moved[0, 0])
    gather(0, 1, 1, moved[0, 1])
    last1()
    gather(0, 1, 0)
    gather(0, 2, 1, moved[0, 2])
    vector(0, block(0))
    slots1(0)
    gather(0, 2, 0)
    vector(0, block(1))
    slots1(1)
    last2()
    vector(0, block(2))
    slots1(2)
    vcopy(T.lf[:], bank(6)[:, 0:96], ["bank6"], ["lf"])
    first("V", 1, 0, 1)
    first("S", 1, 0, 0)
    gather(1, 0, 1, moved[1, 0])
    for k in range(1, 3):
        gather(1, k, 0)
        gather(1, k, 1, moved[1, k])
    vector(1, block(0))
    vector(1, [(1, 2, 0), (1, 2, 1), (1, 3, 0), (1, 3, 1), (1, 1, 0), (2, 2, 0), (1, 1, 1), (2, 3, 0), (2, 1, 0), (2, 2, 1), (2, 3, 1), (2, 1, 1)])

    nst = [0]

    def final(e, a, b):
        h = 0 if b <= 48 else 1
        out, src = T.yo[:, 16 * a:16 * b], T["n1" + "ab"[h]][:].indirect(T.lf[:, a:b])
        ky = ["lf"] + ["n1%d%d" % (h, k) for k in range(3)]
        if e == "V":
            vcopy(out, src, ky, ["yo%d" % a])
        else:
            act(out, src, ky, ["yo%d" % a])
        op("Y", lambda: g.sync.dma_start(T.y[:, 16 * a:16 * b], T.yo[:, 16 * a:16 * b]), ["yo%d" % a], [], "st%d" % nst[0], 16)
        nst[0] += 1
    final("S", 0, 24)
    final("S", 24, 48)
    final("V", 48, 72)
    final("S", 72, 96)
    for name in sorted(cnt):
        wait("Y", name, cnt[name])
    wait("G", "sent", (1 + 3) * nout)
